import numpy as np, ml_dtypes
CORES = [5,29,101,125,133,157,229,253]
N = 8
import mx_ref
BF = ml_dtypes.bfloat16
def gcols(t, e):
    v = np.concatenate([t.reshape(8, 16, -1, 4), np.zeros((8, 16, 1, 4), BF)], axis=2)
    return np.ascontiguousarray(np.stack([v[g][:, e[g]] for g in range(8)])).reshape(128, -1)
def tile(rs):
    return np.stack(rs, axis=2).reshape(128, -1).astype(BF)
def pick(q, e):
    c = np.concatenate([q[0].reshape(128, -1, 4), np.zeros((128, 1, 4), np.uint8)], axis=1); s = np.concatenate([q[1], np.ones((16, 1), np.uint8)], axis=1)
    return (np.ascontiguousarray(c[:, e].reshape(128, -1)), np.ascontiguousarray(s[:, e]))
def join(*qs):
    return (np.concatenate([q[0] for q in qs], axis=1), np.concatenate([q[1] for q in qs], axis=1))
def put(q, e, v):
    c, s = q[0].reshape(128, -1, 4).copy(), q[1].copy(); c[:, e] = v[0].reshape(128, -1, 4); s[:, e] = v[1]
    return (c.reshape(128, -1), s)
def pk(c, s):
    return (np.ascontiguousarray(c), mx_ref.live(s))
def emit(q):
    return q[0], q[1]
def packed(v, rng):
    q = [mx_ref.quantize(np.ascontiguousarray(v[r])) for r in range(N)]
    return np.stack([a for a, b in q]), np.stack([mx_ref.plane(b, rng) for a, b in q])
def values_of_codes():
    e, c = np.zeros((128, 128, 4), np.float32), np.zeros((128, 2, 4), np.uint8)
    e[np.arange(128), np.arange(128), 0] = 1
    c[:127, :, 0] = np.arange(256).reshape(2, 128).T[:127]
    return mx_ref.matmul(mx_ref.quantize(e.reshape(128, 512).astype(BF)), (c.reshape(128, 8), np.full((16, 2), 127, np.uint8))).T.reshape(-1).astype(np.float64)
CODE_VALUE, SCALE_VALUE = values_of_codes(), 2.0 ** (np.arange(256) - 127.0)
def decode(q):
    return (CODE_VALUE[q[0]].reshape(16, 8, -1, 4) * SCALE_VALUE[q[1]][:, None, :, None] + 0.0).reshape(128, -1).astype(np.float32)
def f(rng, *shape):
    return mx_ref.flush((rng.standard_normal(shape, dtype=np.float32) * np.exp2(rng.integers(-2, 3, shape[:-1] + (1,)))).astype(BF))
def wide(rng, *shape, cols=0):
    v = rng.standard_normal(shape, dtype=np.float32) * np.exp2(rng.integers(-12, 13, shape)).astype(np.float32)
    if cols: v *= np.repeat(np.exp2(rng.integers(-cols, cols + 1, shape[:-2] + (1, shape[-1] // 4))) * (rng.random(shape[:-2] + (1, shape[-1] // 4)) > 0.0625), 4, axis=-1).astype(np.float32)
    return mx_ref.flush(v.astype(BF))
C, A, B, S = 448, 224, 112, 14
def top(s, k):
    return np.sort(np.argsort(-s, axis=-1, kind="stable")[..., :k], axis=-1)
def layer(w, q):
    return tile([np.maximum(mx_ref.matmul(pick(w, np.arange(128 * b, 128 * b + 128)), q), np.float32(0.0)) * np.float32(0.03125) for b in range(4)])
def gadd(t, e, v):
    a, c = t.astype(np.float32).reshape(8, 16, -1, 4), v.astype(np.float32).reshape(8, 16, -1, 4)
    for g in range(8): a[g][:, e[g]] = a[g][:, e[g]] + c[g]
    return a.reshape(128, -1).astype(BF)
def big(v, k):
    v = v.astype(np.float32) * np.float32(k)
    v[np.abs(v) < np.float32(2.0 ** -16)] = 0
    return v.astype(BF)
def numbers_of(rng):
    return {"x": big(f(rng, N, 128, 4 * C), 1), "u1": np.array(f(rng, N, 128, 512)), "u2": np.array(f(rng, N, 128, 512)), "v": np.array(f(rng, N, 128, 512))}
def weights(rng, w, z):
    a, b = packed(w, rng)
    c, e = packed(z, rng)
    return {"wc": a, "ws": b, "zc": c, "zs": e}
def unit(k):
    w = np.zeros((N, 128, 4, 128, 4), np.float32)
    i = np.arange(128)
    for b in range(4): w[:, i, b, i, b] = k
    return w.reshape(N, 128, 2048).astype(BF)
def signs(rng):
    return np.stack([rng.permutation(8) % 2 * 2.0 - 1.0 for r in range(N)])
def steps(n):
    return np.minimum((np.arange(n) + 1) // 2, n // 2 - 1)
def planted(rng, p1, p2, k):
    d = numbers_of(rng)
    s1, t, s2 = np.zeros((N, 8, C), int), np.zeros((N, 8, A), int), np.zeros((N, 8, C), int)
    np.put_along_axis(s1, p1, np.broadcast_to(steps(C), p1.shape), axis=2)
    np.put_along_axis(t, p2, np.broadcast_to(steps(A), p2.shape), axis=2)
    first = top(s1, A)
    np.put_along_axis(s2, first, t, axis=2)
    x = d["x"].astype(np.float32).reshape(N, 8, 16, C, 4)
    x[:, :, 0] = 0
    x[:, :, 0, :, 0] = 1
    np.put_along_axis(x[:, :, 0, :, 1], p1[..., -1:], np.float32(2.0 ** 13), axis=2)
    np.put_along_axis(x[:, :, 0, :, 1], p1[..., :1], np.float32(-2.0 ** 30), axis=2)
    np.put_along_axis(x[:, :, 0, :, 2], np.take_along_axis(first, p2[..., -1:], axis=2), np.float32(2.0 ** 13), axis=2)
    for s, at in ((s1, 8), (s2, 10)):
        g = ((s[..., None] >> np.arange(8)) & 1) * np.exp2(np.arange(8) - 23.0)
        x[:, :, at] = g[..., :4]
        x[:, :, at + 1] = g[..., 4:]
    x[:, :, 12] = 0
    x[:, :, 12, :, 0] = 2.0 ** -10
    x[:, :, 13:] = rng.integers(4, 8, (N, 8, 3, C, 4)) * rng.choice([-1.0, 1.0], (N, 8, 3, C, 4)) * 2.0 ** -20
    d["x"] = x.reshape(N, 128, 4 * C).astype(BF)
    for n, at, far in (("u1", 8, 1), ("u2", 10, 2)):
        u = d[n].reshape(N, 128, 128, 4)
        u[:, :, ::16] = 0
        g = (signs(rng) * k).astype(BF)
        for i in range(8):
            u[:, 16 * i, 16 * i, 0] = g[:, i]
            u[:, 16 * i, 16 * i, far] = 2.0 ** 13 * k
            u[:, 16 * i + at:16 * i + at + 2, 16 * i] = k
            u[:, 16 * i + 12, 16 * i, 0] = g[:, i]
        d[n] = u.reshape(N, 128, 512)
    return {**d, **weights(rng, unit(32), f(rng, N, 128, 2048))}
def setup_inputs(rng):
    return {**numbers_of(rng), **weights(rng, f(rng, N, 128, 2048), f(rng, N, 128, 2048))}
def setup_inputs_ties(rng):
    d = numbers_of(rng)
    e = rng.permutation(N)
    x = d["x"].reshape(N, 8, 16, C, 4)
    for r in range(N):
        k = np.zeros(C, int) if r == e[0] else rng.permutation(C) % 3
        a = x[r][:, :8, :3].copy()
        a[:, :, 2] = 0
        x[r][:, :8] = a[:, :, k]
    d["x"] = x.reshape(N, 128, 4 * C)
    w = np.array(f(rng, N, 128, 2048)).reshape(N, 8, 16, 4, 8, 16, 4)
    w[:, :, 8:, :, :, :8] = 0
    for g in range(8): w[:, np.arange(8) != g, :, :, g, :8] = 0
    for n in ("u1", "u2"):
        u = d[n].reshape(N, 8, 16, 128, 4)
        u[:, :, 8:, ::16] = 0
        for g in range(8): u[:, np.arange(8) != g, :, 16 * g] = 0
        d[n] = u.reshape(N, 128, 512)
    return {**d, **weights(rng, w.reshape(N, 128, 2048), f(rng, N, 128, 2048))}
def setup_inputs_near(rng):
    p = []
    for n, k in ((C, A), (A, B)):
        a = rng.permuted(np.tile(np.arange(n), (N, 8, 1)), axis=2)
        a[:, :, n - k - 3:n - k + 1] = np.sort(a[:, :, n - k - 3:n - k + 1], axis=2)
        p.append(a)
    return planted(rng, p[0], p[1], 1.0)
def setup_inputs_runs(rng):
    a, b = signs(rng)[:, :, None] > 0, signs(rng)[:, :, None] > 0
    return planted(rng, np.where(a, np.arange(C), np.arange(C)[::-1]), np.where(b, np.arange(A), np.arange(A)[::-1]), 2.0 ** -30)
def setup_inputs_huge(rng):
    d = numbers_of(rng)
    c = np.stack([rng.permutation(C) % 2 * 2.0 - 1.0 for r in range(N)])
    c[rng.permutation(N) < N // 2] = -1
    x = 2.0 ** 30 * (0.6 + 0.3 * rng.random((N, 128, C, 4))) * c[:, None, :, None]
    d["x"] = x.astype(np.float32).reshape(N, 128, 4 * C).astype(BF)
    for n in ("u1", "u2"):
        u = d[n].reshape(N, 128, 128, 4)
        a = 2.0 ** 30 * (1 - 0.25 * rng.random((N, 128, 8, 4))) * signs(rng)[:, None, :, None]
        u[:, :, ::16] = a.astype(np.float32).astype(BF)
        d[n] = u.reshape(N, 128, 512)
    return {**d, **weights(rng, unit(-32), big(f(rng, N, 128, 2048), 2.0 ** -6))}
def setup_inputs_spread(rng):
    d = setup_inputs(rng)
    d["x"] = big(wide(rng, N, 128, 4 * C, cols=6), 1)
    return d
def check_inputs(d):
    b = []
    for k in ("x", "u1", "u2", "v"):
        a = np.abs(d[k].astype(np.float32))
        if not (np.isfinite(a).all() and ((a == 0) | (a >= 2.0 ** -30) & (a <= 2.0 ** 30)).all()): b.append("a value of " + k)
    return b
def reference(x, u1, u2, v, wc, ws, zc, zs):
    one, two, h, down = [], [], [], []
    for r in range(N):
        p = mx_ref.matmul(mx_ref.quantize(u1[r]), mx_ref.quantize(x[r]))
        one.append(top(p[::16] + np.float32(0.0), A))
        h.append(layer(pk(wc[r], ws[r]), mx_ref.quantize(gcols(x[r], one[r]))))
        p = mx_ref.matmul(mx_ref.quantize(u2[r]), mx_ref.quantize(h[r]))
        two.append(top(p[::16] + np.float32(0.0), B))
        down.append(mx_ref.quantize(gcols(h[r], two[r])))
    done = []
    for d in range(N):
        q = join(*[pick(down[r], S * d + np.arange(S)) for r in range(N)])
        done.append(mx_ref.quantize(layer(pk(zc[d], zs[d]), q)))
    y, ol = np.zeros((N, 128, C), np.float32), np.zeros((N, 8, B), np.float32)
    oc, osc = np.zeros((N, 128, 4 * C), np.uint8), np.zeros((N, 16, C), np.uint8)
    for r in range(N):
        came = decode(join(*[pick(done[d], S * r + np.arange(S)) for d in range(N)]))
        q = mx_ref.quantize(gadd(x[r], one[r], gadd(h[r], two[r], came)))
        y[r] = mx_ref.matmul(mx_ref.quantize(v[r]), q)
        ol[r] = np.take_along_axis(one[r], two[r], axis=1)
        oc[r], osc[r] = emit(q)
    return {"y": y, "ol": ol, "oc": oc, "osc": osc}

@@ -1,0 +1,549 @@
+from concourse.bass import DstId, RemoteDMATransfer
+from concourse.mybir import dt, AluOpType, AxisListType, ActivationFunctionType
+
+C, A, B, S = 448, 224, 112, 14
+BIG = float(2 ** 90)
+HOLD = float(2 ** 20)
+NS1, NS2 = 16, 9
+NV1, NV2 = 28 - NS1, 14 - NS2
+Q4, U8 = "float8_e4m3fn_x4", "uint8"
+
+
+def _sb(n, d):
+    return ("sbuf", [128, n], d)
+
+
+SCRATCH = {
+    "xb": _sb(4 * C, "bfloat16"), "x2": _sb(4 * C, "bfloat16"),
+    "u1b": _sb(512, "bfloat16"), "u2b": _sb(512, "bfloat16"), "vb": _sb(512, "bfloat16"),
+    "xq": _sb(C, Q4), "xs": _sb(C, U8),
+    "u1q": _sb(128, Q4), "u1s": _sb(128, U8), "u1pq": _sb(256, Q4), "u1ps": _sb(256, U8),
+    "u2q": _sb(128, Q4), "u2s": _sb(128, U8), "u2pq": _sb(256, Q4), "u2ps": _sb(256, U8),
+    "vq": _sb(128, Q4), "vs": _sb(128, U8),
+    "wq": _sb(512, Q4), "wp": _sb(512, U8), "zq": _sb(512, Q4), "zp": _sb(512, U8),
+    "eb": _sb(2048, "bfloat16"), "eq": _sb(512, Q4), "es": _sb(512, U8),
+    "ft": _sb(4 * A, "bfloat16"), "fq": _sb(A, Q4), "fs": _sb(A, U8),
+    "ht": _sb(4 * A, "bfloat16"), "hq": _sb(A, Q4), "hs": _sb(A, U8),
+    "gt": _sb(512, "bfloat16"), "gq": _sb(240, Q4), "gs": _sb(240, U8),
+    "tt": _sb(512, "bfloat16"), "tq": _sb(240, Q4), "ts": _sb(240, U8),
+    "gcomp": _sb(4 * B, "bfloat16"), "il": _sb(8 * B, "bfloat16"), "io2": _sb(8 * B, "bfloat16"),
+    "keep": _sb(8 * B, "bfloat16"), "a1": _sb(4 * A, "bfloat16"),
+    "oq": _sb(C, Q4), "osb": _sb(C, U8), "yb": _sb(C, "float32"),
+    "rq1": _sb(32, Q4), "rs1": _sb(128, U8), "rq2": _sb(28, Q4), "rs2": _sb(112, U8),
+    "ki": _sb(160, "int32"), "kj": _sb(128, "int32"), "kf": _sb(1280, "float32"), "kc": _sb(768, "float32"),
+    "opick": _sb(16, "uint16"), "oread": _sb(2, "uint16"), "operm": _sb(16, "uint16"),
+    "od1": _sb(32, "uint16"), "od2": _sb(16, "uint16"),
+    "of": _sb(56, "uint16"), "og": _sb(32, "uint16"), "ox": _sb(28, "uint16"),
+    "tn1": _sb(C, "float32"), "tn2": _sb(A, "float32"),
+    "junk1": _sb(NS1 * C, "bfloat16"), "junk2": _sb(NS2 * A, "bfloat16"),
+    "fl1": _sb(NV1 * C, "bfloat16"), "fl2": _sb(NV2 * A, "bfloat16"),
+    "so1": _sb(NV1 * C // 2, "bfloat16"), "so2": _sb(NV2 * A // 2, "bfloat16"),
+    "w1": _sb(1280, "float32"), "w2": _sb(1280, "float32"),
+    "win1": _sb(960, "float32"), "win2": _sb(480, "float32"), "win3": _sb(480, "float32"),
+    "ex1": _sb(A, "float32"), "ex2": _sb(B, "float32"), "v1": _sb(256, "float32"),
+    "olb": _sb(B, "float32"), "yx": _sb(256, "float32"),
+}
+for _i in range(8):
+    SCRATCH["ps%d" % _i] = ("psum", [128, 512], "float32")
+
+NPOOL = 140
+SEMAPHORES = ["arr1", "arr2", "hin1", "hin2", "sent"] + ["s%d" % _i for _i in range(NPOOL)]
+
+ALU = AluOpType
+ACT = ActivationFunctionType
+DIRECT_CODES, DIRECT_SCALES = (4, 2, 2), (2, 2, 4)
+HOP = 4
+
+
+def _plan(core, T, topo):
+    far = [d for d in T.cores if d != core and not topo.may_write(core, d)]
+    near = [d for d in T.cores if d != core and topo.may_write(core, d)]
+    hs = [h for h in topo.cores_of(core) if h != core and all(topo.may_write(h, d) for d in far)]
+    hs.sort(key=lambda h: (topo.die(h) != topo.die(core), h))
+    return far, near, hs
+
+
+def _masks(engines, sizes):
+    out, at = [], 0
+    for n in sizes:
+        m = 0
+        for e in engines[at:at + n]:
+            m |= 1 << e
+        out.append(m)
+        at += n
+    return out
+
+
+def _xfer(topo, src_core, dst_core, mask, sem, src, dst):
+    rid, pid = topo.addr(dst_core, src_core)
+    return RemoteDMATransfer(dst_ids=[DstId(rid=rid, pnc=pid)], dma_engine_mask=mask, remote_sem=sem, src=src, dst=dst)
+
+
+def _slot(dst, src, T, topo):
+    far, near, hs = _plan(dst, T, topo)
+    return (far + near).index(src)
+
+
+def _arrivals(core, T, topo):
+    far, near, hs = _plan(core, T, topo)
+    n = 2 * HOP * len(far)
+    for s in near:
+        i = _plan(s, T, topo)[1].index(core)
+        n += DIRECT_CODES[i] + DIRECT_SCALES[i]
+    return n
+
+
+def _u8(v):
+    return v.bitcast(dt.uint8)
+
+
+def helper_program(g, core, T, topo, home):
+    far, near, hs = _plan(home, T, topo)
+    if core not in hs:
+        return
+    j = hs.index(core)
+    pair = (2 * (j % 2), 2 * (j % 2) + 1)
+    masks = _masks(topo.engines(core, far[0]), (HOP, HOP))
+    for phase in (1, 2):
+        g.wait_ge(T.sem["hin%d" % phase], HOP)
+        xs = []
+        for n, i in enumerate(pair):
+            d = far[i]
+            at = (S if phase == 1 else 128) + S * _slot(d, home, T, topo)
+            if j < 2:
+                src = T.rq1[:, 16 * n + 2:16 * n + 16] if phase == 1 else T.rq2[:, S * n:S * n + S]
+                dst = (T.gq if phase == 1 else T.tq)[:, at:at + S]
+                src, dst = _u8(src), _u8(dst)
+            else:
+                src = T.rs1[:, 16 * i + 18:16 * i + 32] if phase == 1 else T.rs2[:, S * i + S:S * i + 2 * S]
+                dst = (T.gs if phase == 1 else T.ts)[:, at:at + S]
+            xs.append(_xfer(topo, core, d, masks[n], T.sem["arr%d" % phase], src, dst))
+        g.remote_dma_fused(xs, local_sem=T.sem.sent)
+    g.wait_ge(T.sem.sent, 4 * HOP)
+
+
+def rank_program(g, core, T, topo):
+    rank = T.rank_of(core)
+    if rank is None:
+        for c in topo.cores_of(core):
+            if T.rank_of(c) is not None:
+                helper_program(g, core, T, topo, c)
+        return
+    far, near, hs = _plan(core, T, topo)
+    order = [T.rank_of(d) for d in [core] + far + near]
+    V, SC, PE, SY = g.vector, g.scalar, g.tensor, g.sync
+    eng = {"g": g, "v": V, "a": SC, "p": PE, "y": SY}
+
+    pool = [0]
+    known = {e: set() for e in eng}
+    stage = {e: None for e in eng}
+    stages = []
+    writer, readers = {}, {}
+
+    def new_stage(sem=None, count=0):
+        if sem is None:
+            sem = "s%d" % pool[0]
+            pool[0] += 1
+        st = {"sem": sem, "n": count, "before": set(), "k": len(stages), "waited": False}
+        stages.append(st)
+        return st
+
+    def need(e, st):
+        if st["k"] in known[e]:
+            return
+        for q in stage:
+            if stage[q] is st:
+                stage[q] = None
+        eng[e].wait_ge(T.sem[st["sem"]], st["n"])
+        st["waited"] = True
+        known[e].add(st["k"])
+        known[e].update(st["before"])
+
+    def deps(e, r, w):
+        sts = []
+        for n in r:
+            sts += writer.get(n, [])
+        for n in w:
+            sts += readers.get(n, [])
+        for st in sorted(sts, key=lambda s: -s["k"]):
+            need(e, st)
+
+    def mark(st, r, w):
+        for n in r:
+            readers.setdefault(n, []).append(st)
+        for n in w:
+            writer.setdefault(n, []).append(st)
+
+    def op(e, call, r, w):
+        deps(e, r, w)
+        if stage[e] is None:
+            stage[e] = new_stage()
+        st = stage[e]
+        call().then_inc(T.sem[st["sem"]], 1)
+        st["n"] += 1
+        st["before"].update(known[e])
+        mark(st, r, w)
+
+    def cut(e):
+        stage[e] = None
+
+    def dma(e, pairs, r, w):
+        deps(e, r, w)
+        st = new_stage()
+        for out, in_ in pairs:
+            eng[e].dma_start(out, in_).then_inc(T.sem[st["sem"]], 16)
+            st["n"] += 16
+        st["before"].update(known[e])
+        mark(st, r, w)
+
+    def ts(out, in0, s1, s2, o0, o1, r, w):
+        if o1 is None:
+            op("v", lambda: V.tensor_scalar(out, in0, s1, None, o0), r, w)
+        else:
+            op("v", lambda: V.tensor_scalar(out, in0, s1, s2, o0, o1), r, w)
+
+    def tt(out, a, b, o, r, w):
+        op("v", lambda: V.tensor_tensor(out, a, b, o), r, w)
+
+    def cp(out, in_, r, w):
+        op("v", lambda: V.tensor_copy(out, in_), r, w)
+
+    def ms(out, c, w):
+        op("v", lambda: V.memset(out, c), [], w)
+
+    def red(out, in_, o, r, w):
+        op("v", lambda: V.tensor_reduce(out, in_, AxisListType.X, o), r, w)
+
+    def tr(out, in_, r, w):
+        op("v", lambda: V.transpose(out, in_), r, w)
+
+    def scan(out, d0, d1, init, o0, o1, r, w):
+        op("v", lambda: V.tensor_tensor_scan(out, d0, d1, init, o0, o1), r, w)
+
+    def quant(q, s, t, r, w):
+        op("v", lambda: V.quantize_mx(q, s, t), r, w)
+
+    def act(out, in_, f, r, w, **kw):
+        op("a", lambda: SC.activation(out, in_, f, **kw), r, w)
+
+    def mm(bank, n, lq, ls, rq, rs, r):
+        name = "ps%d" % bank
+        op("p", lambda: PE.matmul_mx(T[name][:, 0:n], lq, ls, rq, rs, True, True), r, [name])
+        writer[name] = writer[name][-1:]
+        readers[name] = []
+        cut("p")
+
+    def iota(out, pattern, base, cm, w, whole=False):
+        if whole:
+            op("g", lambda: g.iota(out, pattern, base, cm), [], w)
+        else:
+            op("g", lambda: g.iota(out, pattern, base, cm, allow_small_or_imprecise_dtypes=True), [], w)
+
+    dma("a", [(T.u1b[:], T.u1[:])], [], ["u1b"])
+    dma("y", [(T.xb[:, 0:896], T.x[:, 0:896])], [], ["xb0"])
+    dma("a", [(T.xb[:, 896:1792], T.x[:, 896:1792])], [], ["xb1"])
+    dma("y", [(T.u2b[:], T.u2[:])], [], ["u2b"])
+    dma("y", [(_u8(T.wq[:]), T.wc[:]), (T.wp[:], T.ws[:])], ["xb0", "xb1"], ["w"])
+    dma("y", [(_u8(T.zq[:]), T.zc[:]), (T.zp[:], T.zs[:])], [], ["z"])
+    dma("y", [(T.vb[:], T.v[:]), (T.x2[:], T.x[:])], [], ["vb", "x2"])
+
+    kf, kc, ki, kj = T.kf, T.kc, T.ki, T.kj
+    J32, J16, JH, R4 = kf[:, 0:32], kf[:, 32:64], kf[:, 64:96], kf[:, 96:320]
+    VAL1, VAL2, RROW = kf[:, 320:832], kf[:, 832:1088], kf[:, 1088:1120]
+    iota(ki[:, 0:16], [[16, 2], [32, 4], [0, 2]], 0, 0, ["ipick"], True)
+    iota(ki[:, 16:17], [[0, 1]], 0, 1, ["ip"], True)
+    cut("g")
+    iota(J32, [[1, 32]], 0, 0, ["J"])
+    iota(J16, [[0, 2], [1, 16]], 0, 0, ["J"])
+    iota(JH, [[1, 2], [0, 16]], 0, 0, ["J"])
+    cut("g")
+    iota(R4, [[0, 56], [1, 4]], 0, 0, ["R4"])
+    cut("g")
+    iota(VAL1, [[4, 32], [128, 16]], 0, 0, ["VAL"])
+    iota(VAL2, [[4, 16], [64, 16]], 0, 0, ["VAL"])
+    iota(ki[:, 32:32 + B], [[0, 8], [1, S]], 2, 0, ["R14"], True)
+    for p in range(8):
+        iota(kf[:, 1088 + 4 * p:1092 + 4 * p], [[4, 4]], S * order[p] + 1, 0, ["RROW"])
+    cut("g")
+    iota(T.keep[:], [[0, 4 * B], [1, 2]], 0, 0, ["keep"])
+    iota(T.eb[:], [[0, 2048]], 1, 0, ["eb0"])
+    op("g", lambda: g.affine_select(T.eb[:], T.eb[:], [[1, 4], [-1, 512]], ALU.is_equal, 0.0, 0, 4), ["eb0"], ["eb"])
+    cut("g")
+
+    w1, w2 = T.w1, T.w2
+    names = ["V", "U", "Sp", "Sc", "Uc", "x1", "x2", "f", "mb0", "mb1", "mb2", "tb0", "tb1", "tb2", "col", "gt", "ge",
+             "cg", "cge", "e", "mc0", "mc1", "tc0", "tc1", "dx", "dy", "dd", "A", "B", "ns", "m", "nz", "dest", "St", "Ut"]
+    at = {n: 32 * i for i, n in enumerate(names)}
+
+    def tile(wb, n, a=0, b=32, s=1):
+        return wb[:, at[n] + a:at[n] + b:s]
+
+    ms(tile(w1, "V"), -1.0, ["V1p"])
+    ms(tile(w2, "V"), -1.0, ["V2p"])
+    ms(tile(w1, "U", 30, 32), BIG, ["U1"])
+    ms(tile(w2, "U", 30, 32), BIG, ["U2"])
+    ms(tile(w1, "Sp"), -BIG, ["Sp1p"])
+    ms(tile(w2, "Sp"), -BIG, ["Sp2p"])
+    ms(T.tt[:, 0:4 * S], 0.0, ["tt"])
+    ms(kc[:, 608:640], 0.0, ["ZERO"])
+    ZERO = kc[:, 608:640]
+    cp(T.opick[:], ki[:, 0:16], ["ipick"], ["opick"])
+    P = ki[:, 16:17]
+    ts(kj[:, 112:113], P, 15, None, ALU.bitwise_and, None, ["ip"], ["I4"])
+    ts(kj[:, 113:114], P, 15, 2, ALU.bitwise_and, ALU.logical_shift_right, ["ip"], ["I4"])
+    ts(kj[:, 114:115], P, 3, None, ALU.bitwise_and, None, ["ip"], ["I4"])
+    ts(kj[:, 115:116], P, 4, 1, ALU.logical_shift_right, ALU.bitwise_and, ["ip"], ["I4"])
+    cp(kc[:, 0:4], kj[:, 112:116], ["I4"], ["F4"])
+    PM, PQ, PT, PH = kc[:, 0:1], kc[:, 1:2], kc[:, 2:3], kc[:, 3:4]
+    PM32, PM16, N0, M0, M1 = kc[:, 4:5], kc[:, 5:6], kc[:, 6:7], kc[:, 7:8], kc[:, 8:9]
+    OWN, TRI0, TRI, UP, MLO, MHI = (kc[:, 32 * i:32 * i + 32] for i in range(1, 7))
+    Z1, Z2, C1, C2 = kc[:, 224:256], kc[:, 256:272], kc[:, 272:496], kc[:, 496:608]
+    ts(PM32, PM, 32.0, None, ALU.mult, None, ["F4"], ["F5"])
+    ts(OWN, JH, PH, None, ALU.is_equal, None, ["F4", "J"], ["OWN"])
+    ts(TRI0, J16, PM, None, ALU.is_gt, None, ["F4", "J"], ["OWN"])
+    tt(TRI, TRI0, OWN, ALU.mult, ["OWN"], ["TRI"])
+    ts(MLO, OWN, -2.0 * BIG, BIG, ALU.mult, ALU.add, ["OWN"], ["MSK"])
+    ts(MHI, OWN, 2.0 * BIG, -BIG, ALU.mult, ALU.add, ["OWN"], ["MSK"])
+    ts(Z1, J32, PM32, float(A + 1), ALU.add, ALU.add, ["F5", "J"], ["MSK"])
+    tt(UP, OWN, TRI, ALU.subtract, ["OWN", "TRI"], ["UP"])
+    ts(C1, R4, PQ, HOLD, ALU.is_equal, ALU.mult, ["R4", "F4"], ["C1"])
+    cut("v")
+
+    def pick(u, n):
+        q, s, pq, ps = T[u + "q"], T[u + "s"], T[u + "pq"], T[u + "ps"]
+        quant(q[:], s[:], T[u + "b"][:], [u + "b"], [u + "q"])
+        cp(pq[:].bitcast(dt.uint32), q[:].bitcast(dt.uint32).indirect(T.opick[:]), [u + "q", "opick"], [u + "pq"])
+        cut("v")
+        act(ps[:], s[:].indirect(T.opick[:]), ACT.Copy, [u + "q", "opick"], [u + "ps"])
+        cut("a")
+
+    def scores(u, n, q, s, name):
+        pq, ps = T[u + "pq"], T[u + "ps"]
+        mm(0, n, T[u + "q"][:], T[u + "s"][:], q, s, [u + "q"] + name)
+        mm(1, n, pq[:, 0:128], ps[:, 0:128], q, s, [u + "pq", u + "ps"] + name)
+        mm(2, n, pq[:, 128:256], ps[:, 128:256], q, s, [u + "pq", u + "ps"] + name)
+        mm(3, n, pq[:, 128:256], ps[:, 128:256], q, s, [u + "pq", u + "ps"] + name)
+
+    def select(L):
+        n, k, wb, ns, nv = (C, A, w1, NS1, NV1) if L == 1 else (A, B, w2, NS2, NV2)
+        tn, junk, fl, so = T["tn%d" % L], T["junk%d" % L], T["fl%d" % L], T["so%d" % L]
+        nb, W = n // 32, (32 if L == 1 else 16)
+        hcol = 16 if L == 1 else 8
+        first = 128 if L == 1 else 64
+        X = lambda s: s + str(L)
+        t = lambda s, a=0, b=W, st=1: tile(wb, s, a, b, st)
+        tr(tn[:, 0:first], T.ps0[:, 0:first], ["ps0"], [X("tna")])
+        cut("v")
+        tr(tn[:, first:n], T.ps0[:, first:n], ["ps0"], [X("tnb")])
+        cut("v")
+        for i in range(ns):
+            h, b = (0, i) if i < nb else (1, i - nb)
+            c = 32 * b + 16 * h
+            act(junk[:, n * i:n * i + n], T["ps1" if h == 0 else "ps3"][:, 0:n], ACT.Sign,
+                ["ps1" if h == 0 else "ps3", X("tna") if c < first else X("tnb"), X("V") + "p"], [X("V")],
+                bias=tn[:, c:c + 1], scale=-1.0, accum_out=tile(wb, "V", hcol * h + b, hcol * h + b + 1))
+        cut("a")
+        b0 = ns - nb
+        for i in range(nv):
+            c = 32 * (b0 + i) + 16
+            ts(fl[:, n * i:n * i + n], T.ps2[:, 0:n], tn[:, c:c + 1], 0.5, ALU.is_lt, ALU.subtract,
+               ["ps2", X("tna"), X("tnb")], [X("fl")])
+        if L == 1:
+            for h in range(2):
+                cp(tile(wb, "Sp", 16 * h, 16 * h + nb), tn[:, 16 * h:n:32], [X("tna"), X("tnb"), "Sp1p"], [X("Sp")])
+        else:
+            for h in range(2):
+                for half, m in ((0, N0), (1, PH)):
+                    ts(tile(wb, "Sp", 16 * h + half, 16 * h + 2 * nb, 2), tn[:, 16 * h:n:32], m, None, ALU.mult, None,
+                       [X("tna"), X("tnb"), "Sp2p", "K2"], [X("Sp")])
+        for i in range(nv):
+            scan(so[:, k * i:k * i + k], fl[:, n * i:n * i + k], fl[:, n * i + k:n * i + n], 0.0, ALU.add, ALU.add,
+                 [X("fl")], [X("so")])
+        last = so[:, k - 1:k * nv:k]
+        if L == 1:
+            tr(t("Sc"), tile(wb, "Sp"), [X("Sp")], [X("Sc")])
+            ts(tile(wb, "U", 16 + b0, 30), last, 0.25, -BIG, ALU.add, ALU.mult, [X("so")], [X("U")])
+            ts(tile(wb, "U", 0, 16 + b0), tile(wb, "V", 0, 16 + b0), 0.25, -BIG, ALU.add, ALU.mult, [X("V")], [X("U")])
+            tr(t("Uc"), tile(wb, "U"), [X("U")], [X("Uc")])
+        else:
+            tr(tile(wb, "St"), tile(wb, "Sp"), [X("Sp")], [X("St")])
+            tt(t("Sc"), tile(wb, "St", 0, 16), tile(wb, "St", 16, 32), ALU.add, [X("St")], [X("Sc")])
+            e = 2 * (8 + b0)
+            for half, m in ((0, M0), (1, M1)):
+                ts(tile(wb, "U", e + half, 30, 2), last, 0.25, m, ALU.add, ALU.mult, [X("so"), "K2"], [X("U")])
+            for half, m in ((0, M0), (1, M1)):
+                ts(tile(wb, "U", half, e, 2), tile(wb, "V", 0, 8 + b0), 0.25, m, ALU.add, ALU.mult, [X("V"), "K2"], [X("U")])
+            tr(tile(wb, "Ut"), tile(wb, "U"), [X("U")], [X("Ut")])
+            tt(t("Uc"), tile(wb, "Ut", 0, 16), tile(wb, "Ut", 16, 32), ALU.add, [X("Ut")], [X("Uc")])
+        col = lambda i: tile(wb, "col", i, i + 1)
+        wide = lambda s, m: wb[:, at[s]:at[s] + 32 * m]
+        tt(t("x1"), t("Sc"), t("Uc"), ALU.max, [X("Sc"), X("Uc")], [X("x")])
+        tt(t("x2"), t("Sc"), t("Uc"), ALU.min, [X("Sc"), X("Uc")], [X("x")])
+        ts(t("f"), t("Uc"), 0.0, (k - 0.5) / (16 * W), ALU.is_lt, ALU.subtract, [X("Uc")], [X("x")])
+        red(col(0), t("x1"), ALU.min, [X("x")], [X("c0")])
+        red(col(1), t("x2"), ALU.max, [X("x")], [X("c0")])
+        red(col(2), t("f"), ALU.add, [X("x")], [X("c0")])
+        ts(tile(wb, "mb0"), MLO, col(0), None, ALU.max, None, [X("c0"), "MSK"], [X("mb")])
+        ts(tile(wb, "mb1"), MHI, col(1), None, ALU.min, None, [X("c0"), "MSK"], [X("mb")])
+        ts(tile(wb, "mb2"), OWN, col(2), BIG, ALU.mult, ALU.mult, [X("c0"), "OWN"], [X("mb")])
+        tr(wide("tb0", 3), wide("mb0", 3), [X("mb")], [X("tb")])
+        red(col(3), tile(wb, "tb0"), ALU.min, [X("tb")], [X("c1")])
+        red(col(4), tile(wb, "tb1"), ALU.max, [X("tb")], [X("c1")])
+        red(col(5), tile(wb, "tb2"), ALU.add, [X("tb")], [X("c1")])
+        ts(col(6), col(5), col(3), col(4), ALU.min, ALU.max, [X("c1")], [X("t")])
+        ts(t("gt"), t("Sc"), col(6), None, ALU.is_gt, None, [X("t")], [X("g")])
+        ts(t("ge"), t("Sc"), col(6), None, ALU.is_ge, None, [X("t")], [X("g")])
+        scan(t("cge"), kc[:, 608:608 + W], t("ge"), 0.0, ALU.add, ALU.add, [X("g"), "ZERO"], [X("cum")])
+        scan(t("cg"), kc[:, 608:608 + W], t("gt"), 0.0, ALU.add, ALU.add, [X("g"), "ZERO"], [X("cum")])
+        tt(t("e"), t("gt"), t("ge"), ALU.add, [X("g")], [X("cum")])
+        ts(tile(wb, "mc0"), TRI, t("cge", W - 1, W), None, ALU.mult, None, [X("cum"), "TRI"], [X("mc")])
+        ts(tile(wb, "mc1"), UP, t("cg", W - 1, W), None, ALU.mult, None, [X("cum"), "UP"], [X("mc")])
+        tt(t("dx"), t("cge"), t("cg"), ALU.subtract, [X("cum")], [X("mc")])
+        ts(t("dy"), t("e"), -2048.0, 2048.0, ALU.mult, ALU.add, [X("cum")], [X("mc")])
+        tr(wide("tc0", 2), wide("mc0", 2), [X("mc")], [X("tc")])
+        tt(t("dd"), t("dx"), t("dy"), ALU.add, [X("mc")], [X("tc")])
+        red(col(7), tile(wb, "tc0"), ALU.add, [X("tc")], [X("c2")])
+        red(col(8), tile(wb, "tc1"), ALU.add, [X("tc")], [X("c2")])
+        red(col(9), wide("tc0", 2), ALU.add, [X("tc")], [X("c2")])
+        ts(t("ns"), t("dd"), col(9), float(k), ALU.add, ALU.is_gt, [X("c2")], [X("ab")])
+        ts(t("A"), t("cge"), col(7), -1.0, ALU.add, ALU.add, [X("c2")], [X("ab")])
+        ts(t("B"), t("cg"), col(8), float(k - 1), ALU.subtract, ALU.add, [X("c2")], [X("ab")])
+        tt(t("nz"), t("ns"), Z1 if L == 1 else Z2, ALU.mult, [X("ab"), "MSK", "K2b"], [X("mz")])
+        tt(t("m"), t("A"), t("B"), ALU.min, [X("ab")], [X("mz")])
+        tt(t("dest"), t("m"), t("nz"), ALU.add, [X("mz")], [X("dest")])
+        cp(T["od%d" % L][:], t("dest"), [X("dest")], [X("od")])
+
+    def relu4(out, n, skip, bank0, w):
+        for b in range(4):
+            o, src, name = out[:, 4 * skip + b:4 * (skip + n):4], T["ps%d" % (bank0 + b)][:, 0:n], "ps%d" % (bank0 + b)
+            if b % 2 == 0:
+                act(o, src, ACT.Relu, [name], [w], scale=0.03125)
+            else:
+                ts(o, src, 0.0, 0.03125, ALU.max, ALU.mult, [name], [w])
+        cut("a")
+
+    pick("u1", C)
+    quant(T.xq[:, 0:224], T.xs[:, 0:224], T.xb[:, 0:896], ["xb0"], ["xq"])
+    quant(T.xq[:, 224:448], T.xs[:, 224:448], T.xb[:, 896:1792], ["xb1"], ["xq"])
+    cut("v")
+    scores("u1", C, T.xq[:], T.xs[:], ["xq"])
+    pick("u2", A)
+    select(1)
+    cp(T.win1[:].indirect(T.od1[:]), VAL1, ["od1", "VAL"], ["win1"])
+    scan(T.ex1[:], C1, T.win1[:, 0:A], 0.0, ALU.add, ALU.min, ["win1", "C1"], ["ex1"])
+    ts(T.of[:], T.ex1[:, 3:A:4], PT, None, ALU.add, None, ["ex1", "F4"], ["of"])
+    act(T.ft[:, 448:896], T.xb[:].indirect(T.of[:, 28:56]), ACT.Copy, ["of", "xb0", "xb1"], ["ft"])
+    cut("a")
+    cp(T.ft[:, 0:448], T.xb[:].indirect(T.of[:, 0:28]), ["of", "xb0", "xb1"], ["ft"])
+    quant(T.fq[:], T.fs[:], T.ft[:], ["ft"], ["fq"])
+    cut("v")
+    for b in range(4):
+        mm(4 + b, A, T.wq[:, 128 * b:128 * b + 128], T.wp[:, 128 * b:128 * b + 128], T.fq[:], T.fs[:], ["w", "fq"])
+    ts(PM16, PM, 16.0, None, ALU.mult, None, ["F4"], ["K2a"])
+    ts(N0, PH, -1.0, 1.0, ALU.mult, ALU.add, ["F4"], ["K2"])
+    ts(M0, PH, BIG, -BIG, ALU.mult, ALU.add, ["F4"], ["K2"])
+    ts(M1, PH, -BIG, None, ALU.mult, None, ["F4"], ["K2"])
+    ts(kj[:, 0:B], ki[:, 32:32 + B], 3, None, ALU.bitwise_and, None, ["R14"], ["K2a"])
+    ts(kc[:, 640:672], J16, PM, None, ALU.is_equal, None, ["F4", "J"], ["K2a"])
+    relu4(T.ht, A, 0, 4, "ht")
+    quant(T.hq[:], T.hs[:], T.ht[:], ["ht"], ["hq"])
+    cut("v")
+    scores("u2", A, T.hq[:], T.hs[:], ["hq"])
+    ts(Z2, kf[:, 0:16], PM16, float(B + 1), ALU.add, ALU.add, ["K2a"], ["K2b"])
+    ts(C2, kj[:, 0:B], PQ, HOLD, ALU.is_equal, ALU.mult, ["K2a"], ["K2b"])
+    tt(kc[:, 672:704], kc[:, 640:672], RROW, ALU.mult, ["K2a", "RROW"], ["K2b"])
+    red(kc[:, 704:705], kc[:, 672:688], ALU.add, ["K2b"], ["K2c"])
+    red(kc[:, 705:706], kc[:, 688:704], ALU.add, ["K2b"], ["K2c"])
+    cp(T.oread[:], kc[:, 704:706], ["K2c"], ["oread"])
+    cut("v")
+
+    select(2)
+    cp(T.win2[:].indirect(T.od2[:]), VAL2, ["od2", "VAL"], ["win2"])
+    scan(T.ex2[:], C2, T.win2[:, 0:B], 0.0, ALU.add, ALU.min, ["win2", "K2b"], ["ex2"])
+    ts(T.og[:], T.ex2[:].indirect(T.oread[:]), PT, None, ALU.add, None, ["ex2", "oread"], ["og"])
+    act(T.gt[:, 256:512], T.ht[:].indirect(T.og[:, 16:32]), ACT.Copy, ["og", "ht"], ["gt"])
+    cut("a")
+    cp(T.gt[:, 0:256], T.ht[:].indirect(T.og[:, 0:16]), ["og", "ht"], ["gt"])
+    quant(T.gq[:, 112:240], T.gs[:, 112:240], T.gt[:], ["gt"], ["gq"])
+    cut("v")
+
+    def send(phase):
+        q, s = (T.gq, T.gs) if phase == 1 else (T.tq, T.ts)
+        deps("g", ["gq" if phase == 1 else "tq"], [])
+        hm = _masks(topo.engines(core, hs[0]), (HOP,) * 4)
+        hin, arr = T.sem["hin%d" % phase], T.sem["arr%d" % phase]
+        xs = []
+        for j in range(4):
+            if phase == 1:
+                src, dst = (_u8(q[:, 128 + 32 * j:160 + 32 * j]), _u8(T.rq1[:])) if j < 2 else (s[:, 112:240], T.rs1[:])
+            else:
+                src, dst = (_u8(q[:, S + 28 * j:S + 28 * j + 28]), _u8(T.rq2[:])) if j < 2 else (s[:, 0:112], T.rs2[:])
+            xs.append(_xfer(topo, core, hs[j], hm[j], hin, src, dst))
+        g.remote_dma_fused(xs, local_sem=T.sem.sent)
+        for sizes, buf, wrap in ((DIRECT_CODES, q, _u8), (DIRECT_SCALES, s, lambda a: a)):
+            dm = _masks(topo.engines(core, near[0]), sizes)
+            xs = []
+            for i, d in enumerate(near):
+                a = 112 + 16 * (5 + i) + 2 if phase == 1 else S + S * (4 + i)
+                to = (S if phase == 1 else 128) + S * _slot(d, core, T, topo)
+                xs.append(_xfer(topo, core, d, dm[i], arr, wrap(buf[:, a:a + S]), wrap(buf[:, to:to + S])))
+            g.remote_dma_fused(xs, local_sem=T.sem.sent)
+        mark(new_stage("arr%d" % phase, _arrivals(core, T, topo)), [], ["land%d" % phase])
+
+    send(1)
+    ts(T.operm[:], kf[:, 0:16], PM16, float(A - 1), ALU.add, ALU.min, ["K2a"], ["operm"])
+    tt(T.a1[:], T.ft[:], T.ht[:], ALU.add, ["ft", "ht"], ["a1"])
+    act(T.v1[:], T.win1[:, 0:A].indirect(T.operm[:]), ACT.Copy, ["operm", "win1"], ["v1"])
+    for p in range(8):
+        act(T.gcomp[:, 56 * p:56 * p + 56], T.gt[:, 64 * p + 8:64 * p + 64], ACT.Copy, ["gt"], ["gcomp"])
+    cut("a")
+    cp(T.x2[:].indirect(T.of[:]), T.a1[:], ["a1", "of", "x2"], ["x2a"])
+    cut("v")
+
+    for b in range(4):
+        mm(4 + b, 128, T.zq[:, 128 * b:128 * b + 128], T.zp[:, 128 * b:128 * b + 128], T.gq[:, 14:142], T.gs[:, 14:142],
+           ["z", "gq", "land1"])
+    relu4(T.tt, 114, S, 4, "tt")
+    quant(T.tq[:, 0:128], T.ts[:, 0:128], T.tt[:], ["tt"], ["tq"])
+    cut("v")
+    send(2)
+    cp(T.win3[:].indirect(T.od2[:]), T.v1[:], ["od2", "v1"], ["win3"])
+    quant(T.eq[:], T.es[:], T.eb[:], ["eb"], ["eq"])
+    for p in range(8):
+        tt(T.yx[:, S * p:S * p + S], T.win3[:, S * order[p]:S * order[p] + S], kc[:, 272 + S * p:272 + S * p + S], ALU.mult,
+           ["win3", "C1"], ["yx0"])
+    ts(T.olb[:], T.win3[:, 0:B], 0.25, None, ALU.mult, None, ["win3"], ["olb"])
+    tt(T.yx[:, 128:156], T.yx[:, 0:B:4], T.yx[:, 1:B:4], ALU.add, ["yx0"], ["yx1"])
+    tt(T.yx[:, 160:188], T.yx[:, 2:B:4], T.yx[:, 3:B:4], ALU.add, ["yx0"], ["yx1"])
+    dma("y", [(T.ol[i:i + 1, :], T.olb[16 * i:16 * i + 1, :]) for i in range(8)], ["olb"], [])
+    tt(T.yx[:, 192:220], T.yx[:, 128:156], T.yx[:, 160:188], ALU.add, ["yx1"], ["yx2"])
+    ts(T.ox[:], T.yx[:, 192:220], 1.0 / HOLD, PT, ALU.mult, ALU.add, ["yx2"], ["ox"])
+    act(T.il[:, 0:8 * B:2], T.xb[:].indirect(T.ox[:]), ACT.Copy, ["ox"], ["il"])
+    cut("a")
+    quant(T.vq[:], T.vs[:], T.vb[:], ["vb"], ["vq"])
+    cut("v")
+
+    for b in range(4):
+        mm(b, 128, T.eq[:, 128 * b:128 * b + 128], T.es[:, 128 * b:128 * b + 128], T.tq[:, 98:226], T.ts[:, 98:226],
+           ["eq", "tq", "land2"])
+    for b in range(4):
+        tt(T.il[:, 2 * b + 1:8 * B:8], T.gcomp[:, b:4 * B:4], T["ps%d" % b][:, 16:128], ALU.add, ["gcomp", "ps%d" % b], ["il"])
+    scan(T.io2[:], T.keep[:], T.il[:], 0.0, ALU.mult, ALU.add, ["il", "keep"], ["io2"])
+    cp(T.x2[:].indirect(T.ox[:]), T.io2[:, 1:8 * B:2], ["io2", "ox", "x2a"], ["x2b"])
+    for h in range(2):
+        a, b = 224 * h, 224 * h + 224
+        quant(T.oq[:, a:b], T.osb[:, a:b], T.x2[:, 4 * a:4 * b], ["x2b"], ["oq%d" % h])
+        cut("v")
+        mm(4 + h, 224, T.vq[:], T.vs[:], T.oq[:, a:b], T.osb[:, a:b], ["vq", "oq%d" % h])
+        dma("y", [(T.oc[:, 4 * a:4 * b], _u8(T.oq[:, a:b]))], ["oq%d" % h], [])
+    dma("y", [(T.osc[4 * i:4 * i + 4, :], T.osb[32 * i:32 * i + 4, :]) for i in (0, 1)], ["oq0", "oq1"], [])
+    act(T.yb[:, 0:224], T.ps4[:, 0:224], ACT.Copy, ["ps4"], ["y0"])
+    cp(T.yb[:, 224:448], T.ps5[:, 0:224], ["ps5"], ["y1"])
+    dma("a", [(T.y[:, 0:224], T.yb[:, 0:224])], ["y0"], [])
+    dma("y", [(T.y[:, 224:448], T.yb[:, 224:448])], ["y1"], [])
+    dma("a", [(T.osc[4 * i:4 * i + 4, :], T.osb[32 * i:32 * i + 4, :]) for i in (2, 3)], ["oq0", "oq1"], [])
+
+    g.wait_ge(T.sem.sent, 2 * (4 * HOP + sum(DIRECT_CODES) + sum(DIRECT_SCALES)))
+    for st in stages:
+        if not st["waited"]:
+            need("g", st)

@@ -7,6 +7,9 @@ HOLD = float(2 ** 20)
 NS1, NS2 = 16, 9
 NV1, NV2 = 28 - NS1, 14 - NS2
 Q4, U8 = "float8_e4m3fn_x4", "uint8"
+FV, GV = 28, 16
+X1 = 28
+O1 = 256
 
 
 def _sb(n, d):
@@ -27,10 +30,10 @@ SCRATCH = {
     "gt": _sb(512, "bfloat16"), "gq": _sb(240, Q4), "gs": _sb(240, U8),
     "tt": _sb(512, "bfloat16"), "tq": _sb(240, Q4), "ts": _sb(240, U8),
     "gcomp": _sb(4 * B, "bfloat16"), "il": _sb(8 * B, "bfloat16"), "io2": _sb(8 * B, "bfloat16"),
-    "keep": _sb(8 * B, "bfloat16"), "a1": _sb(4 * A, "bfloat16"),
+    "keep": _sb(8 * B, "bfloat16"), "fh": _sb(8 * A, "bfloat16"), "a1": _sb(8 * A, "bfloat16"),
     "oq": _sb(C, Q4), "osb": _sb(C, U8), "yb": _sb(C, "float32"),
     "rq1": _sb(32, Q4), "rs1": _sb(128, U8), "rq2": _sb(28, Q4), "rs2": _sb(112, U8),
-    "ki": _sb(160, "int32"), "kj": _sb(128, "int32"), "kf": _sb(1280, "float32"), "kc": _sb(768, "float32"),
+    "ki": _sb(32, "int32"), "kj": _sb(128, "int32"), "kf": _sb(1280, "float32"), "kc": _sb(896, "float32"),
     "opick": _sb(16, "uint16"), "oread": _sb(2, "uint16"), "operm": _sb(16, "uint16"),
     "od1": _sb(32, "uint16"), "od2": _sb(16, "uint16"),
     "of": _sb(56, "uint16"), "og": _sb(32, "uint16"), "ox": _sb(28, "uint16"),
@@ -38,15 +41,16 @@ SCRATCH = {
     "junk1": _sb(NS1 * C, "bfloat16"), "junk2": _sb(NS2 * A, "bfloat16"),
     "fl1": _sb(NV1 * C, "bfloat16"), "fl2": _sb(NV2 * A, "bfloat16"),
     "so1": _sb(NV1 * C // 2, "bfloat16"), "so2": _sb(NV2 * A // 2, "bfloat16"),
-    "w1": _sb(1280, "float32"), "w2": _sb(1280, "float32"),
-    "win1": _sb(960, "float32"), "win2": _sb(480, "float32"), "win3": _sb(480, "float32"),
+    "wa": _sb(1024, "float32"), "w1": _sb(1024, "float32"), "w2": _sb(1024, "float32"),
+    "win1": _sb(4608, "float32"), "win2": _sb(2304, "float32"), "win3": _sb(2304, "float32"),
+    "val1": _sb(512, "float32"),
     "ex1": _sb(A, "float32"), "ex2": _sb(B, "float32"), "v1": _sb(256, "float32"),
     "olb": _sb(B, "float32"), "yx": _sb(256, "float32"),
 }
 for _i in range(8):
     SCRATCH["ps%d" % _i] = ("psum", [128, 512], "float32")
 
-NPOOL = 140
+NPOOL = 130
 SEMAPHORES = ["arr1", "arr2", "hin1", "hin2", "sent"] + ["s%d" % _i for _i in range(NPOOL)]
 
 ALU = AluOpType
@@ -138,7 +142,7 @@ def rank_program(g, core, T, topo):
     known = {e: set() for e in eng}
     stage = {e: None for e in eng}
     stages = []
-    writer, readers = {}, {}
+    writer, readers, latest = {}, {}, {}
 
     def new_stage(sem=None, count=0):
         if sem is None:
@@ -177,7 +181,12 @@ def rank_program(g, core, T, topo):
     def op(e, call, r, w):
         deps(e, r, w)
         if stage[e] is None:
-            stage[e] = new_stage()
+            old = latest.get(e)
+            if old is not None and old["k"] in known[e]:
+                stage[e] = new_stage(old["sem"], old["n"])
+            else:
+                stage[e] = new_stage()
+            latest[e] = stage[e]
         st = stage[e]
         call().then_inc(T.sem[st["sem"]], 1)
         st["n"] += 1
@@ -239,179 +248,202 @@ def rank_program(g, core, T, topo):
         else:
             op("g", lambda: g.iota(out, pattern, base, cm, allow_small_or_imprecise_dtypes=True), [], w)
 
+    def choose(out, in_, pattern, o, fill, base, cm, r, w):
+        op("g", lambda: g.affine_select(out, in_, pattern, o, fill, base, cm), r, w)
+
     dma("a", [(T.u1b[:], T.u1[:])], [], ["u1b"])
     dma("y", [(T.xb[:, 0:896], T.x[:, 0:896])], [], ["xb0"])
     dma("a", [(T.xb[:, 896:1792], T.x[:, 896:1792])], [], ["xb1"])
-    dma("y", [(T.u2b[:], T.u2[:])], [], ["u2b"])
-    dma("y", [(_u8(T.wq[:]), T.wc[:]), (T.wp[:], T.ws[:])], ["xb0", "xb1"], ["w"])
+    dma("y", [(T.u2b[:], T.u2[:])], ["xb0", "xb1"], ["u2b"])
+    dma("y", [(_u8(T.wq[:]), T.wc[:]), (T.wp[:], T.ws[:])], [], ["w"])
     dma("y", [(_u8(T.zq[:]), T.zc[:]), (T.zp[:], T.zs[:])], [], ["z"])
     dma("y", [(T.vb[:], T.v[:]), (T.x2[:], T.x[:])], [], ["vb", "x2"])
 
-    kf, kc, ki, kj = T.kf, T.kc, T.ki, T.kj
-    J32, J16, JH, R4 = kf[:, 0:32], kf[:, 32:64], kf[:, 64:96], kf[:, 96:320]
-    VAL1, VAL2, RROW = kf[:, 320:832], kf[:, 832:1088], kf[:, 1088:1120]
+    kf, kc, ki, kj, wa = T.kf, T.kc, T.ki, T.kj, T.wa
+    KR, R4 = kf[:, 64:128], kf[:, 128:352]
+    VAL1, VAL2, J16 = T.val1[:], kf[:, 864:1120], kf[:, 1120:1136]
+
+    def rounds(L):
+        W = 32 if L == 1 else 16
+        return W, 128, 128 + 4 * (W + 1), 128 + 4 * (2 * W + 1), 128 + 4 * (3 * W + 2), 128 + 4 * (4 * W + 2)
+
+    def round_constants(L):
+        wb, k = T["w%d" % L], (A if L == 1 else B)
+        W, pre, d1, post, d0, out = rounds(L)
+        a, b = "Ra%d" % L, "Rb%d" % L
+        iota(wb[:, pre:pre + 4 * W], [[0, 4 * W]], 1, 0, [a])
+        iota(wb[:, pre + 4 * W:pre + 4 * W + 1], [[0, 1]], -(k + W), -W, [a])
+        iota(wb[:, pre + 4 * W + 2:pre + 4 * W + 3], [[0, 1]], k, W, [a])
+        iota(wb[:, post:post + 4 * (W + 1)], [[0, 4 * (W + 1)]], 0, 0, [a])
+        iota(wb[:, d0:d0 + 4 * W], [[-1, W], [0, 4]], -(k + 1), -W, [b + "0"])
+        choose(wb[:, d0:d0 + 4 * W], wb[:, d0:d0 + 4 * W], [[0, W], [-1, 4]], ALU.is_ge, 1.0, 2, 0, [b + "0"], [b + "1"])
+        choose(wb[:, d0:d0 + 4 * W], wb[:, d0:d0 + 4 * W], [[0, W], [1, 4]], ALU.is_ge, 0.0, -2, 0, [b + "1"], [b])
+        cut("g")
+
     iota(ki[:, 0:16], [[16, 2], [32, 4], [0, 2]], 0, 0, ["ipick"], True)
-    iota(ki[:, 16:17], [[0, 1]], 0, 1, ["ip"], True)
     cut("g")
-    iota(J32, [[1, 32]], 0, 0, ["J"])
-    iota(J16, [[0, 2], [1, 16]], 0, 0, ["J"])
-    iota(JH, [[1, 2], [0, 16]], 0, 0, ["J"])
+    pen, tri, upn = (kc[0:32, 32 * i:32 * i + 32] for i in (1, 2, 3))
+    iota(kc[0:32, 32:96], [[1, 2], [0, 32]], 0, 0, ["M0"])
+    iota(upn, [[0, 32]], -1, 0, ["M0"])
+    iota(KR, [[0, 64]], 1, 0, ["M0"])
+    choose(pen, pen, [[-16, 2], [0, 16]], ALU.is_ge, BIG, 0, 1, ["M0"], ["M1"])
+    choose(tri, tri, [[-16, 2], [0, 16]], ALU.is_ge, 0.0, 0, 1, ["M0"], ["M1"])
+    choose(upn, upn, [[16, 2], [0, 16]], ALU.is_ge, 0.0, 15, -1, ["M0"], ["M1"])
+    choose(KR, KR, [[1, 64]], ALU.not_equal, 0.0, -32, 0, ["M0"], ["KR"])
+    choose(pen, pen, [[16, 2], [0, 16]], ALU.is_ge, BIG, 15, -1, ["M1"], ["M2"])
+    choose(tri, tri, [[1, 32]], ALU.is_gt, 0.0, 0, -1, ["M1"], ["M2"])
+    choose(upn, upn, [[-1, 32]], ALU.is_gt, 0.0, 0, 1, ["M1"], ["M2"])
     cut("g")
+    dma("y", [(kc[32 * a:32 * a + 32, 32:128], kc[0:32, 32:128]) for a in (1, 2, 3)], ["M2"], ["MASK"])
+    round_constants(1)
+    iota(kf[:, 0:32], [[-4, 32]], 0, 1, ["N0"])
+    iota(kf[:, 32:64], [[0, 8], [-1, 4]], 0, 0, ["N0"])
+    iota(kf[:, 1136:1144], [[-256, 8]], 0, 16, ["N0"])
+    iota(kf[:, 1144:1152], [[0, 4], [1, 2]], 0, 0, ["N0"])
     iota(R4, [[0, 56], [1, 4]], 0, 0, ["R4"])
+    choose(kf[:, 0:64], kf[:, 0:64], [[0, 2], [-4, 32]], ALU.is_ge, 0.0, 0, 1, ["N0"], ["N1"])
+    choose(kf[:, 1136:1152], kf[:, 1136:1152], [[0, 2], [-16, 8]], ALU.is_ge, 0.0, 0, 1, ["N0"], ["N1"])
+    choose(kf[:, 0:64], kf[:, 0:64], [[0, 2], [4, 32]], ALU.is_ge, 0.0, 3, -1, ["N1"], ["N2"])
+    choose(kf[:, 1136:1152], kf[:, 1136:1152], [[0, 2], [16, 8]], ALU.is_ge, 0.0, 15, -1, ["N1"], ["N2"])
     cut("g")
-    iota(VAL1, [[4, 32], [128, 16]], 0, 0, ["VAL"])
-    iota(VAL2, [[4, 16], [64, 16]], 0, 0, ["VAL"])
-    iota(ki[:, 32:32 + B], [[0, 8], [1, S]], 2, 0, ["R14"], True)
+    iota(VAL1, [[4, 32], [128, 16]], 0, 0, ["VAL1"])
+    cut("g")
     for p in range(8):
-        iota(kf[:, 1088 + 4 * p:1092 + 4 * p], [[4, 4]], S * order[p] + 1, 0, ["RROW"])
+        iota(kf[:, 608 + 32 * p:640 + 32 * p], [[4, 4], [0, 8]], S * order[p] + 1, 0, ["RR0"])
+    choose(kf[:, 608:864], kf[:, 608:864], [[0, 2], [1, 16], [16, 8]], ALU.is_equal, 0.0, 0, -1, ["RR0"], ["RR"])
     cut("g")
+    iota(J16, [[1, 16]], 0, 0, ["J16"])
+    iota(VAL2, [[4, 16], [64, 16]], 0, 0, ["VAL2"])
+    round_constants(2)
     iota(T.keep[:], [[0, 4 * B], [1, 2]], 0, 0, ["keep"])
-    iota(T.eb[:], [[0, 2048]], 1, 0, ["eb0"])
-    op("g", lambda: g.affine_select(T.eb[:], T.eb[:], [[1, 4], [-1, 512]], ALU.is_equal, 0.0, 0, 4), ["eb0"], ["eb"])
+    for b in range(4):
+        o = (b + 1) % 2
+        choose(T.eb[:, 512 * b:512 * b + 512], T.keep[:, o:o + 512], [[-1, 512]], ALU.is_equal, 0.0, b, 4, ["keep"], ["eb"])
     cut("g")
 
-    w1, w2 = T.w1, T.w2
-    names = ["V", "U", "Sp", "Sc", "Uc", "x1", "x2", "f", "mb0", "mb1", "mb2", "tb0", "tb1", "tb2", "col", "gt", "ge",
-             "cg", "cge", "e", "mc0", "mc1", "tc0", "tc1", "dx", "dy", "dd", "A", "B", "ns", "m", "nz", "dest", "St", "Ut"]
-    at = {n: 32 * i for i, n in enumerate(names)}
-
-    def tile(wb, n, a=0, b=32, s=1):
-        return wb[:, at[n] + a:at[n] + b:s]
-
-    ms(tile(w1, "V"), -1.0, ["V1p"])
-    ms(tile(w2, "V"), -1.0, ["V2p"])
-    ms(tile(w1, "U", 30, 32), BIG, ["U1"])
-    ms(tile(w2, "U", 30, 32), BIG, ["U2"])
-    ms(tile(w1, "Sp"), -BIG, ["Sp1p"])
-    ms(tile(w2, "Sp"), -BIG, ["Sp2p"])
+    XX, T1, O1_, MB, T2, O2, ZJ, ZB, ZT, MC, TC, O3, COL = 0, 64, 192, 256, 320, 448, 512, 544, 576, 608, 672, 736, 800
+    for wb, n in ((T.w1, "1"), (T.w2, "2")):
+        ms(wb[:, 0:32], -1.0, ["Vp" + n])
+        ms(wb[:, 64:128], -BIG, ["Spp" + n])
+    ms(wa[:, T1:T1 + 32], -BIG, ["KK"])
+    ms(wa[:, T1 + 96:T1 + 97], -BIG, ["KK"])
+    ms(wa[:, T1 + 97:T1 + 128], BIG, ["KK"])
+    ms(wa[:, T2:T2 + 32], -BIG, ["KK"])
+    ms(wa[:, T2 + 96:T2 + 128], BIG, ["KK"])
     ms(T.tt[:, 0:4 * S], 0.0, ["tt"])
-    ms(kc[:, 608:640], 0.0, ["ZERO"])
-    ZERO = kc[:, 608:640]
     cp(T.opick[:], ki[:, 0:16], ["ipick"], ["opick"])
-    P = ki[:, 16:17]
-    ts(kj[:, 112:113], P, 15, None, ALU.bitwise_and, None, ["ip"], ["I4"])
-    ts(kj[:, 113:114], P, 15, 2, ALU.bitwise_and, ALU.logical_shift_right, ["ip"], ["I4"])
-    ts(kj[:, 114:115], P, 3, None, ALU.bitwise_and, None, ["ip"], ["I4"])
-    ts(kj[:, 115:116], P, 4, 1, ALU.logical_shift_right, ALU.bitwise_and, ["ip"], ["I4"])
-    cp(kc[:, 0:4], kj[:, 112:116], ["I4"], ["F4"])
-    PM, PQ, PT, PH = kc[:, 0:1], kc[:, 1:2], kc[:, 2:3], kc[:, 3:4]
-    PM32, PM16, N0, M0, M1 = kc[:, 4:5], kc[:, 5:6], kc[:, 6:7], kc[:, 7:8], kc[:, 8:9]
-    OWN, TRI0, TRI, UP, MLO, MHI = (kc[:, 32 * i:32 * i + 32] for i in range(1, 7))
-    Z1, Z2, C1, C2 = kc[:, 224:256], kc[:, 256:272], kc[:, 272:496], kc[:, 496:608]
-    ts(PM32, PM, 32.0, None, ALU.mult, None, ["F4"], ["F5"])
-    ts(OWN, JH, PH, None, ALU.is_equal, None, ["F4", "J"], ["OWN"])
-    ts(TRI0, J16, PM, None, ALU.is_gt, None, ["F4", "J"], ["OWN"])
-    tt(TRI, TRI0, OWN, ALU.mult, ["OWN"], ["TRI"])
-    ts(MLO, OWN, -2.0 * BIG, BIG, ALU.mult, ALU.add, ["OWN"], ["MSK"])
-    ts(MHI, OWN, 2.0 * BIG, -BIG, ALU.mult, ALU.add, ["OWN"], ["MSK"])
-    ts(Z1, J32, PM32, float(A + 1), ALU.add, ALU.add, ["F5", "J"], ["MSK"])
-    tt(UP, OWN, TRI, ALU.subtract, ["OWN", "TRI"], ["UP"])
-    ts(C1, R4, PQ, HOLD, ALU.is_equal, ALU.mult, ["R4", "F4"], ["C1"])
-    cut("v")
+    PT, NPQ, PM16, PH, N0 = (kc[:, i:i + 1] for i in range(5))
+    PEN, TRI, UPN = (kc[:, 32 * i:32 * i + 32] for i in (1, 2, 3))
+    C1, C1A = kc[:, 256:480], kc[:, 480:704]
+    C2 = kc[:, 704:816]
 
-    def pick(u, n):
-        q, s, pq, ps = T[u + "q"], T[u + "s"], T[u + "pq"], T[u + "ps"]
-        quant(q[:], s[:], T[u + "b"][:], [u + "b"], [u + "q"])
-        cp(pq[:].bitcast(dt.uint32), q[:].bitcast(dt.uint32).indirect(T.opick[:]), [u + "q", "opick"], [u + "pq"])
+    def pick_codes(u):
+        cp(T[u + "pq"][:].bitcast(dt.uint32), T[u + "q"][:].bitcast(dt.uint32).indirect(T.opick[:]), [u + "q", "opick"], [u + "pq"])
         cut("v")
-        act(ps[:], s[:].indirect(T.opick[:]), ACT.Copy, [u + "q", "opick"], [u + "ps"])
+
+    def pick_scales(u):
+        act(T[u + "ps"][:], T[u + "s"][:].indirect(T.opick[:]), ACT.Copy, [u + "q", "opick"], [u + "ps"])
         cut("a")
 
-    def scores(u, n, q, s, name):
-        pq, ps = T[u + "pq"], T[u + "ps"]
-        mm(0, n, T[u + "q"][:], T[u + "s"][:], q, s, [u + "q"] + name)
-        mm(1, n, pq[:, 0:128], ps[:, 0:128], q, s, [u + "pq", u + "ps"] + name)
-        mm(2, n, pq[:, 128:256], ps[:, 128:256], q, s, [u + "pq", u + "ps"] + name)
-        mm(3, n, pq[:, 128:256], ps[:, 128:256], q, s, [u + "pq", u + "ps"] + name)
+    def rows(u, bank, h, n, q, s, name):
+        mm(bank, n, T[u + "pq"][:, 128 * h:128 * h + 128], T[u + "ps"][:, 128 * h:128 * h + 128], q, s, [u + "pq", u + "ps"] + name)
 
-    def select(L):
-        n, k, wb, ns, nv = (C, A, w1, NS1, NV1) if L == 1 else (A, B, w2, NS2, NV2)
-        tn, junk, fl, so = T["tn%d" % L], T["junk%d" % L], T["fl%d" % L], T["so%d" % L]
-        nb, W = n // 32, (32 if L == 1 else 16)
-        hcol = 16 if L == 1 else 8
-        first = 128 if L == 1 else 64
+    def halves(h, half):
+        ts(T.w2[:, 96 + 16 * h + half:110 + 16 * h:2], T.tn2[:, 16 * h:A:32], PH if half else N0, None, ALU.mult, None,
+           ["tna2", "tnb2", "Spp2", "C1"], ["Sd2"])
+
+    spare = {
+        1: [lambda: tr(T.w1[:, 96:128], T.w1[:, 64:96], ["Sp1", "Spp1"], ["Sc1"]), None, None, None,
+            lambda: quant(T.u2q[:], T.u2s[:], T.u2b[:], ["u2b"], ["u2q"]), None],
+        2: [lambda: halves(0, 0), lambda: halves(0, 1), lambda: halves(1, 0), lambda: halves(1, 1),
+            lambda: tr(T.w2[:, 960:992], T.w2[:, 96:128], ["Sd2"], ["St2"]),
+            lambda: tt(T.w2[:, 992:1008], T.w2[:, 960:976], T.w2[:, 976:992], ALU.add, ["St2"], ["Sc2"])],
+    }
+
+    def between(L):
+        cut("v")
+        call = spare[L].pop(0)
+        if call is not None:
+            call()
+            cut("v")
+
+    def passes(L):
+        n, k, ns, nv = (C, A, NS1, NV1) if L == 1 else (A, B, NS2, NV2)
+        wb, tn, junk, fl, so = (T[s + str(L)] for s in ("w", "tn", "junk", "fl", "so"))
+        nb, first = n // 32, (224 if L == 1 else 64)
         X = lambda s: s + str(L)
-        t = lambda s, a=0, b=W, st=1: tile(wb, s, a, b, st)
-        tr(tn[:, 0:first], T.ps0[:, 0:first], ["ps0"], [X("tna")])
-        cut("v")
-        tr(tn[:, first:n], T.ps0[:, first:n], ["ps0"], [X("tnb")])
-        cut("v")
         for i in range(ns):
             h, b = (0, i) if i < nb else (1, i - nb)
             c = 32 * b + 16 * h
             act(junk[:, n * i:n * i + n], T["ps1" if h == 0 else "ps3"][:, 0:n], ACT.Sign,
-                ["ps1" if h == 0 else "ps3", X("tna") if c < first else X("tnb"), X("V") + "p"], [X("V")],
-                bias=tn[:, c:c + 1], scale=-1.0, accum_out=tile(wb, "V", hcol * h + b, hcol * h + b + 1))
+                ["ps1" if h == 0 else "ps3", X("tna") if c < first else X("tnb"), X("Vp")], [X("V")],
+                bias=tn[:, c:c + 1], scale=-1.0, accum_out=wb[:, 16 * h + b:16 * h + b + 1])
         cut("a")
         b0 = ns - nb
         for i in range(nv):
             c = 32 * (b0 + i) + 16
             ts(fl[:, n * i:n * i + n], T.ps2[:, 0:n], tn[:, c:c + 1], 0.5, ALU.is_lt, ALU.subtract,
-               ["ps2", X("tna"), X("tnb")], [X("fl")])
-        if L == 1:
-            for h in range(2):
-                cp(tile(wb, "Sp", 16 * h, 16 * h + nb), tn[:, 16 * h:n:32], [X("tna"), X("tnb"), "Sp1p"], [X("Sp")])
-        else:
-            for h in range(2):
-                for half, m in ((0, N0), (1, PH)):
-                    ts(tile(wb, "Sp", 16 * h + half, 16 * h + 2 * nb, 2), tn[:, 16 * h:n:32], m, None, ALU.mult, None,
-                       [X("tna"), X("tnb"), "Sp2p", "K2"], [X("Sp")])
+               ["ps2", X("tna"), X("tnb")], [X("fl%d" % (i // (nv - 1)))])
+            if i >= nv - 2:
+                cut("v")
+        for h in range(2):
+            cp(wb[:, 64 + 16 * h:64 + 16 * h + nb], tn[:, 16 * h:n:32], [X("tna"), X("tnb"), X("Spp")], [X("Sp")])
+        cut("v")
         for i in range(nv):
             scan(so[:, k * i:k * i + k], fl[:, n * i:n * i + k], fl[:, n * i + k:n * i + n], 0.0, ALU.add, ALU.add,
-                 [X("fl")], [X("so")])
-        last = so[:, k - 1:k * nv:k]
-        if L == 1:
-            tr(t("Sc"), tile(wb, "Sp"), [X("Sp")], [X("Sc")])
-            ts(tile(wb, "U", 16 + b0, 30), last, 0.25, -BIG, ALU.add, ALU.mult, [X("so")], [X("U")])
-            ts(tile(wb, "U", 0, 16 + b0), tile(wb, "V", 0, 16 + b0), 0.25, -BIG, ALU.add, ALU.mult, [X("V")], [X("U")])
-            tr(t("Uc"), tile(wb, "U"), [X("U")], [X("Uc")])
-        else:
-            tr(tile(wb, "St"), tile(wb, "Sp"), [X("Sp")], [X("St")])
-            tt(t("Sc"), tile(wb, "St", 0, 16), tile(wb, "St", 16, 32), ALU.add, [X("St")], [X("Sc")])
-            e = 2 * (8 + b0)
-            for half, m in ((0, M0), (1, M1)):
-                ts(tile(wb, "U", e + half, 30, 2), last, 0.25, m, ALU.add, ALU.mult, [X("so"), "K2"], [X("U")])
-            for half, m in ((0, M0), (1, M1)):
-                ts(tile(wb, "U", half, e, 2), tile(wb, "V", 0, 8 + b0), 0.25, m, ALU.add, ALU.mult, [X("V"), "K2"], [X("U")])
-            tr(tile(wb, "Ut"), tile(wb, "U"), [X("U")], [X("Ut")])
-            tt(t("Uc"), tile(wb, "Ut", 0, 16), tile(wb, "Ut", 16, 32), ALU.add, [X("Ut")], [X("Uc")])
-        col = lambda i: tile(wb, "col", i, i + 1)
-        wide = lambda s, m: wb[:, at[s]:at[s] + 32 * m]
-        tt(t("x1"), t("Sc"), t("Uc"), ALU.max, [X("Sc"), X("Uc")], [X("x")])
-        tt(t("x2"), t("Sc"), t("Uc"), ALU.min, [X("Sc"), X("Uc")], [X("x")])
-        ts(t("f"), t("Uc"), 0.0, (k - 0.5) / (16 * W), ALU.is_lt, ALU.subtract, [X("Uc")], [X("x")])
-        red(col(0), t("x1"), ALU.min, [X("x")], [X("c0")])
-        red(col(1), t("x2"), ALU.max, [X("x")], [X("c0")])
-        red(col(2), t("f"), ALU.add, [X("x")], [X("c0")])
-        ts(tile(wb, "mb0"), MLO, col(0), None, ALU.max, None, [X("c0"), "MSK"], [X("mb")])
-        ts(tile(wb, "mb1"), MHI, col(1), None, ALU.min, None, [X("c0"), "MSK"], [X("mb")])
-        ts(tile(wb, "mb2"), OWN, col(2), BIG, ALU.mult, ALU.mult, [X("c0"), "OWN"], [X("mb")])
-        tr(wide("tb0", 3), wide("mb0", 3), [X("mb")], [X("tb")])
-        red(col(3), tile(wb, "tb0"), ALU.min, [X("tb")], [X("c1")])
-        red(col(4), tile(wb, "tb1"), ALU.max, [X("tb")], [X("c1")])
-        red(col(5), tile(wb, "tb2"), ALU.add, [X("tb")], [X("c1")])
-        ts(col(6), col(5), col(3), col(4), ALU.min, ALU.max, [X("c1")], [X("t")])
-        ts(t("gt"), t("Sc"), col(6), None, ALU.is_gt, None, [X("t")], [X("g")])
-        ts(t("ge"), t("Sc"), col(6), None, ALU.is_ge, None, [X("t")], [X("g")])
-        scan(t("cge"), kc[:, 608:608 + W], t("ge"), 0.0, ALU.add, ALU.add, [X("g"), "ZERO"], [X("cum")])
-        scan(t("cg"), kc[:, 608:608 + W], t("gt"), 0.0, ALU.add, ALU.add, [X("g"), "ZERO"], [X("cum")])
-        tt(t("e"), t("gt"), t("ge"), ALU.add, [X("g")], [X("cum")])
-        ts(tile(wb, "mc0"), TRI, t("cge", W - 1, W), None, ALU.mult, None, [X("cum"), "TRI"], [X("mc")])
-        ts(tile(wb, "mc1"), UP, t("cg", W - 1, W), None, ALU.mult, None, [X("cum"), "UP"], [X("mc")])
-        tt(t("dx"), t("cge"), t("cg"), ALU.subtract, [X("cum")], [X("mc")])
-        ts(t("dy"), t("e"), -2048.0, 2048.0, ALU.mult, ALU.add, [X("cum")], [X("mc")])
-        tr(wide("tc0", 2), wide("mc0", 2), [X("mc")], [X("tc")])
-        tt(t("dd"), t("dx"), t("dy"), ALU.add, [X("mc")], [X("tc")])
-        red(col(7), tile(wb, "tc0"), ALU.add, [X("tc")], [X("c2")])
-        red(col(8), tile(wb, "tc1"), ALU.add, [X("tc")], [X("c2")])
-        red(col(9), wide("tc0", 2), ALU.add, [X("tc")], [X("c2")])
-        ts(t("ns"), t("dd"), col(9), float(k), ALU.add, ALU.is_gt, [X("c2")], [X("ab")])
-        ts(t("A"), t("cge"), col(7), -1.0, ALU.add, ALU.add, [X("c2")], [X("ab")])
-        ts(t("B"), t("cg"), col(8), float(k - 1), ALU.subtract, ALU.add, [X("c2")], [X("ab")])
-        tt(t("nz"), t("ns"), Z1 if L == 1 else Z2, ALU.mult, [X("ab"), "MSK", "K2b"], [X("mz")])
-        tt(t("m"), t("A"), t("B"), ALU.min, [X("ab")], [X("mz")])
-        tt(t("dest"), t("m"), t("nz"), ALU.add, [X("mz")], [X("dest")])
-        cp(T["od%d" % L][:], t("dest"), [X("dest")], [X("od")])
+                 [X("fl%d" % (i // (nv - 1)))], [X("so")])
+        between(L)
+        cp(wb[:, 16 + b0:16 + nb], so[:, k - 1:k * nv:k], [X("so"), X("Vp")], [X("Vv")])
+        between(L)
+
+    def tail(L):
+        k, wb = (A if L == 1 else B), T["w%d" % L]
+        W, pre, d1, post, d0, out = rounds(L)
+        X = lambda s: s + str(L)
+        a = lambda at, n: wa[:, at:at + n]
+        Vt, U, Sp = wb[:, 0:32], wb[:, 32:64], wb[:, 64:96]
+        Sc = wb[:, 96:128] if L == 1 else wb[:, 992:1008]
+        for h in range(2):
+            act(a(ZJ + 16 * h, 16), wb[:, 16 * h:16 * h + 16], ACT.Sign, [X("V"), X("Vv")], ["zc"], bias=0.25,
+                accum_out=a(COL + h, 1))
+        for h in range(2):
+            act(a(ZB + 16 * h, 16), a(T2 + 96, 16), ACT.Identity, ["zc", "KK"], ["zb"], scale=a(COL + h, 1),
+                bias=(513 - 2 * k) * BIG / 32)
+        cut("a")
+        ts(U, Vt, 0.25, -BIG, ALU.add, ALU.mult, [X("V"), X("Vv")], [X("U")])
+        between(L)
+        tt(a(XX, 32), Sp, U, ALU.min, [X("U"), X("Sp")], ["xx"])
+        tt(a(XX + 32, 32), Sp, U, ALU.max, [X("U"), X("Sp")], ["xx"])
+        between(L)
+        tr(a(T1 + 32, 64), a(XX, 64), ["xx"], ["t1"])
+        between(L)
+        scan(a(O1_, 64), a(T1 + 64, 64), a(T1, 64), BIG, ALU.min, ALU.max, ["t1", "KK"], ["o1"])
+        cut("v")
+        tr(a(ZT, 32), a(ZB, 32), ["zb"], ["zt"])
+        cut("v")
+        ts(a(MB, 32), PEN, -1.0, a(O1_ + 63, 1), ALU.mult, ALU.add, ["o1", "MASK"], ["mb"])
+        ts(a(MB + 32, 32), PEN, a(O1_ + 31, 1), None, ALU.add, None, ["o1", "MASK"], ["mb"])
+        cut("v")
+        red(a(COL + 2, 1), a(ZT, 32), ALU.add, ["zt"], ["zz"])
+        cut("v")
+        tr(a(T2 + 32, 64), a(MB, 64), ["mb"], ["t2"])
+        between(L)
+        scan(a(O2, 64), a(T2 + 64, 64), a(T2, 64), a(COL + 2, 1), ALU.min, ALU.max, ["t2", "zz"], ["o2"])
+        t = a(O2 + 63, 1)
+        ts(wb[:, d1 + 1:post:4], Sc, t, None, ALU.is_gt, None, ["o2", X("Sc")], [X("fg")])
+        ts(wb[:, d1:post:4], Sc, t, None, ALU.is_equal, None, ["o2", X("Sc")], [X("fg")])
+        scan(wb[:, d1 + 2:d0:4], wb[:, d1 + 1:d0:4], wb[:, pre:post:4], wb[:, pre + 4 * W + 2:pre + 4 * W + 3], ALU.add, ALU.add,
+             [X("fg"), X("Ra")], [X("cum")])
+        own, ceq, tot = wb[:, post + 2:post + 3], wb[:, post + 6:d0:4], wb[:, d0 - 2:d0 - 1]
+        ts(a(MC, 32), TRI, tot, -1.0 / 32, ALU.mult, ALU.add, [X("cum")], ["mc"])
+        ts(a(MC + 32, 32), UPN, own, (k - 1) / 32, ALU.mult, ALU.add, [X("cum")], ["mc"])
+        tr(a(TC, 64), a(MC, 64), ["mc"], ["tc"])
+        scan(a(O3, 64), KR, a(TC, 64), 0.0, ALU.mult, ALU.add, ["tc", "KR"], ["o3"])
+        p1, p2 = a(O3 + 31, 1), a(O3 + 63, 1)
+        ts(wb[:, d1 + 3:post:4], ceq, p1, p2, ALU.add, ALU.min, ["o3"], [X("ws")])
+        ts(wb[:, d0 + 1:out:4], ceq, p1, p2, ALU.add, ALU.is_le, ["o3", X("Rb")], [X("ws")])
+        scan(wb[:, out:out + 4 * W], wb[:, d0:out], wb[:, d1:post], 0.0, ALU.mult, ALU.add, [X("ws")], [X("dest")])
+        ts(T["od%d" % L][:], wb[:, out + 3:out + 4 * W:4], own, None, ALU.subtract, None, [X("dest")], [X("od")])
 
     def relu4(out, n, skip, bank0, w):
         for b in range(4):
@@ -422,48 +454,73 @@ def rank_program(g, core, T, topo):
                 ts(o, src, 0.0, 0.03125, ALU.max, ALU.mult, [name], [w])
         cut("a")
 
-    pick("u1", C)
-    quant(T.xq[:, 0:224], T.xs[:, 0:224], T.xb[:, 0:896], ["xb0"], ["xq"])
-    quant(T.xq[:, 224:448], T.xs[:, 224:448], T.xb[:, 896:1792], ["xb1"], ["xq"])
+    quant(T.u1q[:], T.u1s[:], T.u1b[:], ["u1b"], ["u1q"])
+    pick_codes("u1")
+    pick_scales("u1")
+    quant(T.xq[:, 0:A], T.xs[:, 0:A], T.xb[:, 0:896], ["xb0"], ["xq0"])
     cut("v")
-    scores("u1", C, T.xq[:], T.xs[:], ["xq"])
-    pick("u2", A)
-    select(1)
-    cp(T.win1[:].indirect(T.od1[:]), VAL1, ["od1", "VAL"], ["win1"])
+    mm(0, A, T.u1q[:], T.u1s[:], T.xq[:, 0:A], T.xs[:, 0:A], ["u1q", "xq0"])
+    quant(T.xq[:, A:C], T.xs[:, A:C], T.xb[:, 896:1792], ["xb1"], ["xq1"])
+    cut("v")
+    rows("u1", 1, 0, C, T.xq[:], T.xs[:], ["xq0", "xq1"])
+    mm(4, A, T.u1q[:], T.u1s[:], T.xq[:, A:C], T.xs[:, A:C], ["u1q", "xq1"])
+    rows("u1", 2, 1, C, T.xq[:], T.xs[:], ["xq0", "xq1"])
+    rows("u1", 3, 1, C, T.xq[:], T.xs[:], ["xq0", "xq1"])
+    tr(T.tn1[:, 0:A], T.ps0[:, 0:A], ["ps0"], ["tna1"])
+    cut("v")
+    tr(T.tn1[:, A:C], T.ps4[:, 0:A], ["ps4"], ["tnb1"])
+    cut("v")
+    passes(1)
+    tail(1)
+    for i, (a, b) in enumerate(((0, 32), (32, 64), (1136, 1144), (1144, 1152))):
+        act(kc[:, 128 + 32 * i:128 + 32 * i + b - a], kf[:, a:b], ACT.Identity, ["N2"], ["F4"], accum_out=kc[:, i:i + 1])
+    act(C1A, R4, ACT.Abs, ["R4", "F4"], ["C1a"], bias=NPQ)
+    act(N0, PH, ACT.Identity, ["F4"], ["C1a"], scale=-1.0, bias=1.0)
+    act(C1, C1A, ACT.Relu, ["C1a"], ["C1"], scale=-HOLD, bias=HOLD)
+    cut("a")
+    pick_scales("u2")
+    act(T.yx[:, 0:128], kf[:, 608:736], ACT.Identity, ["RR"], ["C2"], accum_out=kc[:, 12:13])
+    act(T.yx[:, 128:256], kf[:, 736:864], ACT.Identity, ["RR"], ["C2"], accum_out=kc[:, 13:14])
+    for p in range(8):
+        act(kc[:, 704 + S * p:704 + S * p + S], kc[:, 258:272], ACT.Copy, ["C1"], ["C2"])
+    cut("a")
+    cp(T.win1[:].indirect(T.od1[:]), VAL1, ["od1", "VAL1"], ["win1"])
     scan(T.ex1[:], C1, T.win1[:, 0:A], 0.0, ALU.add, ALU.min, ["win1", "C1"], ["ex1"])
     ts(T.of[:], T.ex1[:, 3:A:4], PT, None, ALU.add, None, ["ex1", "F4"], ["of"])
-    act(T.ft[:, 448:896], T.xb[:].indirect(T.of[:, 28:56]), ACT.Copy, ["of", "xb0", "xb1"], ["ft"])
+    act(T.ft[:, 16 * FV:896], T.xb[:].indirect(T.of[:, FV:56]), ACT.Copy, ["of", "xb0", "xb1"], ["ft"])
     cut("a")
-    cp(T.ft[:, 0:448], T.xb[:].indirect(T.of[:, 0:28]), ["of", "xb0", "xb1"], ["ft"])
+    cp(T.ft[:, 0:16 * FV], T.xb[:].indirect(T.of[:, 0:FV]), ["of", "xb0", "xb1"], ["ft"])
     quant(T.fq[:], T.fs[:], T.ft[:], ["ft"], ["fq"])
     cut("v")
     for b in range(4):
         mm(4 + b, A, T.wq[:, 128 * b:128 * b + 128], T.wp[:, 128 * b:128 * b + 128], T.fq[:], T.fs[:], ["w", "fq"])
-    ts(PM16, PM, 16.0, None, ALU.mult, None, ["F4"], ["K2a"])
-    ts(N0, PH, -1.0, 1.0, ALU.mult, ALU.add, ["F4"], ["K2"])
-    ts(M0, PH, BIG, -BIG, ALU.mult, ALU.add, ["F4"], ["K2"])
-    ts(M1, PH, -BIG, None, ALU.mult, None, ["F4"], ["K2"])
-    ts(kj[:, 0:B], ki[:, 32:32 + B], 3, None, ALU.bitwise_and, None, ["R14"], ["K2a"])
-    ts(kc[:, 640:672], J16, PM, None, ALU.is_equal, None, ["F4", "J"], ["K2a"])
+    pick_codes("u2")
     relu4(T.ht, A, 0, 4, "ht")
     quant(T.hq[:], T.hs[:], T.ht[:], ["ht"], ["hq"])
     cut("v")
-    scores("u2", A, T.hq[:], T.hs[:], ["hq"])
-    ts(Z2, kf[:, 0:16], PM16, float(B + 1), ALU.add, ALU.add, ["K2a"], ["K2b"])
-    ts(C2, kj[:, 0:B], PQ, HOLD, ALU.is_equal, ALU.mult, ["K2a"], ["K2b"])
-    tt(kc[:, 672:704], kc[:, 640:672], RROW, ALU.mult, ["K2a", "RROW"], ["K2b"])
-    red(kc[:, 704:705], kc[:, 672:688], ALU.add, ["K2b"], ["K2c"])
-    red(kc[:, 705:706], kc[:, 688:704], ALU.add, ["K2b"], ["K2c"])
-    cp(T.oread[:], kc[:, 704:706], ["K2c"], ["oread"])
+    mm(0, A, T.u2q[:], T.u2s[:], T.hq[:], T.hs[:], ["u2q", "hq"])
+    for bank, h in ((1, 0), (2, 1), (3, 1)):
+        rows("u2", bank, h, A, T.hq[:], T.hs[:], ["hq"])
+    cp(T.oread[:], kc[:, 12:14], ["C2"], ["oread"])
+    ts(T.operm[:], J16, PM16, float(A - 1), ALU.add, ALU.min, ["F4", "J16"], ["operm"])
     cut("v")
 
-    select(2)
-    cp(T.win2[:].indirect(T.od2[:]), VAL2, ["od2", "VAL"], ["win2"])
-    scan(T.ex2[:], C2, T.win2[:, 0:B], 0.0, ALU.add, ALU.min, ["win2", "K2b"], ["ex2"])
-    ts(T.og[:], T.ex2[:].indirect(T.oread[:]), PT, None, ALU.add, None, ["ex2", "oread"], ["og"])
-    act(T.gt[:, 256:512], T.ht[:].indirect(T.og[:, 16:32]), ACT.Copy, ["og", "ht"], ["gt"])
+    tr(T.tn2[:, 0:64], T.ps0[:, 0:64], ["ps0"], ["tna2"])
+    cut("v")
+    tr(T.tn2[:, 64:A], T.ps0[:, 64:A], ["ps0"], ["tnb2"])
+    cut("v")
+    passes(2)
+    tail(2)
+    act(T.fh[:, 0:8 * A:2], T.ft[:], ACT.Copy, ["ft"], ["fh"])
+    act(T.fh[:, 1:8 * A:2], T.ht[:], ACT.Copy, ["ht"], ["fh"])
+    act(T.v1[:], T.win1[:, 0:A].indirect(T.operm[:]), ACT.Copy, ["operm", "win1"], ["v1"])
     cut("a")
-    cp(T.gt[:, 0:256], T.ht[:].indirect(T.og[:, 0:16]), ["og", "ht"], ["gt"])
+    cp(T.win2[:].indirect(T.od2[:]), VAL2, ["od2", "VAL2"], ["win2"])
+    scan(T.ex2[:], C2, T.win2[:, 0:B], 0.0, ALU.add, ALU.min, ["win2", "C2"], ["ex2"])
+    ts(T.og[:], T.ex2[:].indirect(T.oread[:]), PT, None, ALU.add, None, ["ex2", "oread"], ["og"])
+    act(T.gt[:, 16 * GV:512], T.ht[:].indirect(T.og[:, GV:32]), ACT.Copy, ["og", "ht"], ["gt"])
+    cut("a")
+    cp(T.gt[:, 0:16 * GV], T.ht[:].indirect(T.og[:, 0:GV]), ["og", "ht"], ["gt"])
     quant(T.gq[:, 112:240], T.gs[:, 112:240], T.gt[:], ["gt"], ["gq"])
     cut("v")
 
@@ -491,13 +548,25 @@ def rank_program(g, core, T, topo):
         mark(new_stage("arr%d" % phase, _arrivals(core, T, topo)), [], ["land%d" % phase])
 
     send(1)
-    ts(T.operm[:], kf[:, 0:16], PM16, float(A - 1), ALU.add, ALU.min, ["K2a"], ["operm"])
-    tt(T.a1[:], T.ft[:], T.ht[:], ALU.add, ["ft", "ht"], ["a1"])
-    act(T.v1[:], T.win1[:, 0:A].indirect(T.operm[:]), ACT.Copy, ["operm", "win1"], ["v1"])
+    cp(T.win3[:].indirect(T.od2[:]), T.v1[:], ["od2", "v1"], ["win3"])
+    cut("v")
+    for p in range(8):
+        act(T.yx[:, S * p:S * p + S], T.win3[:, S * order[p]:S * order[p] + S], ACT.Identity, ["win3"], ["yx0"], bias=2048.0 * p)
+    cut("a")
     for p in range(8):
         act(T.gcomp[:, 56 * p:56 * p + 56], T.gt[:, 64 * p + 8:64 * p + 64], ACT.Copy, ["gt"], ["gcomp"])
+    act(T.olb[:], T.win3[:, 0:B], ACT.Identity, ["win3"], ["olb"], scale=0.25)
     cut("a")
-    cp(T.x2[:].indirect(T.of[:]), T.a1[:], ["a1", "of", "x2"], ["x2a"])
+    for h in range(2):
+        scan(T.a1[:, 896 * h:896 * h + 896], T.keep[:], T.fh[:, 896 * h:896 * h + 896], 0.0, ALU.mult, ALU.add, ["fh", "keep"], ["a1"])
+    scan(T.yx[:, 128:128 + B], kc[:, 256:256 + B], T.yx[:, 0:B], 0.0, ALU.add, ALU.min, ["yx0", "C1"], ["yx1"])
+    ts(kj[:, 0:28], T.yx[:, 131:128 + B:4], PT, None, ALU.add, None, ["yx1"], ["yx2"])
+    ts(kj[:, 32:60], kj[:, 0:28], 2047, None, ALU.bitwise_and, None, ["yx2"], ["yx3"])
+    cp(T.ox[:], kj[:, 32:60], ["yx3"], ["ox"])
+    cut("v")
+    act(T.il[:, 0:8 * B:2], T.xb[:].indirect(T.ox[:]), ACT.Copy, ["ox"], ["il"])
+    cut("a")
+    cp(T.x2[:].indirect(T.of[:, 0:X1]), T.a1[:, 1:32 * X1:2], ["a1", "of", "x2"], ["x2a"])
     cut("v")
 
     for b in range(4):
@@ -507,40 +576,31 @@ def rank_program(g, core, T, topo):
     quant(T.tq[:, 0:128], T.ts[:, 0:128], T.tt[:], ["tt"], ["tq"])
     cut("v")
     send(2)
-    cp(T.win3[:].indirect(T.od2[:]), T.v1[:], ["od2", "v1"], ["win3"])
     quant(T.eq[:], T.es[:], T.eb[:], ["eb"], ["eq"])
-    for p in range(8):
-        tt(T.yx[:, S * p:S * p + S], T.win3[:, S * order[p]:S * order[p] + S], kc[:, 272 + S * p:272 + S * p + S], ALU.mult,
-           ["win3", "C1"], ["yx0"])
-    ts(T.olb[:], T.win3[:, 0:B], 0.25, None, ALU.mult, None, ["win3"], ["olb"])
-    tt(T.yx[:, 128:156], T.yx[:, 0:B:4], T.yx[:, 1:B:4], ALU.add, ["yx0"], ["yx1"])
-    tt(T.yx[:, 160:188], T.yx[:, 2:B:4], T.yx[:, 3:B:4], ALU.add, ["yx0"], ["yx1"])
-    dma("y", [(T.ol[i:i + 1, :], T.olb[16 * i:16 * i + 1, :]) for i in range(8)], ["olb"], [])
-    tt(T.yx[:, 192:220], T.yx[:, 128:156], T.yx[:, 160:188], ALU.add, ["yx1"], ["yx2"])
-    ts(T.ox[:], T.yx[:, 192:220], 1.0 / HOLD, PT, ALU.mult, ALU.add, ["yx2"], ["ox"])
-    act(T.il[:, 0:8 * B:2], T.xb[:].indirect(T.ox[:]), ACT.Copy, ["ox"], ["il"])
-    cut("a")
+    cut("v")
+    cp(T.x2[:].indirect(T.of[:, X1:56]), T.a1[:, 32 * X1 + 1:8 * A:2], ["a1", "of", "x2a"], ["x2b"])
     quant(T.vq[:], T.vs[:], T.vb[:], ["vb"], ["vq"])
     cut("v")
 
     for b in range(4):
         mm(b, 128, T.eq[:, 128 * b:128 * b + 128], T.es[:, 128 * b:128 * b + 128], T.tq[:, 98:226], T.ts[:, 98:226],
            ["eq", "tq", "land2"])
+    dma("y", [(T.ol[i:i + 1, :], T.olb[16 * i:16 * i + 1, :]) for i in range(8)], ["olb", "land2"], [])
     for b in range(4):
         tt(T.il[:, 2 * b + 1:8 * B:8], T.gcomp[:, b:4 * B:4], T["ps%d" % b][:, 16:128], ALU.add, ["gcomp", "ps%d" % b], ["il"])
     scan(T.io2[:], T.keep[:], T.il[:], 0.0, ALU.mult, ALU.add, ["il", "keep"], ["io2"])
-    cp(T.x2[:].indirect(T.ox[:]), T.io2[:, 1:8 * B:2], ["io2", "ox", "x2a"], ["x2b"])
-    for h in range(2):
-        a, b = 224 * h, 224 * h + 224
-        quant(T.oq[:, a:b], T.osb[:, a:b], T.x2[:, 4 * a:4 * b], ["x2b"], ["oq%d" % h])
+    cp(T.x2[:].indirect(T.ox[:]), T.io2[:, 1:8 * B:2], ["io2", "ox", "x2a", "x2b"], ["x2c"])
+    parts = ((0, O1), (O1, C))
+    for h, (a, b) in enumerate(parts):
+        quant(T.oq[:, a:b], T.osb[:, a:b], T.x2[:, 4 * a:4 * b], ["x2c"], ["oq%d" % h])
         cut("v")
-        mm(4 + h, 224, T.vq[:], T.vs[:], T.oq[:, a:b], T.osb[:, a:b], ["vq", "oq%d" % h])
+        mm(4 + h, b - a, T.vq[:], T.vs[:], T.oq[:, a:b], T.osb[:, a:b], ["vq", "oq%d" % h])
         dma("y", [(T.oc[:, 4 * a:4 * b], _u8(T.oq[:, a:b]))], ["oq%d" % h], [])
     dma("y", [(T.osc[4 * i:4 * i + 4, :], T.osb[32 * i:32 * i + 4, :]) for i in (0, 1)], ["oq0", "oq1"], [])
-    act(T.yb[:, 0:224], T.ps4[:, 0:224], ACT.Copy, ["ps4"], ["y0"])
-    cp(T.yb[:, 224:448], T.ps5[:, 0:224], ["ps5"], ["y1"])
-    dma("a", [(T.y[:, 0:224], T.yb[:, 0:224])], ["y0"], [])
-    dma("y", [(T.y[:, 224:448], T.yb[:, 224:448])], ["y1"], [])
+    act(T.yb[:, 0:O1], T.ps4[:, 0:O1], ACT.Copy, ["ps4"], ["y0"])
+    cp(T.yb[:, O1:C], T.ps5[:, 0:C - O1], ["ps5"], ["y1"])
+    dma("a", [(T.y[:, 0:O1], T.yb[:, 0:O1])], ["y0"], [])
+    dma("y", [(T.y[:, O1:C], T.yb[:, O1:C])], ["y1"], [])
     dma("a", [(T.osc[4 * i:4 * i + 4, :], T.osb[32 * i:32 * i + 4, :]) for i in (2, 3)], ["oq0", "oq1"], [])
 
     g.wait_ge(T.sem.sent, 2 * (4 * HOP + sum(DIRECT_CODES) + sum(DIRECT_SCALES)))

@@ -7,7 +7,8 @@ HOLD = float(2 ** 20)
 NS1, NS2 = 16, 9
 NV1, NV2 = 28 - NS1, 14 - NS2
 Q4, U8 = "float8_e4m3fn_x4", "uint8"
-FV, GV = 28, 16
+GV = 16
+XA = 320
 X1 = 28
 O1 = 256
 
@@ -25,8 +26,8 @@ SCRATCH = {
     "vq": _sb(128, Q4), "vs": _sb(128, U8),
     "wq": _sb(512, Q4), "wp": _sb(512, U8), "zq": _sb(512, Q4), "zp": _sb(512, U8),
     "eb": _sb(2048, "bfloat16"), "eq": _sb(512, Q4), "es": _sb(512, U8),
-    "ft": _sb(4 * A, "bfloat16"), "fq": _sb(A, Q4), "fs": _sb(A, U8),
-    "ht": _sb(4 * A, "bfloat16"), "hq": _sb(A, Q4), "hs": _sb(A, U8),
+    "ft": _sb(4 * A, "bfloat16"), "fq": _sb(256, Q4), "fs": _sb(256, U8),
+    "ht": _sb(1024, "bfloat16"), "hq": _sb(256, Q4), "hs": _sb(256, U8),
     "gt": _sb(512, "bfloat16"), "gq": _sb(240, Q4), "gs": _sb(240, U8),
     "tt": _sb(512, "bfloat16"), "tq": _sb(240, Q4), "ts": _sb(240, U8),
     "gcomp": _sb(4 * B, "bfloat16"), "il": _sb(8 * B, "bfloat16"), "io2": _sb(8 * B, "bfloat16"),
@@ -35,7 +36,7 @@ SCRATCH = {
     "rq1": _sb(32, Q4), "rs1": _sb(128, U8), "rq2": _sb(28, Q4), "rs2": _sb(112, U8),
     "ki": _sb(32, "int32"), "kj": _sb(128, "int32"), "kf": _sb(1280, "float32"), "kc": _sb(896, "float32"),
     "opick": _sb(16, "uint16"), "oread": _sb(2, "uint16"), "operm": _sb(16, "uint16"),
-    "od1": _sb(32, "uint16"), "od2": _sb(16, "uint16"),
+    "od1": _sb(28, "uint16"), "od2": _sb(16, "uint16"),
     "of": _sb(56, "uint16"), "og": _sb(32, "uint16"), "ox": _sb(28, "uint16"),
     "tn1": _sb(C, "float32"), "tn2": _sb(A, "float32"),
     "junk1": _sb(NS1 * C, "bfloat16"), "junk2": _sb(NS2 * A, "bfloat16"),
@@ -43,14 +44,14 @@ SCRATCH = {
     "so1": _sb(NV1 * C // 2, "bfloat16"), "so2": _sb(NV2 * A // 2, "bfloat16"),
     "wa": _sb(1024, "float32"), "w1": _sb(1024, "float32"), "w2": _sb(1024, "float32"),
     "win1": _sb(4608, "float32"), "win2": _sb(2304, "float32"), "win3": _sb(2304, "float32"),
-    "val1": _sb(512, "float32"),
+    "val1": _sb(C, "float32"), "runs": ("dram", [8, 512], "float32"),
     "ex1": _sb(A, "float32"), "ex2": _sb(B, "float32"), "v1": _sb(256, "float32"),
     "olb": _sb(B, "float32"), "yx": _sb(256, "float32"),
 }
 for _i in range(8):
     SCRATCH["ps%d" % _i] = ("psum", [128, 512], "float32")
 
-NPOOL = 130
+NPOOL = 135
 SEMAPHORES = ["arr1", "arr2", "hin1", "hin2", "sent"] + ["s%d" % _i for _i in range(NPOOL)]
 
 ALU = AluOpType
@@ -220,9 +221,6 @@ def rank_program(g, core, T, topo):
     def ms(out, c, w):
         op("v", lambda: V.memset(out, c), [], w)
 
-    def red(out, in_, o, r, w):
-        op("v", lambda: V.tensor_reduce(out, in_, AxisListType.X, o), r, w)
-
     def tr(out, in_, r, w):
         op("v", lambda: V.transpose(out, in_), r, w)
 
@@ -252,19 +250,17 @@ def rank_program(g, core, T, topo):
         op("g", lambda: g.affine_select(out, in_, pattern, o, fill, base, cm), r, w)
 
     dma("a", [(T.u1b[:], T.u1[:])], [], ["u1b"])
-    dma("y", [(T.xb[:, 0:896], T.x[:, 0:896])], [], ["xb0"])
-    dma("a", [(T.xb[:, 896:1792], T.x[:, 896:1792])], [], ["xb1"])
+    dma("y", [(T.xb[:, 0:4 * XA], T.x[:, 0:4 * XA])], [], ["xb0"])
+    dma("a", [(T.xb[:, 4 * XA:4 * C], T.x[:, 4 * XA:4 * C])], [], ["xb1"])
     dma("y", [(T.u2b[:], T.u2[:])], ["xb0", "xb1"], ["u2b"])
     dma("y", [(_u8(T.wq[:]), T.wc[:]), (T.wp[:], T.ws[:])], [], ["w"])
-    dma("y", [(_u8(T.zq[:]), T.zc[:]), (T.zp[:], T.zs[:])], [], ["z"])
-    dma("y", [(T.vb[:], T.v[:]), (T.x2[:], T.x[:])], [], ["vb", "x2"])
 
     kf, kc, ki, kj, wa = T.kf, T.kc, T.ki, T.kj, T.wa
     KR, R4 = kf[:, 64:128], kf[:, 128:352]
     VAL1, VAL2, J16 = T.val1[:], kf[:, 864:1120], kf[:, 1120:1136]
 
     def rounds(L):
-        W = 32 if L == 1 else 16
+        W = 28 if L == 1 else 16
         return W, 128, 128 + 4 * (W + 1), 128 + 4 * (2 * W + 1), 128 + 4 * (3 * W + 2), 128 + 4 * (4 * W + 2)
 
     def round_constants(L):
@@ -282,19 +278,17 @@ def rank_program(g, core, T, topo):
 
     iota(ki[:, 0:16], [[16, 2], [32, 4], [0, 2]], 0, 0, ["ipick"], True)
     cut("g")
-    pen, tri, upn = (kc[0:32, 32 * i:32 * i + 32] for i in (1, 2, 3))
-    iota(kc[0:32, 32:96], [[1, 2], [0, 32]], 0, 0, ["M0"])
+    tri, upn = (kc[0:32, 32 * i:32 * i + 32] for i in (2, 3))
+    iota(tri, [[0, 32]], 1, 0, ["M0"])
     iota(upn, [[0, 32]], -1, 0, ["M0"])
     iota(KR, [[0, 64]], 1, 0, ["M0"])
-    choose(pen, pen, [[-16, 2], [0, 16]], ALU.is_ge, BIG, 0, 1, ["M0"], ["M1"])
     choose(tri, tri, [[-16, 2], [0, 16]], ALU.is_ge, 0.0, 0, 1, ["M0"], ["M1"])
     choose(upn, upn, [[16, 2], [0, 16]], ALU.is_ge, 0.0, 15, -1, ["M0"], ["M1"])
     choose(KR, KR, [[1, 64]], ALU.not_equal, 0.0, -32, 0, ["M0"], ["KR"])
-    choose(pen, pen, [[16, 2], [0, 16]], ALU.is_ge, BIG, 15, -1, ["M1"], ["M2"])
     choose(tri, tri, [[1, 32]], ALU.is_gt, 0.0, 0, -1, ["M1"], ["M2"])
     choose(upn, upn, [[-1, 32]], ALU.is_gt, 0.0, 0, 1, ["M1"], ["M2"])
     cut("g")
-    dma("y", [(kc[32 * a:32 * a + 32, 32:128], kc[0:32, 32:128]) for a in (1, 2, 3)], ["M2"], ["MASK"])
+    dma("y", [(kc[32 * a:32 * a + 32, 64:128], kc[0:32, 64:128]) for a in (1, 2, 3)], ["M2"], ["MASK"])
     round_constants(1)
     iota(kf[:, 0:32], [[-4, 32]], 0, 1, ["N0"])
     iota(kf[:, 32:64], [[0, 8], [-1, 4]], 0, 0, ["N0"])
@@ -306,7 +300,7 @@ def rank_program(g, core, T, topo):
     choose(kf[:, 0:64], kf[:, 0:64], [[0, 2], [4, 32]], ALU.is_ge, 0.0, 3, -1, ["N1"], ["N2"])
     choose(kf[:, 1136:1152], kf[:, 1136:1152], [[0, 2], [16, 8]], ALU.is_ge, 0.0, 15, -1, ["N1"], ["N2"])
     cut("g")
-    iota(VAL1, [[4, 32], [128, 16]], 0, 0, ["VAL1"])
+    iota(VAL1, [[4, 28], [112, 16]], 0, 0, ["VAL1"])
     cut("g")
     for p in range(8):
         iota(kf[:, 608 + 32 * p:640 + 32 * p], [[4, 4], [0, 8]], S * order[p] + 1, 0, ["RR0"])
@@ -321,28 +315,29 @@ def rank_program(g, core, T, topo):
         choose(T.eb[:, 512 * b:512 * b + 512], T.keep[:, o:o + 512], [[-1, 512]], ALU.is_equal, 0.0, b, 4, ["keep"], ["eb"])
     cut("g")
 
-    XX, T1, O1_, MB, T2, O2, ZJ, ZB, ZT, MC, TC, O3, COL = 0, 64, 192, 256, 320, 448, 512, 544, 576, 608, 672, 736, 800
+    XX, MB, T2, O2, ZJ, ZB, ZT, MC, TC, O3, COL = 32, 192, 320, 448, 512, 544, 576, 608, 672, 736, 800
     for wb, n in ((T.w1, "1"), (T.w2, "2")):
         ms(wb[:, 0:32], -1.0, ["Vp" + n])
         ms(wb[:, 64:128], -BIG, ["Spp" + n])
-    ms(wa[:, T1:T1 + 32], -BIG, ["KK"])
-    ms(wa[:, T1 + 96:T1 + 97], -BIG, ["KK"])
-    ms(wa[:, T1 + 97:T1 + 128], BIG, ["KK"])
+    for at, c in ((0, BIG), (48, BIG), (64, -BIG), (112, -BIG)):
+        ms(wa[:, XX + at:XX + at + 16], c, ["KK"])
     ms(wa[:, T2:T2 + 32], -BIG, ["KK"])
     ms(wa[:, T2 + 96:T2 + 128], BIG, ["KK"])
     ms(T.tt[:, 0:4 * S], 0.0, ["tt"])
+    ms(T.ht[:, 896:1024], 0.0, ["tt"])
     cp(T.opick[:], ki[:, 0:16], ["ipick"], ["opick"])
     PT, NPQ, PM16, PH, N0 = (kc[:, i:i + 1] for i in range(5))
-    PEN, TRI, UPN = (kc[:, 32 * i:32 * i + 32] for i in (1, 2, 3))
+    TRI, UPN = (kc[:, 32 * i:32 * i + 32] for i in (2, 3))
     C1, C1A = kc[:, 256:480], kc[:, 480:704]
     C2 = kc[:, 704:816]
 
-    def pick_codes(u):
-        cp(T[u + "pq"][:].bitcast(dt.uint32), T[u + "q"][:].bitcast(dt.uint32).indirect(T.opick[:]), [u + "q", "opick"], [u + "pq"])
+    def pick_codes(u, a=0, b=2):
+        cp(T[u + "pq"][:, 128 * a:128 * b].bitcast(dt.uint32), T[u + "q"][:].bitcast(dt.uint32).indirect(T.opick[:, 8 * a:8 * b]),
+           [u + "q", "opick"], [u + "pq"])
         cut("v")
 
-    def pick_scales(u):
-        act(T[u + "ps"][:], T[u + "s"][:].indirect(T.opick[:]), ACT.Copy, [u + "q", "opick"], [u + "ps"])
+    def pick_scales(u, a=0, b=2):
+        act(T[u + "ps"][:, 128 * a:128 * b], T[u + "s"][:].indirect(T.opick[:, 8 * a:8 * b]), ACT.Copy, [u + "q", "opick"], [u + "ps"])
         cut("a")
 
     def rows(u, bank, h, n, q, s, name):
@@ -353,11 +348,12 @@ def rank_program(g, core, T, topo):
            ["tna2", "tnb2", "Spp2", "C1"], ["Sd2"])
 
     spare = {
-        1: [lambda: tr(T.w1[:, 96:128], T.w1[:, 64:96], ["Sp1", "Spp1"], ["Sc1"]), None, None, None,
-            lambda: quant(T.u2q[:], T.u2s[:], T.u2b[:], ["u2b"], ["u2q"]), None],
-        2: [lambda: halves(0, 0), lambda: halves(0, 1), lambda: halves(1, 0), lambda: halves(1, 1),
+        1: [None, None, lambda: quant(T.u2q[:], T.u2s[:], T.u2b[:], ["u2b"], ["u2q"]), None, None,
+            lambda: pick_codes("u2", 0, 1), lambda: pick_codes("u2", 1, 2)],
+        2: [lambda: [halves(0, 0), halves(0, 1)], lambda: [halves(1, 0), halves(1, 1)],
             lambda: tr(T.w2[:, 960:992], T.w2[:, 96:128], ["Sd2"], ["St2"]),
-            lambda: tt(T.w2[:, 992:1008], T.w2[:, 960:976], T.w2[:, 976:992], ALU.add, ["St2"], ["Sc2"])],
+            lambda: tt(T.w2[:, 992:1008], T.w2[:, 960:976], T.w2[:, 976:992], ALU.add, ["St2"], ["Sc2"]),
+            None, None, None],
     }
 
     def between(L):
@@ -370,25 +366,33 @@ def rank_program(g, core, T, topo):
     def passes(L):
         n, k, ns, nv = (C, A, NS1, NV1) if L == 1 else (A, B, NS2, NV2)
         wb, tn, junk, fl, so = (T[s + str(L)] for s in ("w", "tn", "junk", "fl", "so"))
-        nb, first = n // 32, (224 if L == 1 else 64)
+        nb, first = n // 32, (XA if L == 1 else 128)
         X = lambda s: s + str(L)
         for i in range(ns):
             h, b = (0, i) if i < nb else (1, i - nb)
             c = 32 * b + 16 * h
             act(junk[:, n * i:n * i + n], T["ps1" if h == 0 else "ps3"][:, 0:n], ACT.Sign,
-                ["ps1" if h == 0 else "ps3", X("tna") if c < first else X("tnb"), X("Vp")], [X("V")],
+                ["ps1" if h == 0 else "ps3", X("tn0") if c < 64 else X("tna") if c < first else X("tnb"), X("Vp")], [X("V")],
                 bias=tn[:, c:c + 1], scale=-1.0, accum_out=wb[:, 16 * h + b:16 * h + b + 1])
         cut("a")
         b0 = ns - nb
         for i in range(nv):
             c = 32 * (b0 + i) + 16
             ts(fl[:, n * i:n * i + n], T.ps2[:, 0:n], tn[:, c:c + 1], 0.5, ALU.is_lt, ALU.subtract,
-               ["ps2", X("tna"), X("tnb")], [X("fl%d" % (i // (nv - 1)))])
+               ["ps2", X("tn0"), X("tna"), X("tnb")], [X("fl%d" % (i // (nv - 1)))])
+            if i == 0:
+                for h in range(2):
+                    cp(wb[:, 64 + 16 * h:64 + 16 * h + nb], tn[:, 16 * h:n:32], [X("tna"), X("tnb"), X("Spp")], [X("Sp")])
+                cut("v")
+            if i == 1 and L == 1:
+                tr(wb[:, 96:128], wb[:, 64:96], ["Sp1", "Spp1"], ["St1"])
+                cut("v")
+                dma("y", [(T.runs[:], wb[:, 96:128])], ["St1"], ["runs"])
+                dma("y", [(wb[:, 960:988], T.runs[:, 0:C])], ["runs"], ["Sc1"])
+                dma("y", [(_u8(T.zq[:]), T.zc[:]), (T.zp[:], T.zs[:])], [], ["z"])
+                dma("y", [(T.vb[:], T.v[:]), (T.x2[:], T.x[:])], [], ["vb", "x2"])
             if i >= nv - 2:
                 cut("v")
-        for h in range(2):
-            cp(wb[:, 64 + 16 * h:64 + 16 * h + nb], tn[:, 16 * h:n:32], [X("tna"), X("tnb"), X("Spp")], [X("Sp")])
-        cut("v")
         for i in range(nv):
             scan(so[:, k * i:k * i + k], fl[:, n * i:n * i + k], fl[:, n * i + k:n * i + n], 0.0, ALU.add, ALU.add,
                  [X("fl%d" % (i // (nv - 1)))], [X("so")])
@@ -401,8 +405,9 @@ def rank_program(g, core, T, topo):
         W, pre, d1, post, d0, out = rounds(L)
         X = lambda s: s + str(L)
         a = lambda at, n: wa[:, at:at + n]
+        back = lambda at: wa[:, at + 31:at - 1:-1]
         Vt, U, Sp = wb[:, 0:32], wb[:, 32:64], wb[:, 64:96]
-        Sc = wb[:, 96:128] if L == 1 else wb[:, 992:1008]
+        Sc = wb[:, 960:988] if L == 1 else wb[:, 992:1008]
         for h in range(2):
             act(a(ZJ + 16 * h, 16), wb[:, 16 * h:16 * h + 16], ACT.Sign, [X("V"), X("Vv")], ["zc"], bias=0.25,
                 accum_out=a(COL + h, 1))
@@ -412,21 +417,19 @@ def rank_program(g, core, T, topo):
         cut("a")
         ts(U, Vt, 0.25, -BIG, ALU.add, ALU.mult, [X("V"), X("Vv")], [X("U")])
         between(L)
-        tt(a(XX, 32), Sp, U, ALU.min, [X("U"), X("Sp")], ["xx"])
-        tt(a(XX + 32, 32), Sp, U, ALU.max, [X("U"), X("Sp")], ["xx"])
+        tt(a(XX + 16, 32), Sp, U, ALU.max, [X("U"), X("Sp")], ["xx"])
+        tt(a(XX + 80, 32), Sp, U, ALU.min, [X("U"), X("Sp")], ["xx"])
         between(L)
-        tr(a(T1 + 32, 64), a(XX, 64), ["xx"], ["t1"])
-        between(L)
-        scan(a(O1_, 64), a(T1 + 64, 64), a(T1, 64), BIG, ALU.min, ALU.max, ["t1", "KK"], ["o1"])
+        for x, m, c, o0, o1, idle in ((XX, MB + 64, BIG, ALU.min, ALU.max, T2), (XX + 64, MB, -BIG, ALU.max, ALU.min, T2 + 96)):
+            scan(a(m, 32), back(x), a(idle, 32), c, o0, o1, ["xx", "KK"], ["mb"])
+            scan(back(m + 32), a(x + 32, 32), a(idle, 32), c, o0, o1, ["xx", "KK"], ["mb"])
         cut("v")
         tr(a(ZT, 32), a(ZB, 32), ["zb"], ["zt"])
         cut("v")
-        ts(a(MB, 32), PEN, -1.0, a(O1_ + 63, 1), ALU.mult, ALU.add, ["o1", "MASK"], ["mb"])
-        ts(a(MB + 32, 32), PEN, a(O1_ + 31, 1), None, ALU.add, None, ["o1", "MASK"], ["mb"])
-        cut("v")
-        red(a(COL + 2, 1), a(ZT, 32), ALU.add, ["zt"], ["zz"])
-        cut("v")
-        tr(a(T2 + 32, 64), a(MB, 64), ["mb"], ["t2"])
+        act(a(ZJ, 32), a(ZT, 32), ACT.Identity, ["zt"], ["zz"], accum_out=a(COL + 2, 1))
+        cut("a")
+        tr(a(T2 + 32, 32), a(MB + 16, 32), ["mb"], ["t2"])
+        tr(a(T2 + 64, 32), a(MB + 80, 32), ["mb"], ["t2"])
         between(L)
         scan(a(O2, 64), a(T2 + 64, 64), a(T2, 64), a(COL + 2, 1), ALU.min, ALU.max, ["t2", "zz"], ["o2"])
         t = a(O2 + 63, 1)
@@ -435,20 +438,22 @@ def rank_program(g, core, T, topo):
         scan(wb[:, d1 + 2:d0:4], wb[:, d1 + 1:d0:4], wb[:, pre:post:4], wb[:, pre + 4 * W + 2:pre + 4 * W + 3], ALU.add, ALU.add,
              [X("fg"), X("Ra")], [X("cum")])
         own, ceq, tot = wb[:, post + 2:post + 3], wb[:, post + 6:d0:4], wb[:, d0 - 2:d0 - 1]
-        ts(a(MC, 32), TRI, tot, -1.0 / 32, ALU.mult, ALU.add, [X("cum")], ["mc"])
+        ts(a(MC, 32), TRI, tot, -1.0 / 32, ALU.mult, ALU.add, [X("cum"), "MASK"], ["mc"])
         ts(a(MC + 32, 32), UPN, own, (k - 1) / 32, ALU.mult, ALU.add, [X("cum")], ["mc"])
         tr(a(TC, 64), a(MC, 64), ["mc"], ["tc"])
+        between(L)
         scan(a(O3, 64), KR, a(TC, 64), 0.0, ALU.mult, ALU.add, ["tc", "KR"], ["o3"])
+        between(L)
         p1, p2 = a(O3 + 31, 1), a(O3 + 63, 1)
         ts(wb[:, d1 + 3:post:4], ceq, p1, p2, ALU.add, ALU.min, ["o3"], [X("ws")])
         ts(wb[:, d0 + 1:out:4], ceq, p1, p2, ALU.add, ALU.is_le, ["o3", X("Rb")], [X("ws")])
         scan(wb[:, out:out + 4 * W], wb[:, d0:out], wb[:, d1:post], 0.0, ALU.mult, ALU.add, [X("ws")], [X("dest")])
         ts(T["od%d" % L][:], wb[:, out + 3:out + 4 * W:4], own, None, ALU.subtract, None, [X("dest")], [X("od")])
 
-    def relu4(out, n, skip, bank0, w):
+    def relu4(out, n, skip, bank0, w, at=0, scalar=(0, 2)):
         for b in range(4):
-            o, src, name = out[:, 4 * skip + b:4 * (skip + n):4], T["ps%d" % (bank0 + b)][:, 0:n], "ps%d" % (bank0 + b)
-            if b % 2 == 0:
+            o, src, name = out[:, 4 * skip + b:4 * (skip + n):4], T["ps%d" % (bank0 + b)][:, at:at + n], "ps%d" % (bank0 + b)
+            if b in scalar:
                 act(o, src, ACT.Relu, [name], [w], scale=0.03125)
             else:
                 ts(o, src, 0.0, 0.03125, ALU.max, ALU.mult, [name], [w])
@@ -457,18 +462,20 @@ def rank_program(g, core, T, topo):
     quant(T.u1q[:], T.u1s[:], T.u1b[:], ["u1b"], ["u1q"])
     pick_codes("u1")
     pick_scales("u1")
-    quant(T.xq[:, 0:A], T.xs[:, 0:A], T.xb[:, 0:896], ["xb0"], ["xq0"])
+    quant(T.xq[:, 0:XA], T.xs[:, 0:XA], T.xb[:, 0:4 * XA], ["xb0"], ["xq0"])
     cut("v")
-    mm(0, A, T.u1q[:], T.u1s[:], T.xq[:, 0:A], T.xs[:, 0:A], ["u1q", "xq0"])
-    quant(T.xq[:, A:C], T.xs[:, A:C], T.xb[:, 896:1792], ["xb1"], ["xq1"])
+    mm(0, XA, T.u1q[:], T.u1s[:], T.xq[:, 0:XA], T.xs[:, 0:XA], ["u1q", "xq0"])
+    quant(T.xq[:, XA:C], T.xs[:, XA:C], T.xb[:, 4 * XA:4 * C], ["xb1"], ["xq1"])
     cut("v")
     rows("u1", 1, 0, C, T.xq[:], T.xs[:], ["xq0", "xq1"])
-    mm(4, A, T.u1q[:], T.u1s[:], T.xq[:, A:C], T.xs[:, A:C], ["u1q", "xq1"])
+    mm(4, C - XA, T.u1q[:], T.u1s[:], T.xq[:, XA:C], T.xs[:, XA:C], ["u1q", "xq1"])
     rows("u1", 2, 1, C, T.xq[:], T.xs[:], ["xq0", "xq1"])
     rows("u1", 3, 1, C, T.xq[:], T.xs[:], ["xq0", "xq1"])
-    tr(T.tn1[:, 0:A], T.ps0[:, 0:A], ["ps0"], ["tna1"])
+    tr(T.tn1[:, 0:64], T.ps0[:, 0:64], ["ps0"], ["tn01"])
     cut("v")
-    tr(T.tn1[:, A:C], T.ps4[:, 0:A], ["ps4"], ["tnb1"])
+    tr(T.tn1[:, 64:XA], T.ps0[:, 64:XA], ["ps0"], ["tna1"])
+    cut("v")
+    tr(T.tn1[:, XA:C], T.ps4[:, 0:C - XA], ["ps4"], ["tnb1"])
     cut("v")
     passes(1)
     tail(1)
@@ -478,49 +485,65 @@ def rank_program(g, core, T, topo):
     act(N0, PH, ACT.Identity, ["F4"], ["C1a"], scale=-1.0, bias=1.0)
     act(C1, C1A, ACT.Relu, ["C1a"], ["C1"], scale=-HOLD, bias=HOLD)
     cut("a")
-    pick_scales("u2")
+    pick_scales("u2", 0, 1)
+    pick_scales("u2", 1, 2)
     act(T.yx[:, 0:128], kf[:, 608:736], ACT.Identity, ["RR"], ["C2"], accum_out=kc[:, 12:13])
     act(T.yx[:, 128:256], kf[:, 736:864], ACT.Identity, ["RR"], ["C2"], accum_out=kc[:, 13:14])
     for p in range(8):
         act(kc[:, 704 + S * p:704 + S * p + S], kc[:, 258:272], ACT.Copy, ["C1"], ["C2"])
     cut("a")
     cp(T.win1[:].indirect(T.od1[:]), VAL1, ["od1", "VAL1"], ["win1"])
-    scan(T.ex1[:], C1, T.win1[:, 0:A], 0.0, ALU.add, ALU.min, ["win1", "C1"], ["ex1"])
-    ts(T.of[:], T.ex1[:, 3:A:4], PT, None, ALU.add, None, ["ex1", "F4"], ["of"])
-    act(T.ft[:, 16 * FV:896], T.xb[:].indirect(T.of[:, FV:56]), ACT.Copy, ["of", "xb0", "xb1"], ["ft"])
+    for n, a, b in (("a", 0, 128), ("b", 128, A)):
+        scan(T.ex1[:, a:b], kc[:, 256 + a:256 + b], T.win1[:, a:b], 0.0, ALU.add, ALU.min, ["win1", "C1"], ["ex1" + n])
+        cut("v")
+    for n, a, b in (("a", 0, 128), ("b", 128, A)):
+        ts(T.of[:, a // 4:b // 4], T.ex1[:, a + 3:b:4], PT, None, ALU.add, None, ["ex1" + n, "F4"], ["of" + n, "of"])
+        cut("v")
+    act(T.ft[:, 512:896], T.xb[:].indirect(T.of[:, 32:56]), ACT.Copy, ["ofb", "xb0", "xb1"], ["ft"])
     cut("a")
-    cp(T.ft[:, 0:16 * FV], T.xb[:].indirect(T.of[:, 0:FV]), ["of", "xb0", "xb1"], ["ft"])
-    quant(T.fq[:], T.fs[:], T.ft[:], ["ft"], ["fq"])
+    cp(T.ft[:, 0:512], T.xb[:].indirect(T.of[:, 0:32]), ["ofa", "xb0", "xb1"], ["fta", "ft"])
     cut("v")
-    for b in range(4):
-        mm(4 + b, A, T.wq[:, 128 * b:128 * b + 128], T.wp[:, 128 * b:128 * b + 128], T.fq[:], T.fs[:], ["w", "fq"])
-    pick_codes("u2")
-    relu4(T.ht, A, 0, 4, "ht")
-    quant(T.hq[:], T.hs[:], T.ht[:], ["ht"], ["hq"])
-    cut("v")
-    mm(0, A, T.u2q[:], T.u2s[:], T.hq[:], T.hs[:], ["u2q", "hq"])
-    for bank, h in ((1, 0), (2, 1), (3, 1)):
-        rows("u2", bank, h, A, T.hq[:], T.hs[:], ["hq"])
     cp(T.oread[:], kc[:, 12:14], ["C2"], ["oread"])
     ts(T.operm[:], J16, PM16, float(A - 1), ALU.add, ALU.min, ["F4", "J16"], ["operm"])
     cut("v")
-
-    tr(T.tn2[:, 0:64], T.ps0[:, 0:64], ["ps0"], ["tna2"])
+    quant(T.fq[:, 0:128], T.fs[:, 0:128], T.ft[:, 0:512], ["fta"], ["fq0"])
     cut("v")
-    tr(T.tn2[:, 64:A], T.ps0[:, 64:A], ["ps0"], ["tnb2"])
+    quant(T.fq[:, 128:256], T.fs[:, 128:256], T.ft[:, 384:896], ["ft"], ["fq1"])
+    cut("v")
+    for h in range(2):
+        for b in range(4):
+            mm(4 * h + b, 128, T.wq[:, 128 * b:128 * b + 128], T.wp[:, 128 * b:128 * b + 128],
+               T.fq[:, 128 * h:128 * h + 128], T.fs[:, 128 * h:128 * h + 128], ["w", "fq%d" % h])
+    relu4(T.ht, 128, 0, 0, "hta")
+    cut("v")
+    relu4(T.ht, 96, 128, 4, "htb", 32, (0, 2, 3))
+    cut("v")
+    quant(T.hq[:, 0:128], T.hs[:, 0:128], T.ht[:, 0:512], ["hta"], ["hqa"])
+    cut("v")
+    mm(0, 128, T.u2q[:], T.u2s[:], T.hq[:, 0:128], T.hs[:, 0:128], ["u2q", "hqa"])
+    quant(T.hq[:, 128:256], T.hs[:, 128:256], T.ht[:, 512:1024], ["htb", "tt"], ["hq"])
+    cut("v")
+    rows("u2", 1, 0, A, T.hq[:, 0:A], T.hs[:, 0:A], ["hq", "hqa"])
+    mm(4, 128, T.u2q[:], T.u2s[:], T.hq[:, 128:256], T.hs[:, 128:256], ["u2q", "hq"])
+    rows("u2", 2, 1, A, T.hq[:, 0:A], T.hs[:, 0:A], ["hq"])
+    rows("u2", 3, 1, A, T.hq[:, 0:A], T.hs[:, 0:A], ["hq"])
+
+    tr(T.tn2[:, 0:128], T.ps0[:, 0:128], ["ps0"], ["tn02", "tna2"])
+    cut("v")
+    tr(T.tn2[:, 128:A], T.ps4[:, 0:96], ["ps4"], ["tnb2"])
     cut("v")
     passes(2)
     tail(2)
     act(T.fh[:, 0:8 * A:2], T.ft[:], ACT.Copy, ["ft"], ["fh"])
-    act(T.fh[:, 1:8 * A:2], T.ht[:], ACT.Copy, ["ht"], ["fh"])
+    act(T.fh[:, 1:8 * A:2], T.ht[:, 0:896], ACT.Copy, ["hta", "htb"], ["fh"])
     act(T.v1[:], T.win1[:, 0:A].indirect(T.operm[:]), ACT.Copy, ["operm", "win1"], ["v1"])
     cut("a")
     cp(T.win2[:].indirect(T.od2[:]), VAL2, ["od2", "VAL2"], ["win2"])
     scan(T.ex2[:], C2, T.win2[:, 0:B], 0.0, ALU.add, ALU.min, ["win2", "C2"], ["ex2"])
     ts(T.og[:], T.ex2[:].indirect(T.oread[:]), PT, None, ALU.add, None, ["ex2", "oread"], ["og"])
-    act(T.gt[:, 16 * GV:512], T.ht[:].indirect(T.og[:, GV:32]), ACT.Copy, ["og", "ht"], ["gt"])
+    act(T.gt[:, 16 * GV:512], T.ht[:, 0:896].indirect(T.og[:, GV:32]), ACT.Copy, ["og", "hta", "htb"], ["gt"])
     cut("a")
-    cp(T.gt[:, 0:16 * GV], T.ht[:].indirect(T.og[:, 0:GV]), ["og", "ht"], ["gt"])
+    cp(T.gt[:, 0:16 * GV], T.ht[:, 0:896].indirect(T.og[:, 0:GV]), ["og", "hta", "htb"], ["gt"])
     quant(T.gq[:, 112:240], T.gs[:, 112:240], T.gt[:], ["gt"], ["gq"])
     cut("v")
 
@@ -586,12 +609,16 @@ def rank_program(g, core, T, topo):
         mm(b, 128, T.eq[:, 128 * b:128 * b + 128], T.es[:, 128 * b:128 * b + 128], T.tq[:, 98:226], T.ts[:, 98:226],
            ["eq", "tq", "land2"])
     dma("y", [(T.ol[i:i + 1, :], T.olb[16 * i:16 * i + 1, :]) for i in range(8)], ["olb", "land2"], [])
-    for b in range(4):
-        tt(T.il[:, 2 * b + 1:8 * B:8], T.gcomp[:, b:4 * B:4], T["ps%d" % b][:, 16:128], ALU.add, ["gcomp", "ps%d" % b], ["il"])
-    scan(T.io2[:], T.keep[:], T.il[:], 0.0, ALU.mult, ALU.add, ["il", "keep"], ["io2"])
+    for h in range(2):
+        for b in range(4):
+            tt(T.il[:, 448 * h + 2 * b + 1:448 * h + 448:8], T.gcomp[:, A * h + b:A * h + A:4], T["ps%d" % b][:, 16 + 56 * h:72 + 56 * h],
+               ALU.add, ["gcomp", "ps%d" % b], ["il%d" % h])
+        cut("v")
+    for h in range(2):
+        scan(T.io2[:, 448 * h:448 * h + 448], T.keep[:, 0:448], T.il[:, 448 * h:448 * h + 448], 0.0, ALU.mult, ALU.add,
+             ["il", "il%d" % h, "keep"], ["io2"])
     cp(T.x2[:].indirect(T.ox[:]), T.io2[:, 1:8 * B:2], ["io2", "ox", "x2a", "x2b"], ["x2c"])
-    parts = ((0, O1), (O1, C))
-    for h, (a, b) in enumerate(parts):
+    for h, (a, b) in enumerate(((0, O1), (O1, C))):
         quant(T.oq[:, a:b], T.osb[:, a:b], T.x2[:, 4 * a:4 * b], ["x2c"], ["oq%d" % h])
         cut("v")
         mm(4 + h, b - a, T.vq[:], T.vs[:], T.oq[:, a:b], T.osb[:, a:b], ["vq", "oq%d" % h])

@@ -3,14 +3,22 @@ from concourse.mybir import dt, AluOpType, AxisListType, ActivationFunctionType
 
 C, A, B, S = 448, 224, 112, 14
 BIG = float(2 ** 90)
+DIM = 2.0 ** -60
 HOLD = float(2 ** 20)
-NS1, NS2 = 16, 9
-NV1, NV2 = 28 - NS1, 14 - NS2
 Q4, U8 = "float8_e4m3fn_x4", "uint8"
-GV = 16
+GV = 8
 XA = 320
-X1 = 28
-O1 = 256
+XS = (0, 20, 24, 28, 32, 34, 40, 56)
+O1 = 192
+FA, FB = 16, 50
+FIRST = (4, 2)
+P1 = ("a2 a0 a3 TB T1 R1 T2 S R2 T4 T3 v4 v5 v6 v7 s4 s5 a10 a9 a11 a8 a1 u10+2 s7 s6 q10+2 u8+2 u4+4 c4+4 q4+4 q8+2 "
+      "v18 v17 v16 s18 s17 D s16 c18 c16+2 a19 a13 a15 a14 a12")
+V1 = (4, 5, 6, 7, 16, 17, 18)
+P2 = "TB a0 a2 a4 a6 a8 a10 a12 a1 a3 v5 S v7 v9 v11 v13 s5 s7 s9 s11 s13 B c5+5/2 B"
+V2 = (5, 7, 9, 11, 13)
+PLAN = {1: (2, 4, 0, 4, P1.split(), V1), 2: (7, 0, 0, 0, P2.split(), V2)}
+NS1, NS2, NV1, NV2 = 13, 9, 7, 5
 
 
 def _sb(n, d):
@@ -29,30 +37,33 @@ SCRATCH = {
     "ft": _sb(4 * A, "bfloat16"), "fq": _sb(256, Q4), "fs": _sb(256, U8),
     "ht": _sb(1024, "bfloat16"), "hq": _sb(256, Q4), "hs": _sb(256, U8),
     "gt": _sb(512, "bfloat16"), "gq": _sb(240, Q4), "gs": _sb(240, U8),
-    "tt": _sb(512, "bfloat16"), "tq": _sb(240, Q4), "ts": _sb(240, U8),
+    "gf": _sb(512, "bfloat16"), "gfq": _sb(128, Q4), "gfs": _sb(128, U8),
+    "tt": _sb(512, "bfloat16"), "tq": _sb(176, Q4), "ts": _sb(176, U8),
+    "tf": _sb(512, "bfloat16"), "tfq": _sb(184, Q4), "tfs": _sb(184, U8),
     "gcomp": _sb(4 * B, "bfloat16"), "il": _sb(8 * B, "bfloat16"), "io2": _sb(8 * B, "bfloat16"),
     "keep": _sb(8 * B, "bfloat16"), "fh": _sb(8 * A, "bfloat16"), "a1": _sb(8 * A, "bfloat16"),
     "oq": _sb(C, Q4), "osb": _sb(C, U8), "yb": _sb(C, "float32"),
     "rq1": _sb(32, Q4), "rs1": _sb(128, U8), "rq2": _sb(28, Q4), "rs2": _sb(112, U8),
     "ki": _sb(32, "int32"), "kj": _sb(128, "int32"), "kf": _sb(1280, "float32"), "kc": _sb(896, "float32"),
-    "opick": _sb(16, "uint16"), "oread": _sb(2, "uint16"), "operm": _sb(16, "uint16"),
+    "opick": _sb(16, "uint16"), "oread": _sb(2, "uint16"),
     "od1": _sb(28, "uint16"), "od2": _sb(16, "uint16"),
-    "of": _sb(56, "uint16"), "og": _sb(32, "uint16"), "ox": _sb(28, "uint16"),
+    "of": _sb(56, "uint16"), "og": _sb(32, "uint16"), "oh": _sb(32, "uint16"), "ox": _sb(28, "uint16"),
     "tn1": _sb(C, "float32"), "tn2": _sb(A, "float32"),
     "junk1": _sb(NS1 * C, "bfloat16"), "junk2": _sb(NS2 * A, "bfloat16"),
     "fl1": _sb(NV1 * C, "bfloat16"), "fl2": _sb(NV2 * A, "bfloat16"),
     "so1": _sb(NV1 * C // 2, "bfloat16"), "so2": _sb(NV2 * A // 2, "bfloat16"),
     "wa": _sb(1024, "float32"), "w1": _sb(1024, "float32"), "w2": _sb(1024, "float32"),
-    "win1": _sb(4608, "float32"), "win2": _sb(2304, "float32"), "win3": _sb(2304, "float32"),
+    "dd": _sb(136, "float32"), "cm1": _sb(256, "float32"), "cm2": _sb(256, "float32"),
+    "win1": _sb(4608, "float32"), "win2": _sb(2304, "float32"), "both": _sb(512, "float32"),
     "val1": _sb(C, "float32"), "runs": ("dram", [8, 512], "float32"),
-    "ex1": _sb(A, "float32"), "ex2": _sb(B, "float32"), "v1": _sb(256, "float32"),
+    "ex1": _sb(A, "float32"), "ex2": _sb(B, "float32"),
     "olb": _sb(B, "float32"), "yx": _sb(256, "float32"),
 }
 for _i in range(8):
     SCRATCH["ps%d" % _i] = ("psum", [128, 512], "float32")
 
-NPOOL = 135
-SEMAPHORES = ["arr1", "arr2", "hin1", "hin2", "sent"] + ["s%d" % _i for _i in range(NPOOL)]
+NPOOL = 143
+SEMAPHORES = ["arr1", "arr2", "arn1", "arn2", "hin1", "hin2", "sent"] + ["s%d" % _i for _i in range(NPOOL)]
 
 ALU = AluOpType
 ACT = ActivationFunctionType
@@ -90,9 +101,8 @@ def _slot(dst, src, T, topo):
 
 
 def _arrivals(core, T, topo):
-    far, near, hs = _plan(core, T, topo)
-    n = 2 * HOP * len(far)
-    for s in near:
+    n = 0
+    for s in _plan(core, T, topo)[1]:
         i = _plan(s, T, topo)[1].index(core)
         n += DIRECT_CODES[i] + DIRECT_SCALES[i]
     return n
@@ -110,18 +120,18 @@ def helper_program(g, core, T, topo, home):
     pair = (2 * (j % 2), 2 * (j % 2) + 1)
     masks = _masks(topo.engines(core, far[0]), (HOP, HOP))
     for phase in (1, 2):
-        g.wait_ge(T.sem["hin%d" % phase], HOP)
+        g.wait_ge(T.sem["hin%d" % phase], FIRST[phase - 1])
         xs = []
         for n, i in enumerate(pair):
             d = far[i]
             at = (S if phase == 1 else 128) + S * _slot(d, home, T, topo)
             if j < 2:
                 src = T.rq1[:, 16 * n + 2:16 * n + 16] if phase == 1 else T.rq2[:, S * n:S * n + S]
-                dst = (T.gq if phase == 1 else T.tq)[:, at:at + S]
+                dst = (T.gq if phase == 1 else T.tfq)[:, at:at + S]
                 src, dst = _u8(src), _u8(dst)
             else:
-                src = T.rs1[:, 16 * i + 18:16 * i + 32] if phase == 1 else T.rs2[:, S * i + S:S * i + 2 * S]
-                dst = (T.gs if phase == 1 else T.ts)[:, at:at + S]
+                src = T.rs1[:, 16 * i + 2:16 * i + 16] if phase == 1 else T.rs2[:, S * i:S * i + S]
+                dst = (T.gs if phase == 1 else T.tfs)[:, at:at + S]
             xs.append(_xfer(topo, core, d, masks[n], T.sem["arr%d" % phase], src, dst))
         g.remote_dma_fused(xs, local_sem=T.sem.sent)
     g.wait_ge(T.sem.sent, 4 * HOP)
@@ -135,7 +145,7 @@ def rank_program(g, core, T, topo):
                 helper_program(g, core, T, topo, c)
         return
     far, near, hs = _plan(core, T, topo)
-    order = [T.rank_of(d) for d in [core] + far + near]
+    order = [T.rank_of(d) for d in far + [core] + near]
     V, SC, PE, SY = g.vector, g.scalar, g.tensor, g.sync
     eng = {"g": g, "v": V, "a": SC, "p": PE, "y": SY}
 
@@ -182,12 +192,10 @@ def rank_program(g, core, T, topo):
     def op(e, call, r, w):
         deps(e, r, w)
         if stage[e] is None:
-            old = latest.get(e)
-            if old is not None and old["k"] in known[e]:
-                stage[e] = new_stage(old["sem"], old["n"])
-            else:
-                stage[e] = new_stage()
-            latest[e] = stage[e]
+            mine = latest.setdefault(e, {})
+            done = [old for old in mine.values() if old["k"] in known[e]]
+            stage[e] = new_stage(done[-1]["sem"], done[-1]["n"]) if done else new_stage()
+            mine[stage[e]["sem"]] = stage[e]
         st = stage[e]
         call().then_inc(T.sem[st["sem"]], 1)
         st["n"] += 1
@@ -240,11 +248,11 @@ def rank_program(g, core, T, topo):
         readers[name] = []
         cut("p")
 
-    def iota(out, pattern, base, cm, w, whole=False):
+    def iota(out, pattern, base, cm, w, r=(), whole=False):
         if whole:
-            op("g", lambda: g.iota(out, pattern, base, cm), [], w)
+            op("g", lambda: g.iota(out, pattern, base, cm), r, w)
         else:
-            op("g", lambda: g.iota(out, pattern, base, cm, allow_small_or_imprecise_dtypes=True), [], w)
+            op("g", lambda: g.iota(out, pattern, base, cm, allow_small_or_imprecise_dtypes=True), r, w)
 
     def choose(out, in_, pattern, o, fill, base, cm, r, w):
         op("g", lambda: g.affine_select(out, in_, pattern, o, fill, base, cm), r, w)
@@ -255,50 +263,49 @@ def rank_program(g, core, T, topo):
     dma("y", [(T.u2b[:], T.u2[:])], ["xb0", "xb1"], ["u2b"])
     dma("y", [(_u8(T.wq[:]), T.wc[:]), (T.wp[:], T.ws[:])], [], ["w"])
 
-    kf, kc, ki, kj, wa = T.kf, T.kc, T.ki, T.kj, T.wa
-    KR, R4 = kf[:, 64:128], kf[:, 128:352]
-    VAL1, VAL2, J16 = T.val1[:], kf[:, 864:1120], kf[:, 1120:1136]
+    kf, kc, ki, kj, wa, dd = T.kf, T.kc, T.ki, T.kj, T.wa, T.dd
+    KR, R4 = kf[:, 1152:1248], kf[:, 128:352]
+    VAL1, VAL2 = T.val1[:], kf[:, 864:1120]
 
     def rounds(L):
         W = 28 if L == 1 else 16
-        return W, 128, 128 + 4 * (W + 1), 128 + 4 * (2 * W + 1), 128 + 4 * (3 * W + 2), 128 + 4 * (4 * W + 2)
+        return W, 128, 128 + 4 * W, 128 + 8 * W
 
     def round_constants(L):
-        wb, k = T["w%d" % L], (A if L == 1 else B)
-        W, pre, d1, post, d0, out = rounds(L)
+        wb, cm, k = T["w%d" % L], T["cm%d" % L], (A if L == 1 else B)
+        W, d1, d0, out = rounds(L)
         a, b = "Ra%d" % L, "Rb%d" % L
-        iota(wb[:, pre:pre + 4 * W], [[0, 4 * W]], 1, 0, [a])
-        iota(wb[:, pre + 4 * W:pre + 4 * W + 1], [[0, 1]], -(k + W), -W, [a])
-        iota(wb[:, pre + 4 * W + 2:pre + 4 * W + 3], [[0, 1]], k, W, [a])
-        iota(wb[:, post:post + 4 * (W + 1)], [[0, 4 * (W + 1)]], 0, 0, [a])
-        iota(wb[:, d0:d0 + 4 * W], [[-1, W], [0, 4]], -(k + 1), -W, [b + "0"])
-        choose(wb[:, d0:d0 + 4 * W], wb[:, d0:d0 + 4 * W], [[0, W], [-1, 4]], ALU.is_ge, 1.0, 2, 0, [b + "0"], [b + "1"])
-        choose(wb[:, d0:d0 + 4 * W], wb[:, d0:d0 + 4 * W], [[0, W], [1, 4]], ALU.is_ge, 0.0, -2, 0, [b + "1"], [b])
+        iota(cm[:, 0:128], [[0, 128]], 0, 0, [a + "0"])
+        iota(wb[:, d0:out], [[-1, W], [0, 4]], -(k + 1), -W, [b + "0"])
+        iota(cm[:, 0:1], [[0, 1]], k, W, [a], [a + "0"])
+        iota(cm[:, 31:32], [[0, 1]], -(k + W), -W, [a], [a + "0"])
+        choose(wb[:, d0:out], wb[:, d0:out], [[0, W], [-1, 4]], ALU.is_ge, 1.0, 2, 0, [b + "0"], [b + "1"])
+        choose(wb[:, d0:out], wb[:, d0:out], [[0, W], [1, 4]], ALU.is_ge, 0.0, -2, 0, [b + "1"], [b])
         cut("g")
 
-    iota(ki[:, 0:16], [[16, 2], [32, 4], [0, 2]], 0, 0, ["ipick"], True)
+    iota(ki[:, 0:16], [[16, 2], [32, 4], [0, 2]], 0, 0, ["ipick"], whole=True)
     cut("g")
-    tri, upn = (kc[0:32, 32 * i:32 * i + 32] for i in (2, 3))
-    iota(tri, [[0, 32]], 1, 0, ["M0"])
-    iota(upn, [[0, 32]], -1, 0, ["M0"])
-    iota(KR, [[0, 64]], 1, 0, ["M0"])
-    choose(tri, tri, [[-16, 2], [0, 16]], ALU.is_ge, 0.0, 0, 1, ["M0"], ["M1"])
-    choose(upn, upn, [[16, 2], [0, 16]], ALU.is_ge, 0.0, 15, -1, ["M0"], ["M1"])
-    choose(KR, KR, [[1, 64]], ALU.not_equal, 0.0, -32, 0, ["M0"], ["KR"])
-    choose(tri, tri, [[1, 32]], ALU.is_gt, 0.0, 0, -1, ["M1"], ["M2"])
-    choose(upn, upn, [[-1, 32]], ALU.is_gt, 0.0, 0, 1, ["M1"], ["M2"])
+    iota(dd[0:32, :], [[0, 136]], 1, 0, ["M0"])
+    iota(KR, [[0, 96]], 1, 0, ["M0"])
+    choose(dd[0:32, 32:64], dd[0:32, 32:64], [[1, 32]], ALU.not_equal, DIM, 0, -1, ["M0"], ["M1"])
+    choose(dd[0:32, 96:128], dd[0:32, 96:128], [[1, 32]], ALU.not_equal, 1 / DIM, -1, -1, ["M0"], ["M1"])
+    choose(KR, KR, [[1, 96]], ALU.not_equal, 0.0, -64, 0, ["M0"], ["KR"])
+    choose(dd[0:32, 32:33], dd[0:32, 32:33], [[0, 1]], ALU.is_ge, DIM, 15, -1, ["M1"], ["M2"])
+    choose(dd[0:32, 48:49], dd[0:32, 130:131], [[0, 1]], ALU.is_ge, 1 / DIM, 16, -1, ["M1"], ["M2"])
+    choose(dd[0:32, 64:65], dd[0:32, 64:65], [[0, 1]], ALU.is_gt, 1 / DIM, 0, 0, ["M1"], ["M2"])
+    choose(dd[0:32, 96:97], dd[0:32, 96:97], [[0, 1]], ALU.is_gt, DIM, 0, 0, ["M1"], ["M2"])
+    choose(dd[0:32, 112:113], dd[0:32, 131:132], [[0, 1]], ALU.is_ge, DIM, -15, 1, ["M1"], ["M2"])
     cut("g")
-    dma("y", [(kc[32 * a:32 * a + 32, 64:128], kc[0:32, 64:128]) for a in (1, 2, 3)], ["M2"], ["MASK"])
+    dma("y", [(dd[32 * a:32 * a + 32, 0:128], dd[0:32, 0:128]) for a in (1, 2, 3)], ["M2"], ["MASK"])
     round_constants(1)
     iota(kf[:, 0:32], [[-4, 32]], 0, 1, ["N0"])
     iota(kf[:, 32:64], [[0, 8], [-1, 4]], 0, 0, ["N0"])
-    iota(kf[:, 1136:1144], [[-256, 8]], 0, 16, ["N0"])
     iota(kf[:, 1144:1152], [[0, 4], [1, 2]], 0, 0, ["N0"])
     iota(R4, [[0, 56], [1, 4]], 0, 0, ["R4"])
     choose(kf[:, 0:64], kf[:, 0:64], [[0, 2], [-4, 32]], ALU.is_ge, 0.0, 0, 1, ["N0"], ["N1"])
-    choose(kf[:, 1136:1152], kf[:, 1136:1152], [[0, 2], [-16, 8]], ALU.is_ge, 0.0, 0, 1, ["N0"], ["N1"])
+    choose(kf[:, 1144:1152], kf[:, 1144:1152], [[-16, 8]], ALU.is_ge, 0.0, 0, 1, ["N0"], ["N1"])
     choose(kf[:, 0:64], kf[:, 0:64], [[0, 2], [4, 32]], ALU.is_ge, 0.0, 3, -1, ["N1"], ["N2"])
-    choose(kf[:, 1136:1152], kf[:, 1136:1152], [[0, 2], [16, 8]], ALU.is_ge, 0.0, 15, -1, ["N1"], ["N2"])
+    choose(kf[:, 1144:1152], kf[:, 1144:1152], [[16, 8]], ALU.is_ge, 0.0, 15, -1, ["N1"], ["N2"])
     cut("g")
     iota(VAL1, [[4, 28], [112, 16]], 0, 0, ["VAL1"])
     cut("g")
@@ -306,28 +313,32 @@ def rank_program(g, core, T, topo):
         iota(kf[:, 608 + 32 * p:640 + 32 * p], [[4, 4], [0, 8]], S * order[p] + 1, 0, ["RR0"])
     choose(kf[:, 608:864], kf[:, 608:864], [[0, 2], [1, 16], [16, 8]], ALU.is_equal, 0.0, 0, -1, ["RR0"], ["RR"])
     cut("g")
-    iota(J16, [[1, 16]], 0, 0, ["J16"])
-    iota(VAL2, [[4, 16], [64, 16]], 0, 0, ["VAL2"])
-    round_constants(2)
     iota(T.keep[:], [[0, 4 * B], [1, 2]], 0, 0, ["keep"])
+    cut("g")
     for b in range(4):
         o = (b + 1) % 2
         choose(T.eb[:, 512 * b:512 * b + 512], T.keep[:, o:o + 512], [[-1, 512]], ALU.is_equal, 0.0, b, 4, ["keep"], ["eb"])
     cut("g")
+    round_constants(2)
+    iota(VAL2, [[4, 16], [64, 16]], 0, 0, ["VAL2"])
+    cut("g")
 
-    XX, MB, T2, O2, ZJ, ZB, ZT, MC, TC, O3, COL = 32, 192, 320, 448, 512, 544, 576, 608, 672, 736, 800
+    XX, MB, T2, O2, ZJ, ZB, ZT, TC, O3, COL = 32, 192, 320, 448, 512, 544, 576, 608, 704, 800
+    UW, SPW, SD, LO = 704, 752, 800, 816
+    ms(T.w1[:, SD:SD + 16], BIG, ["SD1"])
     for wb, n in ((T.w1, "1"), (T.w2, "2")):
-        ms(wb[:, 0:32], -1.0, ["Vp" + n])
         ms(wb[:, 64:128], -BIG, ["Spp" + n])
-    for at, c in ((0, BIG), (48, BIG), (64, -BIG), (112, -BIG)):
-        ms(wa[:, XX + at:XX + at + 16], c, ["KK"])
+    for at, c in ((20, BIG), (84, -BIG)):
+        ms(wa[:, XX + at:XX + at + 32], c, ["KK"])
     ms(wa[:, T2:T2 + 32], -BIG, ["KK"])
     ms(wa[:, T2 + 96:T2 + 128], BIG, ["KK"])
-    ms(T.tt[:, 0:4 * S], 0.0, ["tt"])
-    ms(T.ht[:, 896:1024], 0.0, ["tt"])
+    ms(T.tt[:, 0:280], 0.0, ["tt"])
+    ms(T.tf[:, 224:512], 0.0, ["tf"])
+    ms(T.ht[:, 896:1024], 0.0, ["h0"])
+    ms(T.gf[:, 256:512], 0.0, ["gf"])
+    ms(T.gt[:, 256:512], 0.0, ["gt"])
     cp(T.opick[:], ki[:, 0:16], ["ipick"], ["opick"])
-    PT, NPQ, PM16, PH, N0 = (kc[:, i:i + 1] for i in range(5))
-    TRI, UPN = (kc[:, 32 * i:32 * i + 32] for i in (2, 3))
+    PT, NPQ, PH, N0 = (kc[:, i:i + 1] for i in range(4))
     C1, C1A = kc[:, 256:480], kc[:, 480:704]
     C2 = kc[:, 704:816]
 
@@ -347,14 +358,25 @@ def rank_program(g, core, T, topo):
         ts(T.w2[:, 96 + 16 * h + half:110 + 16 * h:2], T.tn2[:, 16 * h:A:32], PH if half else N0, None, ALU.mult, None,
            ["tna2", "tnb2", "Spp2", "C1"], ["Sd2"])
 
+    def unit(b):
+        quant(T.eq[:, 128 * b:128 * b + 128], T.es[:, 128 * b:128 * b + 128], T.eb[:, 512 * b:512 * b + 512], ["eb"], ["eq"])
+
+    def f_and_h(i):
+        scan(T.a1[:, 448 * i:448 * i + 448], T.keep[:, 0:448], T.fh[:, 448 * i:448 * i + 448], 0.0, ALU.mult, ALU.add,
+             ["fh", "keep"], ["a1"])
+
     spare = {
-        1: [None, None, lambda: quant(T.u2q[:], T.u2s[:], T.u2b[:], ["u2b"], ["u2q"]), None, None,
-            lambda: pick_codes("u2", 0, 1), lambda: pick_codes("u2", 1, 2)],
+        1: [lambda: quant(T.u2q[:], T.u2s[:], T.u2b[:], ["u2b"], ["u2q"]), None,
+            lambda: quant(T.vq[:], T.vs[:], T.vb[:], ["vb"], ["vq"]), lambda: pick_codes("u2", 0, 1), None,
+            lambda: pick_codes("u2", 1, 2), None, None, None],
         2: [lambda: [halves(0, 0), halves(0, 1)], lambda: [halves(1, 0), halves(1, 1)],
             lambda: tr(T.w2[:, 960:992], T.w2[:, 96:128], ["Sd2"], ["St2"]),
             lambda: tt(T.w2[:, 992:1008], T.w2[:, 960:976], T.w2[:, 976:992], ALU.add, ["St2"], ["Sc2"]),
-            None, None, None],
+            lambda: unit(0), lambda: unit(1), lambda: unit(2), lambda: unit(3),
+            lambda: f_and_h(0), lambda: f_and_h(1), lambda: f_and_h(2)],
     }
+    late = {1: lambda: tr(T.tn1[:, XA:C], T.ps4[:, 0:C - XA], ["ps4"], ["tnb1"]),
+            2: lambda: tr(T.tn2[:, 128:A], T.ps4[:, 0:96], ["ps4"], ["tnb2"])}
 
     def between(L):
         cut("v")
@@ -364,91 +386,149 @@ def rank_program(g, core, T, topo):
             cut("v")
 
     def passes(L):
-        n, k, ns, nv = (C, A, NS1, NV1) if L == 1 else (A, B, NS2, NV2)
+        n, k = (C, A) if L == 1 else (A, B)
+        ns, nt, eS, eA, plan, vl = PLAN[L]
         wb, tn, junk, fl, so = (T[s + str(L)] for s in ("w", "tn", "junk", "fl", "so"))
         nb, first = n // 32, (XA if L == 1 else 128)
+        cm, cq, cd = 2 * ns, 2 * ns + 2 * nt, 2 * ns + 4 * nt
         X = lambda s: s + str(L)
-        for i in range(ns):
-            h, b = (0, i) if i < nb else (1, i - nb)
-            c = 32 * b + 16 * h
-            act(junk[:, n * i:n * i + n], T["ps1" if h == 0 else "ps3"][:, 0:n], ACT.Sign,
-                ["ps1" if h == 0 else "ps3", X("tn0") if c < 64 else X("tna") if c < first else X("tnb"), X("Vp")], [X("V")],
-                bias=tn[:, c:c + 1], scale=-1.0, accum_out=wb[:, 16 * h + b:16 * h + b + 1])
-        cut("a")
-        b0 = ns - nb
-        for i in range(nv):
-            c = 32 * (b0 + i) + 16
-            ts(fl[:, n * i:n * i + n], T.ps2[:, 0:n], tn[:, c:c + 1], 0.5, ALU.is_lt, ALU.subtract,
-               ["ps2", X("tn0"), X("tna"), X("tnb")], [X("fl%d" % (i // (nv - 1)))])
-            if i == 0:
+        tns = [X("tn0"), X("tna"), X("tnb")]
+        part = lambda e: X("tn0") if 16 * e < 64 else X("tna") if 16 * e < first else X("tnb")
+        parts = lambda e, m: sorted({part(i) for i in range(e, e + m)})
+        col = lambda e, m: tn[:, 16 * e:16 * (e + m):16]
+        al = [int(s[1:]) for s in plan if s[0] == "a"]
+        ends = lambda c, m: so[:, k * vl.index(c) + k - 1:k * (vl.index(c) + m):k]
+        if nt:
+            lo, hi, mid = (wb[:, LO + 8 * i:LO + 8 * i + 2 * nt] for i in range(3))
+            third, there = col(eA + 4 * nt, 2 * nt), parts(eA + 4 * nt, 2 * nt)
+
+        def pivot(c):
+            if c < cm:
+                return col(eS + c, 1), part(eS + c)
+            return wb[:, SPW + 2 * c + 1:SPW + 2 * c + 2], X("med") if c < cq else X("q%d_" % c)
+
+        for s in plan:
+            kind, c, m, step = s[0], 0, 1, 1
+            if kind in "avscuq":
+                z = [int(i) for i in s[1:].replace("/", "+").split("+")]
+                c, m, step = z + [1, 1][len(z) - 1:]
+            some = range(c, c + m * step, step)
+            if kind == "a":
+                p, name = pivot(c)
+                i, bank = al.index(c), ("ps1", "ps3")[c % 2]
+                act(junk[:, n * i:n * i + n], T[bank][:, 0:n], ACT.Sign, [bank, name], [X("V%d_" % c), X("V")],
+                    bias=p, scale=-1.0, accum_out=wb[:, c:c + 1])
+                if nt:
+                    cut("a")
+                continue
+            if kind == "v":
+                p, name = pivot(c)
+                i, bank = vl.index(c), ("ps5", "ps2")[c % 2]
+                ts(fl[:, n * i:n * i + n], T[bank][:, 0:n], p, 0.5, ALU.is_lt, ALU.subtract, [bank, name], [X("fl%d_" % c)])
+            elif kind == "s":
+                i = vl.index(c)
+                scan(so[:, k * i:k * i + k], fl[:, n * i:n * i + k], fl[:, n * i + k:n * i + n], 0.0, ALU.add, ALU.add,
+                     [X("fl%d_" % c)], [X("so%d_" % c)])
+            elif kind == "c":
+                cp(wb[:, c:c + m * step:step], ends(c, m), [X("so%d_" % i) for i in some], [X("V%d_" % i) for i in some] + [X("V")])
+            elif kind == "u":
+                src, name = (ends(c, m), "so%d_") if c in vl else (wb[:, c:c + m], "V%d_")
+                ts(wb[:, UW + 2 * c:UW + 2 * (c + m):2], src, 0.25, -BIG, ALU.add, ALU.mult, [X(name % i) for i in some], [X("u%d_" % c)])
+            elif kind == "q":
+                j = c - cm
+                scan(wb[:, SPW + 2 * (cq + j):SPW + 2 * (cq + j + m)], wb[:, SD + 2 * j:SD + 2 * (j + m)], wb[:, UW + 2 * c:UW + 2 * (c + m)],
+                     0.0, ALU.max, ALU.min, [X("u%d_" % c), X("ends")], [X("q%d_" % (cq + j + i)) for i in range(m)] + [X("Sp")])
+            elif s == "T1":
+                tt(lo, col(eA, 2 * nt), col(eA + 2 * nt, 2 * nt), ALU.min, parts(eA, 4 * nt), [X("lo")])
+                tt(hi, col(eA, 2 * nt), col(eA + 2 * nt, 2 * nt), ALU.max, parts(eA, 4 * nt), [X("lo")])
+            elif s == "T2":
+                tt(mid, hi, third, ALU.min, [X("lo")] + there, [X("mid")])
+            elif s == "T3":
+                tt(wb[:, SD + 1:SD + 4 * nt:2], lo, third, ALU.min, [X("lo"), X("SD")] + there, [X("ends")])
+                tt(wb[:, UW + 2 * cm + 1:UW + 2 * cq:2], hi, third, ALU.max, [X("lo")] + there, [X("ends")])
+            elif s == "T4":
+                tt(wb[:, SPW + 2 * cm + 1:SPW + 2 * cq:2], lo, mid, ALU.max, [X("lo"), X("mid")], [X("med"), X("Sp")])
+            elif s == "TB":
+                late[L]()
+            elif s == "S":
+                cp(wb[:, SPW + 1:SPW + 2 * cm:2], col(eS, cm), parts(eS, cm), [X("Sp")])
+            elif s == "D":
+                cp(wb[:, cd:cd + 2 * nt], wb[:, cm:cq], [X("V%d_" % i) for i in range(cm, cq)], [X("V")])
+            elif s == "R1":
                 for h in range(2):
-                    cp(wb[:, 64 + 16 * h:64 + 16 * h + nb], tn[:, 16 * h:n:32], [X("tna"), X("tnb"), X("Spp")], [X("Sp")])
-                cut("v")
-            if i == 1 and L == 1:
-                tr(wb[:, 96:128], wb[:, 64:96], ["Sp1", "Spp1"], ["St1"])
+                    cp(wb[:, 64 + 16 * h:64 + 16 * h + nb], tn[:, 16 * h:n:32], tns + ["Spp1"], ["So1"])
+            elif s == "R2":
+                tr(wb[:, 96:128], wb[:, 64:96], ["So1", "Spp1"], ["St1"])
                 cut("v")
                 dma("y", [(T.runs[:], wb[:, 96:128])], ["St1"], ["runs"])
                 dma("y", [(wb[:, 960:988], T.runs[:, 0:C])], ["runs"], ["Sc1"])
+                dma("y", [(T.vb[:], T.v[:])], [], ["vb"])
                 dma("y", [(_u8(T.zq[:]), T.zc[:]), (T.zp[:], T.zs[:])], [], ["z"])
-                dma("y", [(T.vb[:], T.v[:]), (T.x2[:], T.x[:])], [], ["vb", "x2"])
-            if i >= nv - 2:
-                cut("v")
-        for i in range(nv):
-            scan(so[:, k * i:k * i + k], fl[:, n * i:n * i + k], fl[:, n * i + k:n * i + n], 0.0, ALU.add, ALU.add,
-                 [X("fl%d" % (i // (nv - 1)))], [X("so")])
-        between(L)
-        cp(wb[:, 16 + b0:16 + nb], so[:, k - 1:k * nv:k], [X("so"), X("Vp")], [X("Vv")])
-        between(L)
+                dma("y", [(T.x2[:], T.x[:])], [], ["x2"])
+            else:
+                between(L)
+            cut("v")
+        cut("a")
 
     def tail(L):
-        k, wb = (A if L == 1 else B), T["w%d" % L]
-        W, pre, d1, post, d0, out = rounds(L)
+        k, wb, cm = (A if L == 1 else B), T["w%d" % L], T["cm%d" % L]
+        W, d1, d0, out = rounds(L)
+        ns, nt = PLAN[L][:2]
+        R, nb = 2 * ns + 4 * nt, ns + 3 * nt
         X = lambda s: s + str(L)
         a = lambda at, n: wa[:, at:at + n]
-        back = lambda at: wa[:, at + 31:at - 1:-1]
-        Vt, U, Sp = wb[:, 0:32], wb[:, 32:64], wb[:, 64:96]
+        U, Sp = wb[:, UW:UW + 2 * R:2], wb[:, SPW + 1:SPW + 2 * R:2]
         Sc = wb[:, 960:988] if L == 1 else wb[:, 992:1008]
         for h in range(2):
-            act(a(ZJ + 16 * h, 16), wb[:, 16 * h:16 * h + 16], ACT.Sign, [X("V"), X("Vv")], ["zc"], bias=0.25,
-                accum_out=a(COL + h, 1))
+            act(a(ZJ + 16 * h, nb), wb[:, h:2 * nb:2], ACT.Sign, [X("V")], ["zc"], bias=0.25, accum_out=a(COL + h, 1))
         for h in range(2):
-            act(a(ZB + 16 * h, 16), a(T2 + 96, 16), ACT.Identity, ["zc", "KK"], ["zb"], scale=a(COL + h, 1),
-                bias=(513 - 2 * k) * BIG / 32)
+            act(a(ZB + 16 * h, 16), a(T2 + 96, 16), ACT.Identity, ["zc", "KK"], ["zb"], scale=a(COL + h, 1), bias=BIG / 32)
         cut("a")
-        ts(U, Vt, 0.25, -BIG, ALU.add, ALU.mult, [X("V"), X("Vv")], [X("U")])
+        ts(U, wb[:, 0:R], 0.25, -BIG, ALU.add, ALU.mult, [X("V")], [X("U")])
         between(L)
-        tt(a(XX + 16, 32), Sp, U, ALU.max, [X("U"), X("Sp")], ["xx"])
-        tt(a(XX + 80, 32), Sp, U, ALU.min, [X("U"), X("Sp")], ["xx"])
+        tt(a(XX + 20 - R, R), Sp, U, ALU.max, [X("U"), X("Sp")], ["xx"])
+        tt(a(XX + 84 - R, R), Sp, U, ALU.min, [X("U"), X("Sp")], ["xx"])
         between(L)
-        for x, m, c, o0, o1, idle in ((XX, MB + 64, BIG, ALU.min, ALU.max, T2), (XX + 64, MB, -BIG, ALU.max, ALU.min, T2 + 96)):
-            scan(a(m, 32), back(x), a(idle, 32), c, o0, o1, ["xx", "KK"], ["mb"])
-            scan(back(m + 32), a(x + 32, 32), a(idle, 32), c, o0, o1, ["xx", "KK"], ["mb"])
+        w = R // 2 + 16
+        for x, m, c, o0, o1, idle in ((XX + 20 - R, MB + 96, BIG, ALU.min, ALU.max, T2), (XX + 84 - R, MB + 32, -BIG, ALU.max, ALU.min, T2 + 96)):
+            scan(a(m - w, w), wa[:, x:x + 2 * w:2], a(idle, w), c, o0, o1, ["xx", "KK"], ["mb"])
+            scan(wa[:, m + w - 1:m - 1:-1], wa[:, x + 1:x + 2 * w:2], a(idle, w), c, o0, o1, ["xx", "KK"], ["mb"])
         cut("v")
         tr(a(ZT, 32), a(ZB, 32), ["zb"], ["zt"])
         cut("v")
         act(a(ZJ, 32), a(ZT, 32), ACT.Identity, ["zt"], ["zz"], accum_out=a(COL + 2, 1))
         cut("a")
+        if L == 2:
+            act(T.fh[:, 1:8 * A:2], T.ht[:, 0:896], ACT.Copy, ["hta", "htb"], ["fh"])
+            cut("a")
         tr(a(T2 + 32, 32), a(MB + 16, 32), ["mb"], ["t2"])
         tr(a(T2 + 64, 32), a(MB + 80, 32), ["mb"], ["t2"])
         between(L)
         scan(a(O2, 64), a(T2 + 64, 64), a(T2, 64), a(COL + 2, 1), ALU.min, ALU.max, ["t2", "zz"], ["o2"])
         t = a(O2 + 63, 1)
-        ts(wb[:, d1 + 1:post:4], Sc, t, None, ALU.is_gt, None, ["o2", X("Sc")], [X("fg")])
-        ts(wb[:, d1:post:4], Sc, t, None, ALU.is_equal, None, ["o2", X("Sc")], [X("fg")])
-        scan(wb[:, d1 + 2:d0:4], wb[:, d1 + 1:d0:4], wb[:, pre:post:4], wb[:, pre + 4 * W + 2:pre + 4 * W + 3], ALU.add, ALU.add,
-             [X("fg"), X("Ra")], [X("cum")])
-        own, ceq, tot = wb[:, post + 2:post + 3], wb[:, post + 6:d0:4], wb[:, d0 - 2:d0 - 1]
-        ts(a(MC, 32), TRI, tot, -1.0 / 32, ALU.mult, ALU.add, [X("cum"), "MASK"], ["mc"])
-        ts(a(MC + 32, 32), UPN, own, (k - 1) / 32, ALU.mult, ALU.add, [X("cum")], ["mc"])
-        tr(a(TC, 64), a(MC, 64), ["mc"], ["tc"])
+        ts(cm[:, 31 - W:31], Sc, t, 1.0, ALU.is_gt, ALU.add, ["o2", X("Sc"), X("Ra")], [X("fg")])
+        ts(cm[:, 64:64 + W], Sc, t, None, ALU.is_equal, None, ["o2", X("Sc")], [X("fg")])
+        cut("v")
+        ts(wb[:, d1 + 1:d0:4], Sc, t, None, ALU.is_gt, None, ["o2", X("Sc")], [X("slots")])
+        ts(wb[:, d1:d0:4], Sc, t, None, ALU.is_equal, None, ["o2", X("Sc")], [X("slots")])
+        cut("v")
+        scan(cm[:, 159 - W:256], dd[:, 31 - W:128], cm[:, 31 - W:128], cm[:, 0:1], ALU.mult, ALU.add, [X("fg"), "MASK"], [X("cum")])
         between(L)
-        scan(a(O3, 64), KR, a(TC, 64), 0.0, ALU.mult, ALU.add, ["tc", "KR"], ["o3"])
+        own, ceq = cm[:, 159:160], cm[:, 192:192 + W]
+        tr(a(TC, 96), cm[:, 160:256], [X("cum")], ["tc"])
+        cut("v")
+        cp(wb[:, d1 + 2:d0:4], cm[:, 159 - W:159], [X("cum")], [X("slots")])
         between(L)
-        p1, p2 = a(O3 + 31, 1), a(O3 + 63, 1)
-        ts(wb[:, d1 + 3:post:4], ceq, p1, p2, ALU.add, ALU.min, ["o3"], [X("ws")])
-        ts(wb[:, d0 + 1:out:4], ceq, p1, p2, ALU.add, ALU.is_le, ["o3", X("Rb")], [X("ws")])
-        scan(wb[:, out:out + 4 * W], wb[:, d0:out], wb[:, d1:post], 0.0, ALU.mult, ALU.add, [X("ws")], [X("dest")])
-        ts(T["od%d" % L][:], wb[:, out + 3:out + 4 * W:4], own, None, ALU.subtract, None, [X("dest")], [X("od")])
+        scan(a(O3, 96), KR, a(TC, 96), k + 0.25, ALU.mult, ALU.subtract, ["tc", "KR"], ["o3"])
+        between(L)
+        p1, p2 = a(O3 + 95, 1), a(O3 + 31, 1)
+        ts(wb[:, d1 + 3:d0:4], ceq, p1, p2, ALU.subtract, ALU.min, ["o3"], [X("ws")])
+        ts(wb[:, d0 + 1:out:4], ceq, p1, p2, ALU.subtract, ALU.is_le, ["o3", X("Rb")], [X("ws")])
+        between(L)
+        scan(wb[:, out:out + 4 * W], wb[:, d0:out], wb[:, d1:d0], 0.0, ALU.mult, ALU.add, [X("ws"), X("slots")], [X("dest")])
+        between(L)
+        ts(T["od%d" % L][:], wb[:, out + 3:out + 4 * W:4], own, 1.0, ALU.subtract, ALU.subtract, [X("dest")], [X("od")])
+        between(L)
 
     def relu4(out, n, skip, bank0, w, at=0, scalar=(0, 2)):
         for b in range(4):
@@ -469,17 +549,16 @@ def rank_program(g, core, T, topo):
     cut("v")
     rows("u1", 1, 0, C, T.xq[:], T.xs[:], ["xq0", "xq1"])
     mm(4, C - XA, T.u1q[:], T.u1s[:], T.xq[:, XA:C], T.xs[:, XA:C], ["u1q", "xq1"])
-    rows("u1", 2, 1, C, T.xq[:], T.xs[:], ["xq0", "xq1"])
     rows("u1", 3, 1, C, T.xq[:], T.xs[:], ["xq0", "xq1"])
+    rows("u1", 5, 0, C, T.xq[:], T.xs[:], ["xq0", "xq1"])
+    rows("u1", 2, 1, C, T.xq[:], T.xs[:], ["xq0", "xq1"])
     tr(T.tn1[:, 0:64], T.ps0[:, 0:64], ["ps0"], ["tn01"])
     cut("v")
     tr(T.tn1[:, 64:XA], T.ps0[:, 64:XA], ["ps0"], ["tna1"])
     cut("v")
-    tr(T.tn1[:, XA:C], T.ps4[:, 0:C - XA], ["ps4"], ["tnb1"])
-    cut("v")
     passes(1)
     tail(1)
-    for i, (a, b) in enumerate(((0, 32), (32, 64), (1136, 1144), (1144, 1152))):
+    for i, (a, b) in enumerate(((0, 32), (32, 64), (1144, 1152))):
         act(kc[:, 128 + 32 * i:128 + 32 * i + b - a], kf[:, a:b], ACT.Identity, ["N2"], ["F4"], accum_out=kc[:, i:i + 1])
     act(C1A, R4, ACT.Abs, ["R4", "F4"], ["C1a"], bias=NPQ)
     act(N0, PH, ACT.Identity, ["F4"], ["C1a"], scale=-1.0, bias=1.0)
@@ -499,16 +578,20 @@ def rank_program(g, core, T, topo):
     for n, a, b in (("a", 0, 128), ("b", 128, A)):
         ts(T.of[:, a // 4:b // 4], T.ex1[:, a + 3:b:4], PT, None, ALU.add, None, ["ex1" + n, "F4"], ["of" + n, "of"])
         cut("v")
-    act(T.ft[:, 512:896], T.xb[:].indirect(T.of[:, 32:56]), ACT.Copy, ["ofb", "xb0", "xb1"], ["ft"])
+    xr = ["xb0", "xb1"]
+    act(T.ft[:, 16 * FA:512], T.xb[:].indirect(T.of[:, FA:32]), ACT.Copy, ["ofa"] + xr, ["fta", "ft"])
     cut("a")
-    cp(T.ft[:, 0:512], T.xb[:].indirect(T.of[:, 0:32]), ["ofa", "xb0", "xb1"], ["fta", "ft"])
-    cut("v")
-    cp(T.oread[:], kc[:, 12:14], ["C2"], ["oread"])
-    ts(T.operm[:], J16, PM16, float(A - 1), ALU.add, ALU.min, ["F4", "J16"], ["operm"])
+    act(T.ft[:, 512:16 * FB], T.xb[:].indirect(T.of[:, 32:FB]), ACT.Copy, ["ofb"] + xr, ["ft"])
+    cut("a")
+    cp(T.ft[:, 0:16 * FA], T.xb[:].indirect(T.of[:, 0:FA]), ["ofa"] + xr, ["fta", "ft"])
     cut("v")
     quant(T.fq[:, 0:128], T.fs[:, 0:128], T.ft[:, 0:512], ["fta"], ["fq0"])
     cut("v")
-    quant(T.fq[:, 128:256], T.fs[:, 128:256], T.ft[:, 384:896], ["ft"], ["fq1"])
+    cp(T.ft[:, 16 * FB:896], T.xb[:].indirect(T.of[:, FB:56]), ["ofb"] + xr, ["ftb"])
+    cut("v")
+    quant(T.fq[:, 128:256], T.fs[:, 128:256], T.ft[:, 384:896], ["ft", "ftb"], ["fq1"])
+    cut("v")
+    cp(T.oread[:], kc[:, 12:14], ["C2"], ["oread"])
     cut("v")
     for h in range(2):
         for b in range(4):
@@ -521,7 +604,7 @@ def rank_program(g, core, T, topo):
     quant(T.hq[:, 0:128], T.hs[:, 0:128], T.ht[:, 0:512], ["hta"], ["hqa"])
     cut("v")
     mm(0, 128, T.u2q[:], T.u2s[:], T.hq[:, 0:128], T.hs[:, 0:128], ["u2q", "hqa"])
-    quant(T.hq[:, 128:256], T.hs[:, 128:256], T.ht[:, 512:1024], ["htb", "tt"], ["hq"])
+    quant(T.hq[:, 128:256], T.hs[:, 128:256], T.ht[:, 512:1024], ["htb", "h0"], ["hq"])
     cut("v")
     rows("u2", 1, 0, A, T.hq[:, 0:A], T.hs[:, 0:A], ["hq", "hqa"])
     mm(4, 128, T.u2q[:], T.u2s[:], T.hq[:, 128:256], T.hs[:, 128:256], ["u2q", "hq"])
@@ -530,94 +613,128 @@ def rank_program(g, core, T, topo):
 
     tr(T.tn2[:, 0:128], T.ps0[:, 0:128], ["ps0"], ["tn02", "tna2"])
     cut("v")
-    tr(T.tn2[:, 128:A], T.ps4[:, 0:96], ["ps4"], ["tnb2"])
-    cut("v")
+    choose(T.fh[:, 0:8 * A:2], T.ft[:], [[0, 4 * A]], ALU.is_ge, 0.0, 0, 0, ["ft", "ftb"], ["fh"])
+    cut("g")
     passes(2)
     tail(2)
-    act(T.fh[:, 0:8 * A:2], T.ft[:], ACT.Copy, ["ft"], ["fh"])
-    act(T.fh[:, 1:8 * A:2], T.ht[:, 0:896], ACT.Copy, ["hta", "htb"], ["fh"])
-    act(T.v1[:], T.win1[:, 0:A].indirect(T.operm[:]), ACT.Copy, ["operm", "win1"], ["v1"])
-    cut("a")
     cp(T.win2[:].indirect(T.od2[:]), VAL2, ["od2", "VAL2"], ["win2"])
+    cut("v")
+    f_and_h(3)
+    cut("v")
     scan(T.ex2[:], C2, T.win2[:, 0:B], 0.0, ALU.add, ALU.min, ["win2", "C2"], ["ex2"])
     ts(T.og[:], T.ex2[:].indirect(T.oread[:]), PT, None, ALU.add, None, ["ex2", "oread"], ["og"])
-    act(T.gt[:, 16 * GV:512], T.ht[:, 0:896].indirect(T.og[:, GV:32]), ACT.Copy, ["og", "hta", "htb"], ["gt"])
+    cut("v")
+    ts(T.oh[:], T.ex2[:].indirect(T.oread[:]), 0.25, None, ALU.mult, None, ["ex2", "oread"], ["oh"])
+    cut("v")
+    hr = ["og", "hta", "htb"]
+    act(T.gf[:, 128:256], T.ht[:, 0:896].indirect(T.og[:, 8:16]), ACT.Copy, hr, ["gf"])
     cut("a")
-    cp(T.gt[:, 0:16 * GV], T.ht[:, 0:896].indirect(T.og[:, 0:GV]), ["og", "hta", "htb"], ["gt"])
+    act(T.gt[:, 16 * GV:256], T.ht[:, 0:896].indirect(T.og[:, 16 + GV:32]), ACT.Copy, hr, ["gt"])
+    cut("a")
+    cp(T.gf[:, 0:128], T.ht[:, 0:896].indirect(T.og[:, 0:8]), hr, ["gf"])
+    cut("v")
+    cp(T.gt[:, 0:16 * GV], T.ht[:, 0:896].indirect(T.og[:, 16:16 + GV]), hr, ["gt"])
+    cut("v")
+    quant(T.gfq[:], T.gfs[:], T.gf[:], ["gf"], ["gfq"])
+    cut("v")
     quant(T.gq[:, 112:240], T.gs[:, 112:240], T.gt[:], ["gt"], ["gq"])
     cut("v")
 
-    def send(phase):
-        q, s = (T.gq, T.gs) if phase == 1 else (T.tq, T.ts)
-        deps("g", ["gq" if phase == 1 else "tq"], [])
-        hm = _masks(topo.engines(core, hs[0]), (HOP,) * 4)
-        hin, arr = T.sem["hin%d" % phase], T.sem["arr%d" % phase]
+    def send_far(phase):
+        deps("g", ["gfq" if phase == 1 else "tfq"], [])
+        n = FIRST[phase - 1]
+        hm = _masks(topo.engines(core, hs[0])[-4 * n:], (n,) * 4)
         xs = []
         for j in range(4):
             if phase == 1:
-                src, dst = (_u8(q[:, 128 + 32 * j:160 + 32 * j]), _u8(T.rq1[:])) if j < 2 else (s[:, 112:240], T.rs1[:])
+                src, dst = (_u8(T.gfq[:, 32 * j:32 * j + 32]), _u8(T.rq1[:])) if j < 2 else (T.gfs[:], T.rs1[:])
             else:
-                src, dst = (_u8(q[:, S + 28 * j:S + 28 * j + 28]), _u8(T.rq2[:])) if j < 2 else (s[:, 0:112], T.rs2[:])
-            xs.append(_xfer(topo, core, hs[j], hm[j], hin, src, dst))
+                src, dst = (_u8(T.tfq[:, 28 * j:28 * j + 28]), _u8(T.rq2[:])) if j < 2 else (T.tfs[:, 0:112], T.rs2[:])
+            xs.append(_xfer(topo, core, hs[j], hm[j], T.sem["hin%d" % phase], src, dst))
         g.remote_dma_fused(xs, local_sem=T.sem.sent)
+        mark(new_stage("arr%d" % phase, 2 * HOP * len(far)), [], ["far%d" % phase])
+
+    def send_near(phase):
+        q, s = (T.gq, T.gs) if phase == 1 else (T.tq, T.ts)
+        deps("g", ["gq" if phase == 1 else "tq"], [])
         for sizes, buf, wrap in ((DIRECT_CODES, q, _u8), (DIRECT_SCALES, s, lambda a: a)):
             dm = _masks(topo.engines(core, near[0]), sizes)
             xs = []
             for i, d in enumerate(near):
-                a = 112 + 16 * (5 + i) + 2 if phase == 1 else S + S * (4 + i)
-                to = (S if phase == 1 else 128) + S * _slot(d, core, T, topo)
-                xs.append(_xfer(topo, core, d, dm[i], arr, wrap(buf[:, a:a + S]), wrap(buf[:, to:to + S])))
+                a = 128 + 16 * i + 2 if phase == 1 else S + S * (4 + i)
+                to = (S if phase == 1 else 128 - 4 * S) + S * _slot(d, core, T, topo)
+                xs.append(_xfer(topo, core, d, dm[i], T.sem["arn%d" % phase], wrap(buf[:, a:a + S]), wrap(buf[:, to:to + S])))
             g.remote_dma_fused(xs, local_sem=T.sem.sent)
-        mark(new_stage("arr%d" % phase, _arrivals(core, T, topo)), [], ["land%d" % phase])
+        mark(new_stage("arn%d" % phase, _arrivals(core, T, topo)), [], ["near%d" % phase])
 
-    send(1)
-    cp(T.win3[:].indirect(T.od2[:]), T.v1[:], ["od2", "v1"], ["win3"])
-    cut("v")
+    def spread(i):
+        a, b = XS[i:i + 2]
+        cp(T.x2[:].indirect(T.of[:, a:b]), T.a1[:, 32 * a + 1:32 * b:2], ["a1", "of", "x2"], ["x2"])
+        cut("v")
+
+    def layer(bank, q, s, r):
+        for b in range(4):
+            mm(bank + b, 128, T.zq[:, 128 * b:128 * b + 128], T.zp[:, 128 * b:128 * b + 128], q, s, ["z", "gq"] + r)
+
+    def upward(h, bank, q, s, r):
+        for b in range(4):
+            mm(bank + b, 128, T.eq[:, 128 * b:128 * b + 128], T.es[:, 128 * b:128 * b + 128], q, s, ["eq"] + r)
+        for b in range(4):
+            tt(T.il[:, 448 * h + 2 * b + 1:448 * h + 448:8], T.gcomp[:, A * h + b:A * h + A:4], T["ps%d" % (bank + b)][:, 72:128],
+               ALU.add, ["gcomp", "ps%d" % (bank + b)], ["il%d" % h])
+        cut("v")
+        scan(T.io2[:, 448 * h:448 * h + 448], T.keep[:, 0:448], T.il[:, 448 * h:448 * h + 448], 0.0, ALU.mult, ALU.add,
+             ["il", "il%d" % h, "keep"], ["io%d" % h])
+        cp(T.x2[:].indirect(T.ox[:, 14 * h:14 * h + 14]), T.io2[:, 448 * h + 1:448 * h + 448:2], ["io%d" % h, "ox", "x2"], ["x2", "x2c"])
+        cut("v")
+
+    send_far(1)
+    send_near(1)
+    act(T.both[:], T.win1[:, 0:A].indirect(T.oh[:]), ACT.Copy, ["oh", "win1"], ["both"])
     for p in range(8):
-        act(T.yx[:, S * p:S * p + S], T.win3[:, S * order[p]:S * order[p] + S], ACT.Identity, ["win3"], ["yx0"], bias=2048.0 * p)
+        o = 64 * ((p + 4) % 8)
+        act(T.yx[:, S * p:S * p + S], T.both[:, o + 8:o + 64:4], ACT.Identity, ["both"], ["yx0"], bias=2048.0 * p)
     cut("a")
     for p in range(8):
-        act(T.gcomp[:, 56 * p:56 * p + 56], T.gt[:, 64 * p + 8:64 * p + 64], ACT.Copy, ["gt"], ["gcomp"])
-    act(T.olb[:], T.win3[:, 0:B], ACT.Identity, ["win3"], ["olb"], scale=0.25)
+        act(T.gcomp[:, 56 * p:56 * p + 56], (T.gt if p < 4 else T.gf)[:, 64 * (p % 4) + 8:64 * (p % 4) + 64], ACT.Copy,
+            ["gt", "gf"], ["gcomp"])
     cut("a")
-    for h in range(2):
-        scan(T.a1[:, 896 * h:896 * h + 896], T.keep[:], T.fh[:, 896 * h:896 * h + 896], 0.0, ALU.mult, ALU.add, ["fh", "keep"], ["a1"])
+    spread(0)
     scan(T.yx[:, 128:128 + B], kc[:, 256:256 + B], T.yx[:, 0:B], 0.0, ALU.add, ALU.min, ["yx0", "C1"], ["yx1"])
+    cut("v")
+    spread(1)
     ts(kj[:, 0:28], T.yx[:, 131:128 + B:4], PT, None, ALU.add, None, ["yx1"], ["yx2"])
+    cut("v")
+    spread(2)
     ts(kj[:, 32:60], kj[:, 0:28], 2047, None, ALU.bitwise_and, None, ["yx2"], ["yx3"])
+    cut("v")
+    spread(3)
     cp(T.ox[:], kj[:, 32:60], ["yx3"], ["ox"])
     cut("v")
-    act(T.il[:, 0:8 * B:2], T.xb[:].indirect(T.ox[:]), ACT.Copy, ["ox"], ["il"])
-    cut("a")
-    cp(T.x2[:].indirect(T.of[:, 0:X1]), T.a1[:, 1:32 * X1:2], ["a1", "of", "x2"], ["x2a"])
-    cut("v")
+    spread(4)
 
-    for b in range(4):
-        mm(4 + b, 128, T.zq[:, 128 * b:128 * b + 128], T.zp[:, 128 * b:128 * b + 128], T.gq[:, 14:142], T.gs[:, 14:142],
-           ["z", "gq", "land1"])
-    relu4(T.tt, 114, S, 4, "tt")
+    layer(4, T.gq[:, 70:198], T.gs[:, 70:198], ["near1"])
+    relu4(T.tt, 58, 70, 4, "tt", 0, (0, 1, 2, 3))
     quant(T.tq[:, 0:128], T.ts[:, 0:128], T.tt[:], ["tt"], ["tq"])
     cut("v")
-    send(2)
-    quant(T.eq[:], T.es[:], T.eb[:], ["eb"], ["eq"])
+    send_near(2)
+    act(T.il[:, 0:448:2], T.xb[:].indirect(T.ox[:, 0:14]), ACT.Copy, ["ox"], ["il"])
+    cut("a")
+    spread(5)
+    layer(0, T.gq[:, 14:142], T.gs[:, 14:142], ["near1", "far1"])
+    relu4(T.tf, 56, 0, 0, "tf", 0, (0, 1, 2, 3))
+    quant(T.tfq[:, 0:128], T.tfs[:, 0:128], T.tf[:], ["tf"], ["tfq"])
     cut("v")
-    cp(T.x2[:].indirect(T.of[:, X1:56]), T.a1[:, 32 * X1 + 1:8 * A:2], ["a1", "of", "x2a"], ["x2b"])
-    quant(T.vq[:], T.vs[:], T.vb[:], ["vb"], ["vq"])
-    cut("v")
+    send_far(2)
+    act(T.il[:, 448:896:2], T.xb[:].indirect(T.ox[:, 14:28]), ACT.Copy, ["ox"], ["il"])
+    for p in range(8):
+        act(T.olb[:, S * order[p]:S * order[p] + S], T.both[:, 64 * p + 8:64 * p + 64:4], ACT.Identity, ["both"], ["olb"], scale=0.25)
+    cut("a")
+    spread(6)
 
-    for b in range(4):
-        mm(b, 128, T.eq[:, 128 * b:128 * b + 128], T.es[:, 128 * b:128 * b + 128], T.tq[:, 98:226], T.ts[:, 98:226],
-           ["eq", "tq", "land2"])
-    dma("y", [(T.ol[i:i + 1, :], T.olb[16 * i:16 * i + 1, :]) for i in range(8)], ["olb", "land2"], [])
-    for h in range(2):
-        for b in range(4):
-            tt(T.il[:, 448 * h + 2 * b + 1:448 * h + 448:8], T.gcomp[:, A * h + b:A * h + A:4], T["ps%d" % b][:, 16 + 56 * h:72 + 56 * h],
-               ALU.add, ["gcomp", "ps%d" % b], ["il%d" % h])
-        cut("v")
-    for h in range(2):
-        scan(T.io2[:, 448 * h:448 * h + 448], T.keep[:, 0:448], T.il[:, 448 * h:448 * h + 448], 0.0, ALU.mult, ALU.add,
-             ["il", "il%d" % h, "keep"], ["io2"])
-    cp(T.x2[:].indirect(T.ox[:]), T.io2[:, 1:8 * B:2], ["io2", "ox", "x2a", "x2b"], ["x2c"])
+    upward(0, 4, T.tq[:, 42:170], T.ts[:, 42:170], ["tq", "near2"])
+    dma("y", [(T.ol[i:i + 1, :], T.olb[16 * i:16 * i + 1, :]) for i in range(8)], ["olb", "near2"], [])
+    upward(1, 0, T.tfq[:, 56:184], T.tfs[:, 56:184], ["tfq", "far2"])
     for h, (a, b) in enumerate(((0, O1), (O1, C))):
         quant(T.oq[:, a:b], T.osb[:, a:b], T.x2[:, 4 * a:4 * b], ["x2c"], ["oq%d" % h])
         cut("v")
@@ -630,7 +747,7 @@ def rank_program(g, core, T, topo):
     dma("y", [(T.y[:, O1:C], T.yb[:, O1:C])], ["y1"], [])
     dma("a", [(T.osc[4 * i:4 * i + 4, :], T.osb[32 * i:32 * i + 4, :]) for i in (2, 3)], ["oq0", "oq1"], [])
 
-    g.wait_ge(T.sem.sent, 2 * (4 * HOP + sum(DIRECT_CODES) + sum(DIRECT_SCALES)))
+    g.wait_ge(T.sem.sent, 4 * sum(FIRST) + 2 * (sum(DIRECT_CODES) + sum(DIRECT_SCALES)))
     for st in stages:
         if not st["waited"]:
             need("g", st)

from concourse.bass import DstId, RemoteDMATransfer
from concourse.mybir import dt, AluOpType, AxisListType, ActivationFunctionType

C, A, B, S = 448, 224, 112, 14
BIG = float(2 ** 90)
DIM = 2.0 ** -60
HOLD = float(2 ** 20)
Q4, U8 = "float8_e4m3fn_x4", "uint8"
GV = 8
XA = 320
XS = (0, 20, 24, 28, 32, 34, 40, 56)
O1 = 192
FA, FB = 16, 50
FIRST = (4, 2)
P1 = ("a2 a0 a3 TB T1 R1 T2 S R2 T4 T3 v4 v5 v6 v7 s4 s5 a10 a9 a11 a8 a1 u10+2 s7 s6 q10+2 u8+2 u4+4 c4+4 q4+4 q8+2 "
      "v18 v17 v16 s18 s17 D s16 c18 c16+2 a19 a13 a15 a14 a12")
V1 = (4, 5, 6, 7, 16, 17, 18)
P2 = "TB a0 a2 a4 a6 a8 a10 a12 a1 a3 v5 S v7 v9 v11 v13 s5 s7 s9 s11 s13 B c5+5/2 B"
V2 = (5, 7, 9, 11, 13)
PLAN = {1: (2, 4, 0, 4, P1.split(), V1), 2: (7, 0, 0, 0, P2.split(), V2)}
NS1, NS2, NV1, NV2 = 13, 9, 7, 5


def _sb(n, d):
    return ("sbuf", [128, n], d)


SCRATCH = {
    "xb": _sb(4 * C, "bfloat16"), "x2": _sb(4 * C, "bfloat16"),
    "u1b": _sb(512, "bfloat16"), "u2b": _sb(512, "bfloat16"), "vb": _sb(512, "bfloat16"),
    "xq": _sb(C, Q4), "xs": _sb(C, U8),
    "u1q": _sb(128, Q4), "u1s": _sb(128, U8), "u1pq": _sb(256, Q4), "u1ps": _sb(256, U8),
    "u2q": _sb(128, Q4), "u2s": _sb(128, U8), "u2pq": _sb(256, Q4), "u2ps": _sb(256, U8),
    "vq": _sb(128, Q4), "vs": _sb(128, U8),
    "wq": _sb(512, Q4), "wp": _sb(512, U8), "zq": _sb(512, Q4), "zp": _sb(512, U8),
    "eb": _sb(2048, "bfloat16"), "eq": _sb(512, Q4), "es": _sb(512, U8),
    "ft": _sb(4 * A, "bfloat16"), "fq": _sb(256, Q4), "fs": _sb(256, U8),
    "ht": _sb(1024, "bfloat16"), "hq": _sb(256, Q4), "hs": _sb(256, U8),
    "gt": _sb(512, "bfloat16"), "gq": _sb(240, Q4), "gs": _sb(240, U8),
    "gf": _sb(512, "bfloat16"), "gfq": _sb(128, Q4), "gfs": _sb(128, U8),
    "tt": _sb(512, "bfloat16"), "tq": _sb(176, Q4), "ts": _sb(176, U8),
    "tf": _sb(512, "bfloat16"), "tfq": _sb(184, Q4), "tfs": _sb(184, U8),
    "gcomp": _sb(4 * B, "bfloat16"), "il": _sb(8 * B, "bfloat16"), "io2": _sb(8 * B, "bfloat16"),
    "keep": _sb(8 * B, "bfloat16"), "fh": _sb(8 * A, "bfloat16"), "a1": _sb(8 * A, "bfloat16"),
    "oq": _sb(C, Q4), "osb": _sb(C, U8), "yb": _sb(C, "float32"),
    "rq1": _sb(32, Q4), "rs1": _sb(128, U8), "rq2": _sb(28, Q4), "rs2": _sb(112, U8),
    "ki": _sb(32, "int32"), "kj": _sb(128, "int32"), "kf": _sb(1280, "float32"), "kc": _sb(896, "float32"),
    "opick": _sb(16, "uint16"), "oread": _sb(2, "uint16"),
    "od1": _sb(28, "uint16"), "od2": _sb(16, "uint16"),
    "of": _sb(56, "uint16"), "og": _sb(32, "uint16"), "oh": _sb(32, "uint16"), "ox": _sb(28, "uint16"),
    "tn1": _sb(C, "float32"), "tn2": _sb(A, "float32"),
    "junk1": _sb(NS1 * C, "bfloat16"), "junk2": _sb(NS2 * A, "bfloat16"),
    "fl1": _sb(NV1 * C, "bfloat16"), "fl2": _sb(NV2 * A, "bfloat16"),
    "so1": _sb(NV1 * C // 2, "bfloat16"), "so2": _sb(NV2 * A // 2, "bfloat16"),
    "wa": _sb(1024, "float32"), "w1": _sb(1024, "float32"), "w2": _sb(1024, "float32"),
    "dd": _sb(136, "float32"), "cm1": _sb(256, "float32"), "cm2": _sb(256, "float32"),
    "win1": _sb(4608, "float32"), "win2": _sb(2304, "float32"), "both": _sb(512, "float32"),
    "val1": _sb(C, "float32"), "runs": ("dram", [8, 512], "float32"),
    "ex1": _sb(A, "float32"), "ex2": _sb(B, "float32"),
    "olb": _sb(B, "float32"), "yx": _sb(256, "float32"),
}
for _i in range(8):
    SCRATCH["ps%d" % _i] = ("psum", [128, 512], "float32")

NPOOL = 143
SEMAPHORES = ["arr1", "arr2", "arn1", "arn2", "hin1", "hin2", "sent"] + ["s%d" % _i for _i in range(NPOOL)]

ALU = AluOpType
ACT = ActivationFunctionType
DIRECT_CODES, DIRECT_SCALES = (4, 2, 2), (2, 2, 4)
HOP = 4


def _plan(core, T, topo):
    far = [d for d in T.cores if d != core and not topo.may_write(core, d)]
    near = [d for d in T.cores if d != core and topo.may_write(core, d)]
    hs = [h for h in topo.cores_of(core) if h != core and all(topo.may_write(h, d) for d in far)]
    hs.sort(key=lambda h: (topo.die(h) != topo.die(core), h))
    return far, near, hs


def _masks(engines, sizes):
    out, at = [], 0
    for n in sizes:
        m = 0
        for e in engines[at:at + n]:
            m |= 1 << e
        out.append(m)
        at += n
    return out


def _xfer(topo, src_core, dst_core, mask, sem, src, dst):
    rid, pid = topo.addr(dst_core, src_core)
    return RemoteDMATransfer(dst_ids=[DstId(rid=rid, pnc=pid)], dma_engine_mask=mask, remote_sem=sem, src=src, dst=dst)


def _slot(dst, src, T, topo):
    far, near, hs = _plan(dst, T, topo)
    return (far + near).index(src)


def _arrivals(core, T, topo):
    n = 0
    for s in _plan(core, T, topo)[1]:
        i = _plan(s, T, topo)[1].index(core)
        n += DIRECT_CODES[i] + DIRECT_SCALES[i]
    return n


def _u8(v):
    return v.bitcast(dt.uint8)


def helper_program(g, core, T, topo, home):
    far, near, hs = _plan(home, T, topo)
    if core not in hs:
        return
    j = hs.index(core)
    pair = (2 * (j % 2), 2 * (j % 2) + 1)
    masks = _masks(topo.engines(core, far[0]), (HOP, HOP))
    for phase in (1, 2):
        g.wait_ge(T.sem["hin%d" % phase], FIRST[phase - 1])
        xs = []
        for n, i in enumerate(pair):
            d = far[i]
            at = (S if phase == 1 else 128) + S * _slot(d, home, T, topo)
            if j < 2:
                src = T.rq1[:, 16 * n + 2:16 * n + 16] if phase == 1 else T.rq2[:, S * n:S * n + S]
                dst = (T.gq if phase == 1 else T.tfq)[:, at:at + S]
                src, dst = _u8(src), _u8(dst)
            else:
                src = T.rs1[:, 16 * i + 2:16 * i + 16] if phase == 1 else T.rs2[:, S * i:S * i + S]
                dst = (T.gs if phase == 1 else T.tfs)[:, at:at + S]
            xs.append(_xfer(topo, core, d, masks[n], T.sem["arr%d" % phase], src, dst))
        g.remote_dma_fused(xs, local_sem=T.sem.sent)
    g.wait_ge(T.sem.sent, 4 * HOP)


def rank_program(g, core, T, topo):
    rank = T.rank_of(core)
    if rank is None:
        for c in topo.cores_of(core):
            if T.rank_of(c) is not None:
                helper_program(g, core, T, topo, c)
        return
    far, near, hs = _plan(core, T, topo)
    order = [T.rank_of(d) for d in far + [core] + near]
    V, SC, PE, SY = g.vector, g.scalar, g.tensor, g.sync
    eng = {"g": g, "v": V, "a": SC, "p": PE, "y": SY}

    pool = [0]
    known = {e: set() for e in eng}
    stage = {e: None for e in eng}
    stages = []
    writer, readers, latest = {}, {}, {}

    def new_stage(sem=None, count=0):
        if sem is None:
            sem = "s%d" % pool[0]
            pool[0] += 1
        st = {"sem": sem, "n": count, "before": set(), "k": len(stages), "waited": False}
        stages.append(st)
        return st

    def need(e, st):
        if st["k"] in known[e]:
            return
        for q in stage:
            if stage[q] is st:
                stage[q] = None
        eng[e].wait_ge(T.sem[st["sem"]], st["n"])
        st["waited"] = True
        known[e].add(st["k"])
        known[e].update(st["before"])

    def deps(e, r, w):
        sts = []
        for n in r:
            sts += writer.get(n, [])
        for n in w:
            sts += readers.get(n, [])
        for st in sorted(sts, key=lambda s: -s["k"]):
            need(e, st)

    def mark(st, r, w):
        for n in r:
            readers.setdefault(n, []).append(st)
        for n in w:
            writer.setdefault(n, []).append(st)

    def op(e, call, r, w):
        deps(e, r, w)
        if stage[e] is None:
            mine = latest.setdefault(e, {})
            done = [old for old in mine.values() if old["k"] in known[e]]
            stage[e] = new_stage(done[-1]["sem"], done[-1]["n"]) if done else new_stage()
            mine[stage[e]["sem"]] = stage[e]
        st = stage[e]
        call().then_inc(T.sem[st["sem"]], 1)
        st["n"] += 1
        st["before"].update(known[e])
        mark(st, r, w)

    def cut(e):
        stage[e] = None

    def dma(e, pairs, r, w):
        deps(e, r, w)
        st = new_stage()
        for out, in_ in pairs:
            eng[e].dma_start(out, in_).then_inc(T.sem[st["sem"]], 16)
            st["n"] += 16
        st["before"].update(known[e])
        mark(st, r, w)

    def ts(out, in0, s1, s2, o0, o1, r, w):
        if o1 is None:
            op("v", lambda: V.tensor_scalar(out, in0, s1, None, o0), r, w)
        else:
            op("v", lambda: V.tensor_scalar(out, in0, s1, s2, o0, o1), r, w)

    def tt(out, a, b, o, r, w):
        op("v", lambda: V.tensor_tensor(out, a, b, o), r, w)

    def cp(out, in_, r, w):
        op("v", lambda: V.tensor_copy(out, in_), r, w)

    def ms(out, c, w):
        op("v", lambda: V.memset(out, c), [], w)

    def tr(out, in_, r, w):
        op("v", lambda: V.transpose(out, in_), r, w)

    def scan(out, d0, d1, init, o0, o1, r, w):
        op("v", lambda: V.tensor_tensor_scan(out, d0, d1, init, o0, o1), r, w)

    def quant(q, s, t, r, w):
        op("v", lambda: V.quantize_mx(q, s, t), r, w)

    def act(out, in_, f, r, w, **kw):
        op("a", lambda: SC.activation(out, in_, f, **kw), r, w)

    def mm(bank, n, lq, ls, rq, rs, r):
        name = "ps%d" % bank
        op("p", lambda: PE.matmul_mx(T[name][:, 0:n], lq, ls, rq, rs, True, True), r, [name])
        writer[name] = writer[name][-1:]
        readers[name] = []
        cut("p")

    def iota(out, pattern, base, cm, w, r=(), whole=False):
        if whole:
            op("g", lambda: g.iota(out, pattern, base, cm), r, w)
        else:
            op("g", lambda: g.iota(out, pattern, base, cm, allow_small_or_imprecise_dtypes=True), r, w)

    def choose(out, in_, pattern, o, fill, base, cm, r, w):
        op("g", lambda: g.affine_select(out, in_, pattern, o, fill, base, cm), r, w)

    dma("a", [(T.u1b[:], T.u1[:])], [], ["u1b"])
    dma("y", [(T.xb[:, 0:4 * XA], T.x[:, 0:4 * XA])], [], ["xb0"])
    dma("a", [(T.xb[:, 4 * XA:4 * C], T.x[:, 4 * XA:4 * C])], [], ["xb1"])
    dma("y", [(T.u2b[:], T.u2[:])], ["xb0", "xb1"], ["u2b"])
    dma("y", [(_u8(T.wq[:]), T.wc[:]), (T.wp[:], T.ws[:])], [], ["w"])

    kf, kc, ki, kj, wa, dd = T.kf, T.kc, T.ki, T.kj, T.wa, T.dd
    KR, R4 = kf[:, 1152:1248], kf[:, 128:352]
    VAL1, VAL2 = T.val1[:], kf[:, 864:1120]

    def rounds(L):
        W = 28 if L == 1 else 16
        return W, 128, 128 + 4 * W, 128 + 8 * W

    def round_constants(L):
        wb, cm, k = T["w%d" % L], T["cm%d" % L], (A if L == 1 else B)
        W, d1, d0, out = rounds(L)
        a, b = "Ra%d" % L, "Rb%d" % L
        iota(cm[:, 0:128], [[0, 128]], 0, 0, [a + "0"])
        iota(wb[:, d0:out], [[-1, W], [0, 4]], -(k + 1), -W, [b + "0"])
        iota(cm[:, 0:1], [[0, 1]], k, W, [a], [a + "0"])
        iota(cm[:, 31:32], [[0, 1]], -(k + W), -W, [a], [a + "0"])
        choose(wb[:, d0:out], wb[:, d0:out], [[0, W], [-1, 4]], ALU.is_ge, 1.0, 2, 0, [b + "0"], [b + "1"])
        choose(wb[:, d0:out], wb[:, d0:out], [[0, W], [1, 4]], ALU.is_ge, 0.0, -2, 0, [b + "1"], [b])
        cut("g")

    iota(ki[:, 0:16], [[16, 2], [32, 4], [0, 2]], 0, 0, ["ipick"], whole=True)
    cut("g")
    iota(dd[0:32, :], [[0, 136]], 1, 0, ["M0"])
    iota(KR, [[0, 96]], 1, 0, ["M0"])
    choose(dd[0:32, 32:64], dd[0:32, 32:64], [[1, 32]], ALU.not_equal, DIM, 0, -1, ["M0"], ["M1"])
    choose(dd[0:32, 96:128], dd[0:32, 96:128], [[1, 32]], ALU.not_equal, 1 / DIM, -1, -1, ["M0"], ["M1"])
    choose(KR, KR, [[1, 96]], ALU.not_equal, 0.0, -64, 0, ["M0"], ["KR"])
    choose(dd[0:32, 32:33], dd[0:32, 32:33], [[0, 1]], ALU.is_ge, DIM, 15, -1, ["M1"], ["M2"])
    choose(dd[0:32, 48:49], dd[0:32, 130:131], [[0, 1]], ALU.is_ge, 1 / DIM, 16, -1, ["M1"], ["M2"])
    choose(dd[0:32, 64:65], dd[0:32, 64:65], [[0, 1]], ALU.is_gt, 1 / DIM, 0, 0, ["M1"], ["M2"])
    choose(dd[0:32, 96:97], dd[0:32, 96:97], [[0, 1]], ALU.is_gt, DIM, 0, 0, ["M1"], ["M2"])
    choose(dd[0:32, 112:113], dd[0:32, 131:132], [[0, 1]], ALU.is_ge, DIM, -15, 1, ["M1"], ["M2"])
    cut("g")
    dma("y", [(dd[32 * a:32 * a + 32, 0:128], dd[0:32, 0:128]) for a in (1, 2, 3)], ["M2"], ["MASK"])
    round_constants(1)
    iota(kf[:, 0:32], [[-4, 32]], 0, 1, ["N0"])
    iota(kf[:, 32:64], [[0, 8], [-1, 4]], 0, 0, ["N0"])
    iota(kf[:, 1144:1152], [[0, 4], [1, 2]], 0, 0, ["N0"])
    iota(R4, [[0, 56], [1, 4]], 0, 0, ["R4"])
    choose(kf[:, 0:64], kf[:, 0:64], [[0, 2], [-4, 32]], ALU.is_ge, 0.0, 0, 1, ["N0"], ["N1"])
    choose(kf[:, 1144:1152], kf[:, 1144:1152], [[-16, 8]], ALU.is_ge, 0.0, 0, 1, ["N0"], ["N1"])
    choose(kf[:, 0:64], kf[:, 0:64], [[0, 2], [4, 32]], ALU.is_ge, 0.0, 3, -1, ["N1"], ["N2"])
    choose(kf[:, 1144:1152], kf[:, 1144:1152], [[16, 8]], ALU.is_ge, 0.0, 15, -1, ["N1"], ["N2"])
    cut("g")
    iota(VAL1, [[4, 28], [112, 16]], 0, 0, ["VAL1"])
    cut("g")
    for p in range(8):
        iota(kf[:, 608 + 32 * p:640 + 32 * p], [[4, 4], [0, 8]], S * order[p] + 1, 0, ["RR0"])
    choose(kf[:, 608:864], kf[:, 608:864], [[0, 2], [1, 16], [16, 8]], ALU.is_equal, 0.0, 0, -1, ["RR0"], ["RR"])
    cut("g")
    iota(T.keep[:], [[0, 4 * B], [1, 2]], 0, 0, ["keep"])
    cut("g")
    for b in range(4):
        o = (b + 1) % 2
        choose(T.eb[:, 512 * b:512 * b + 512], T.keep[:, o:o + 512], [[-1, 512]], ALU.is_equal, 0.0, b, 4, ["keep"], ["eb"])
    cut("g")
    round_constants(2)
    iota(VAL2, [[4, 16], [64, 16]], 0, 0, ["VAL2"])
    cut("g")

    XX, MB, T2, O2, ZJ, ZB, ZT, TC, O3, COL = 32, 192, 320, 448, 512, 544, 576, 608, 704, 800
    UW, SPW, SD, LO = 704, 752, 800, 816
    ms(T.w1[:, SD:SD + 16], BIG, ["SD1"])
    for wb, n in ((T.w1, "1"), (T.w2, "2")):
        ms(wb[:, 64:128], -BIG, ["Spp" + n])
    for at, c in ((20, BIG), (84, -BIG)):
        ms(wa[:, XX + at:XX + at + 32], c, ["KK"])
    ms(wa[:, T2:T2 + 32], -BIG, ["KK"])
    ms(wa[:, T2 + 96:T2 + 128], BIG, ["KK"])
    ms(T.tt[:, 0:280], 0.0, ["tt"])
    ms(T.tf[:, 224:512], 0.0, ["tf"])
    ms(T.ht[:, 896:1024], 0.0, ["h0"])
    ms(T.gf[:, 256:512], 0.0, ["gf"])
    ms(T.gt[:, 256:512], 0.0, ["gt"])
    cp(T.opick[:], ki[:, 0:16], ["ipick"], ["opick"])
    PT, NPQ, PH, N0 = (kc[:, i:i + 1] for i in range(4))
    C1, C1A = kc[:, 256:480], kc[:, 480:704]
    C2 = kc[:, 704:816]

    def pick_codes(u, a=0, b=2):
        cp(T[u + "pq"][:, 128 * a:128 * b].bitcast(dt.uint32), T[u + "q"][:].bitcast(dt.uint32).indirect(T.opick[:, 8 * a:8 * b]),
           [u + "q", "opick"], [u + "pq"])
        cut("v")

    def pick_scales(u, a=0, b=2):
        act(T[u + "ps"][:, 128 * a:128 * b], T[u + "s"][:].indirect(T.opick[:, 8 * a:8 * b]), ACT.Copy, [u + "q", "opick"], [u + "ps"])
        cut("a")

    def rows(u, bank, h, n, q, s, name):
        mm(bank, n, T[u + "pq"][:, 128 * h:128 * h + 128], T[u + "ps"][:, 128 * h:128 * h + 128], q, s, [u + "pq", u + "ps"] + name)

    def halves(h, half):
        ts(T.w2[:, 96 + 16 * h + half:110 + 16 * h:2], T.tn2[:, 16 * h:A:32], PH if half else N0, None, ALU.mult, None,
           ["tna2", "tnb2", "Spp2", "C1"], ["Sd2"])

    def unit(b):
        quant(T.eq[:, 128 * b:128 * b + 128], T.es[:, 128 * b:128 * b + 128], T.eb[:, 512 * b:512 * b + 512], ["eb"], ["eq"])

    def f_and_h(i):
        scan(T.a1[:, 448 * i:448 * i + 448], T.keep[:, 0:448], T.fh[:, 448 * i:448 * i + 448], 0.0, ALU.mult, ALU.add,
             ["fh", "keep"], ["a1"])

    spare = {
        1: [lambda: quant(T.u2q[:], T.u2s[:], T.u2b[:], ["u2b"], ["u2q"]), None,
            lambda: quant(T.vq[:], T.vs[:], T.vb[:], ["vb"], ["vq"]), lambda: pick_codes("u2", 0, 1), None,
            lambda: pick_codes("u2", 1, 2), None, None, None],
        2: [lambda: [halves(0, 0), halves(0, 1)], lambda: [halves(1, 0), halves(1, 1)],
            lambda: tr(T.w2[:, 960:992], T.w2[:, 96:128], ["Sd2"], ["St2"]),
            lambda: tt(T.w2[:, 992:1008], T.w2[:, 960:976], T.w2[:, 976:992], ALU.add, ["St2"], ["Sc2"]),
            lambda: unit(0), lambda: unit(1), lambda: unit(2), lambda: unit(3),
            lambda: f_and_h(0), lambda: f_and_h(1), lambda: f_and_h(2)],
    }
    late = {1: lambda: tr(T.tn1[:, XA:C], T.ps4[:, 0:C - XA], ["ps4"], ["tnb1"]),
            2: lambda: tr(T.tn2[:, 128:A], T.ps4[:, 0:96], ["ps4"], ["tnb2"])}

    def between(L):
        cut("v")
        call = spare[L].pop(0)
        if call is not None:
            call()
            cut("v")

    def passes(L):
        n, k = (C, A) if L == 1 else (A, B)
        ns, nt, eS, eA, plan, vl = PLAN[L]
        wb, tn, junk, fl, so = (T[s + str(L)] for s in ("w", "tn", "junk", "fl", "so"))
        nb, first = n // 32, (XA if L == 1 else 128)
        cm, cq, cd = 2 * ns, 2 * ns + 2 * nt, 2 * ns + 4 * nt
        X = lambda s: s + str(L)
        tns = [X("tn0"), X("tna"), X("tnb")]
        part = lambda e: X("tn0") if 16 * e < 64 else X("tna") if 16 * e < first else X("tnb")
        parts = lambda e, m: sorted({part(i) for i in range(e, e + m)})
        col = lambda e, m: tn[:, 16 * e:16 * (e + m):16]
        al = [int(s[1:]) for s in plan if s[0] == "a"]
        ends = lambda c, m: so[:, k * vl.index(c) + k - 1:k * (vl.index(c) + m):k]
        if nt:
            lo, hi, mid = (wb[:, LO + 8 * i:LO + 8 * i + 2 * nt] for i in range(3))
            third, there = col(eA + 4 * nt, 2 * nt), parts(eA + 4 * nt, 2 * nt)

        def pivot(c):
            if c < cm:
                return col(eS + c, 1), part(eS + c)
            return wb[:, SPW + 2 * c + 1:SPW + 2 * c + 2], X("med") if c < cq else X("q%d_" % c)

        for s in plan:
            kind, c, m, step = s[0], 0, 1, 1
            if kind in "avscuq":
                z = [int(i) for i in s[1:].replace("/", "+").split("+")]
                c, m, step = z + [1, 1][len(z) - 1:]
            some = range(c, c + m * step, step)
            if kind == "a":
                p, name = pivot(c)
                i, bank = al.index(c), ("ps1", "ps3")[c % 2]
                act(junk[:, n * i:n * i + n], T[bank][:, 0:n], ACT.Sign, [bank, name], [X("V%d_" % c), X("V")],
                    bias=p, scale=-1.0, accum_out=wb[:, c:c + 1])
                if nt:
                    cut("a")
                continue
            if kind == "v":
                p, name = pivot(c)
                i, bank = vl.index(c), ("ps5", "ps2")[c % 2]
                ts(fl[:, n * i:n * i + n], T[bank][:, 0:n], p, 0.5, ALU.is_lt, ALU.subtract, [bank, name], [X("fl%d_" % c)])
            elif kind == "s":
                i = vl.index(c)
                scan(so[:, k * i:k * i + k], fl[:, n * i:n * i + k], fl[:, n * i + k:n * i + n], 0.0, ALU.add, ALU.add,
                     [X("fl%d_" % c)], [X("so%d_" % c)])
            elif kind == "c":
                cp(wb[:, c:c + m * step:step], ends(c, m), [X("so%d_" % i) for i in some], [X("V%d_" % i) for i in some] + [X("V")])
            elif kind == "u":
                src, name = (ends(c, m), "so%d_") if c in vl else (wb[:, c:c + m], "V%d_")
                ts(wb[:, UW + 2 * c:UW + 2 * (c + m):2], src, 0.25, -BIG, ALU.add, ALU.mult, [X(name % i) for i in some], [X("u%d_" % c)])
            elif kind == "q":
                j = c - cm
                scan(wb[:, SPW + 2 * (cq + j):SPW + 2 * (cq + j + m)], wb[:, SD + 2 * j:SD + 2 * (j + m)], wb[:, UW + 2 * c:UW + 2 * (c + m)],
                     0.0, ALU.max, ALU.min, [X("u%d_" % c), X("ends")], [X("q%d_" % (cq + j + i)) for i in range(m)] + [X("Sp")])
            elif s == "T1":
                tt(lo, col(eA, 2 * nt), col(eA + 2 * nt, 2 * nt), ALU.min, parts(eA, 4 * nt), [X("lo")])
                tt(hi, col(eA, 2 * nt), col(eA + 2 * nt, 2 * nt), ALU.max, parts(eA, 4 * nt), [X("lo")])
            elif s == "T2":
                tt(mid, hi, third, ALU.min, [X("lo")] + there, [X("mid")])
            elif s == "T3":
                tt(wb[:, SD + 1:SD + 4 * nt:2], lo, third, ALU.min, [X("lo"), X("SD")] + there, [X("ends")])
                tt(wb[:, UW + 2 * cm + 1:UW + 2 * cq:2], hi, third, ALU.max, [X("lo")] + there, [X("ends")])
            elif s == "T4":
                tt(wb[:, SPW + 2 * cm + 1:SPW + 2 * cq:2], lo, mid, ALU.max, [X("lo"), X("mid")], [X("med"), X("Sp")])
            elif s == "TB":
                late[L]()
            elif s == "S":
                cp(wb[:, SPW + 1:SPW + 2 * cm:2], col(eS, cm), parts(eS, cm), [X("Sp")])
            elif s == "D":
                cp(wb[:, cd:cd + 2 * nt], wb[:, cm:cq], [X("V%d_" % i) for i in range(cm, cq)], [X("V")])
            elif s == "R1":
                for h in range(2):
                    cp(wb[:, 64 + 16 * h:64 + 16 * h + nb], tn[:, 16 * h:n:32], tns + ["Spp1"], ["So1"])
            elif s == "R2":
                tr(wb[:, 96:128], wb[:, 64:96], ["So1", "Spp1"], ["St1"])
                cut("v")
                dma("y", [(T.runs[:], wb[:, 96:128])], ["St1"], ["runs"])
                dma("y", [(wb[:, 960:988], T.runs[:, 0:C])], ["runs"], ["Sc1"])
                dma("y", [(T.vb[:], T.v[:])], [], ["vb"])
                dma("y", [(_u8(T.zq[:]), T.zc[:]), (T.zp[:], T.zs[:])], [], ["z"])
                dma("y", [(T.x2[:], T.x[:])], [], ["x2"])
            else:
                between(L)
            cut("v")
        cut("a")

    def tail(L):
        k, wb, cm = (A if L == 1 else B), T["w%d" % L], T["cm%d" % L]
        W, d1, d0, out = rounds(L)
        ns, nt = PLAN[L][:2]
        R, nb = 2 * ns + 4 * nt, ns + 3 * nt
        X = lambda s: s + str(L)
        a = lambda at, n: wa[:, at:at + n]
        U, Sp = wb[:, UW:UW + 2 * R:2], wb[:, SPW + 1:SPW + 2 * R:2]
        Sc = wb[:, 960:988] if L == 1 else wb[:, 992:1008]
        for h in range(2):
            act(a(ZJ + 16 * h, nb), wb[:, h:2 * nb:2], ACT.Sign, [X("V")], ["zc"], bias=0.25, accum_out=a(COL + h, 1))
        for h in range(2):
            act(a(ZB + 16 * h, 16), a(T2 + 96, 16), ACT.Identity, ["zc", "KK"], ["zb"], scale=a(COL + h, 1), bias=BIG / 32)
        cut("a")
        ts(U, wb[:, 0:R], 0.25, -BIG, ALU.add, ALU.mult, [X("V")], [X("U")])
        between(L)
        tt(a(XX + 20 - R, R), Sp, U, ALU.max, [X("U"), X("Sp")], ["xx"])
        tt(a(XX + 84 - R, R), Sp, U, ALU.min, [X("U"), X("Sp")], ["xx"])
        between(L)
        w = R // 2 + 16
        for x, m, c, o0, o1, idle in ((XX + 20 - R, MB + 96, BIG, ALU.min, ALU.max, T2), (XX + 84 - R, MB + 32, -BIG, ALU.max, ALU.min, T2 + 96)):
            scan(a(m - w, w), wa[:, x:x + 2 * w:2], a(idle, w), c, o0, o1, ["xx", "KK"], ["mb"])
            scan(wa[:, m + w - 1:m - 1:-1], wa[:, x + 1:x + 2 * w:2], a(idle, w), c, o0, o1, ["xx", "KK"], ["mb"])
        cut("v")
        tr(a(ZT, 32), a(ZB, 32), ["zb"], ["zt"])
        cut("v")
        act(a(ZJ, 32), a(ZT, 32), ACT.Identity, ["zt"], ["zz"], accum_out=a(COL + 2, 1))
        cut("a")
        if L == 2:
            act(T.fh[:, 1:8 * A:2], T.ht[:, 0:896], ACT.Copy, ["hta", "htb"], ["fh"])
            cut("a")
        tr(a(T2 + 32, 32), a(MB + 16, 32), ["mb"], ["t2"])
        tr(a(T2 + 64, 32), a(MB + 80, 32), ["mb"], ["t2"])
        between(L)
        scan(a(O2, 64), a(T2 + 64, 64), a(T2, 64), a(COL + 2, 1), ALU.min, ALU.max, ["t2", "zz"], ["o2"])
        t = a(O2 + 63, 1)
        ts(cm[:, 31 - W:31], Sc, t, 1.0, ALU.is_gt, ALU.add, ["o2", X("Sc"), X("Ra")], [X("fg")])
        ts(cm[:, 64:64 + W], Sc, t, None, ALU.is_equal, None, ["o2", X("Sc")], [X("fg")])
        cut("v")
        ts(wb[:, d1 + 1:d0:4], Sc, t, None, ALU.is_gt, None, ["o2", X("Sc")], [X("slots")])
        ts(wb[:, d1:d0:4], Sc, t, None, ALU.is_equal, None, ["o2", X("Sc")], [X("slots")])
        cut("v")
        scan(cm[:, 159 - W:256], dd[:, 31 - W:128], cm[:, 31 - W:128], cm[:, 0:1], ALU.mult, ALU.add, [X("fg"), "MASK"], [X("cum")])
        between(L)
        own, ceq = cm[:, 159:160], cm[:, 192:192 + W]
        tr(a(TC, 96), cm[:, 160:256], [X("cum")], ["tc"])
        cut("v")
        cp(wb[:, d1 + 2:d0:4], cm[:, 159 - W:159], [X("cum")], [X("slots")])
        between(L)
        scan(a(O3, 96), KR, a(TC, 96), k + 0.25, ALU.mult, ALU.subtract, ["tc", "KR"], ["o3"])
        between(L)
        p1, p2 = a(O3 + 95, 1), a(O3 + 31, 1)
        ts(wb[:, d1 + 3:d0:4], ceq, p1, p2, ALU.subtract, ALU.min, ["o3"], [X("ws")])
        ts(wb[:, d0 + 1:out:4], ceq, p1, p2, ALU.subtract, ALU.is_le, ["o3", X("Rb")], [X("ws")])
        between(L)
        scan(wb[:, out:out + 4 * W], wb[:, d0:out], wb[:, d1:d0], 0.0, ALU.mult, ALU.add, [X("ws"), X("slots")], [X("dest")])
        between(L)
        ts(T["od%d" % L][:], wb[:, out + 3:out + 4 * W:4], own, 1.0, ALU.subtract, ALU.subtract, [X("dest")], [X("od")])
        between(L)

    def relu4(out, n, skip, bank0, w, at=0, scalar=(0, 2)):
        for b in range(4):
            o, src, name = out[:, 4 * skip + b:4 * (skip + n):4], T["ps%d" % (bank0 + b)][:, at:at + n], "ps%d" % (bank0 + b)
            if b in scalar:
                act(o, src, ACT.Relu, [name], [w], scale=0.03125)
            else:
                ts(o, src, 0.0, 0.03125, ALU.max, ALU.mult, [name], [w])
        cut("a")

    quant(T.u1q[:], T.u1s[:], T.u1b[:], ["u1b"], ["u1q"])
    pick_codes("u1")
    pick_scales("u1")
    quant(T.xq[:, 0:XA], T.xs[:, 0:XA], T.xb[:, 0:4 * XA], ["xb0"], ["xq0"])
    cut("v")
    mm(0, XA, T.u1q[:], T.u1s[:], T.xq[:, 0:XA], T.xs[:, 0:XA], ["u1q", "xq0"])
    quant(T.xq[:, XA:C], T.xs[:, XA:C], T.xb[:, 4 * XA:4 * C], ["xb1"], ["xq1"])
    cut("v")
    rows("u1", 1, 0, C, T.xq[:], T.xs[:], ["xq0", "xq1"])
    mm(4, C - XA, T.u1q[:], T.u1s[:], T.xq[:, XA:C], T.xs[:, XA:C], ["u1q", "xq1"])
    rows("u1", 3, 1, C, T.xq[:], T.xs[:], ["xq0", "xq1"])
    rows("u1", 5, 0, C, T.xq[:], T.xs[:], ["xq0", "xq1"])
    rows("u1", 2, 1, C, T.xq[:], T.xs[:], ["xq0", "xq1"])
    tr(T.tn1[:, 0:64], T.ps0[:, 0:64], ["ps0"], ["tn01"])
    cut("v")
    tr(T.tn1[:, 64:XA], T.ps0[:, 64:XA], ["ps0"], ["tna1"])
    cut("v")
    passes(1)
    tail(1)
    for i, (a, b) in enumerate(((0, 32), (32, 64), (1144, 1152))):
        act(kc[:, 128 + 32 * i:128 + 32 * i + b - a], kf[:, a:b], ACT.Identity, ["N2"], ["F4"], accum_out=kc[:, i:i + 1])
    act(C1A, R4, ACT.Abs, ["R4", "F4"], ["C1a"], bias=NPQ)
    act(N0, PH, ACT.Identity, ["F4"], ["C1a"], scale=-1.0, bias=1.0)
    act(C1, C1A, ACT.Relu, ["C1a"], ["C1"], scale=-HOLD, bias=HOLD)
    cut("a")
    pick_scales("u2", 0, 1)
    pick_scales("u2", 1, 2)
    act(T.yx[:, 0:128], kf[:, 608:736], ACT.Identity, ["RR"], ["C2"], accum_out=kc[:, 12:13])
    act(T.yx[:, 128:256], kf[:, 736:864], ACT.Identity, ["RR"], ["C2"], accum_out=kc[:, 13:14])
    for p in range(8):
        act(kc[:, 704 + S * p:704 + S * p + S], kc[:, 258:272], ACT.Copy, ["C1"], ["C2"])
    cut("a")
    cp(T.win1[:].indirect(T.od1[:]), VAL1, ["od1", "VAL1"], ["win1"])
    for n, a, b in (("a", 0, 128), ("b", 128, A)):
        scan(T.ex1[:, a:b], kc[:, 256 + a:256 + b], T.win1[:, a:b], 0.0, ALU.add, ALU.min, ["win1", "C1"], ["ex1" + n])
        cut("v")
    for n, a, b in (("a", 0, 128), ("b", 128, A)):
        ts(T.of[:, a // 4:b // 4], T.ex1[:, a + 3:b:4], PT, None, ALU.add, None, ["ex1" + n, "F4"], ["of" + n, "of"])
        cut("v")
    xr = ["xb0", "xb1"]
    act(T.ft[:, 16 * FA:512], T.xb[:].indirect(T.of[:, FA:32]), ACT.Copy, ["ofa"] + xr, ["fta", "ft"])
    cut("a")
    act(T.ft[:, 512:16 * FB], T.xb[:].indirect(T.of[:, 32:FB]), ACT.Copy, ["ofb"] + xr, ["ft"])
    cut("a")
    cp(T.ft[:, 0:16 * FA], T.xb[:].indirect(T.of[:, 0:FA]), ["ofa"] + xr, ["fta", "ft"])
    cut("v")
    quant(T.fq[:, 0:128], T.fs[:, 0:128], T.ft[:, 0:512], ["fta"], ["fq0"])
    cut("v")
    cp(T.ft[:, 16 * FB:896], T.xb[:].indirect(T.of[:, FB:56]), ["ofb"] + xr, ["ftb"])
    cut("v")
    quant(T.fq[:, 128:256], T.fs[:, 128:256], T.ft[:, 384:896], ["ft", "ftb"], ["fq1"])
    cut("v")
    cp(T.oread[:], kc[:, 12:14], ["C2"], ["oread"])
    cut("v")
    for h in range(2):
        for b in range(4):
            mm(4 * h + b, 128, T.wq[:, 128 * b:128 * b + 128], T.wp[:, 128 * b:128 * b + 128],
               T.fq[:, 128 * h:128 * h + 128], T.fs[:, 128 * h:128 * h + 128], ["w", "fq%d" % h])
    relu4(T.ht, 128, 0, 0, "hta")
    cut("v")
    relu4(T.ht, 96, 128, 4, "htb", 32, (0, 2, 3))
    cut("v")
    quant(T.hq[:, 0:128], T.hs[:, 0:128], T.ht[:, 0:512], ["hta"], ["hqa"])
    cut("v")
    mm(0, 128, T.u2q[:], T.u2s[:], T.hq[:, 0:128], T.hs[:, 0:128], ["u2q", "hqa"])
    quant(T.hq[:, 128:256], T.hs[:, 128:256], T.ht[:, 512:1024], ["htb", "h0"], ["hq"])
    cut("v")
    rows("u2", 1, 0, A, T.hq[:, 0:A], T.hs[:, 0:A], ["hq", "hqa"])
    mm(4, 128, T.u2q[:], T.u2s[:], T.hq[:, 128:256], T.hs[:, 128:256], ["u2q", "hq"])
    rows("u2", 2, 1, A, T.hq[:, 0:A], T.hs[:, 0:A], ["hq"])
    rows("u2", 3, 1, A, T.hq[:, 0:A], T.hs[:, 0:A], ["hq"])

    tr(T.tn2[:, 0:128], T.ps0[:, 0:128], ["ps0"], ["tn02", "tna2"])
    cut("v")
    choose(T.fh[:, 0:8 * A:2], T.ft[:], [[0, 4 * A]], ALU.is_ge, 0.0, 0, 0, ["ft", "ftb"], ["fh"])
    cut("g")
    passes(2)
    tail(2)
    cp(T.win2[:].indirect(T.od2[:]), VAL2, ["od2", "VAL2"], ["win2"])
    cut("v")
    f_and_h(3)
    cut("v")
    scan(T.ex2[:], C2, T.win2[:, 0:B], 0.0, ALU.add, ALU.min, ["win2", "C2"], ["ex2"])
    ts(T.og[:], T.ex2[:].indirect(T.oread[:]), PT, None, ALU.add, None, ["ex2", "oread"], ["og"])
    cut("v")
    ts(T.oh[:], T.ex2[:].indirect(T.oread[:]), 0.25, None, ALU.mult, None, ["ex2", "oread"], ["oh"])
    cut("v")
    hr = ["og", "hta", "htb"]
    act(T.gf[:, 128:256], T.ht[:, 0:896].indirect(T.og[:, 8:16]), ACT.Copy, hr, ["gf"])
    cut("a")
    act(T.gt[:, 16 * GV:256], T.ht[:, 0:896].indirect(T.og[:, 16 + GV:32]), ACT.Copy, hr, ["gt"])
    cut("a")
    cp(T.gf[:, 0:128], T.ht[:, 0:896].indirect(T.og[:, 0:8]), hr, ["gf"])
    cut("v")
    cp(T.gt[:, 0:16 * GV], T.ht[:, 0:896].indirect(T.og[:, 16:16 + GV]), hr, ["gt"])
    cut("v")
    quant(T.gfq[:], T.gfs[:], T.gf[:], ["gf"], ["gfq"])
    cut("v")
    quant(T.gq[:, 112:240], T.gs[:, 112:240], T.gt[:], ["gt"], ["gq"])
    cut("v")

    def send_far(phase):
        deps("g", ["gfq" if phase == 1 else "tfq"], [])
        n = FIRST[phase - 1]
        hm = _masks(topo.engines(core, hs[0])[-4 * n:], (n,) * 4)
        xs = []
        for j in range(4):
            if phase == 1:
                src, dst = (_u8(T.gfq[:, 32 * j:32 * j + 32]), _u8(T.rq1[:])) if j < 2 else (T.gfs[:], T.rs1[:])
            else:
                src, dst = (_u8(T.tfq[:, 28 * j:28 * j + 28]), _u8(T.rq2[:])) if j < 2 else (T.tfs[:, 0:112], T.rs2[:])
            xs.append(_xfer(topo, core, hs[j], hm[j], T.sem["hin%d" % phase], src, dst))
        g.remote_dma_fused(xs, local_sem=T.sem.sent)
        mark(new_stage("arr%d" % phase, 2 * HOP * len(far)), [], ["far%d" % phase])

    def send_near(phase):
        q, s = (T.gq, T.gs) if phase == 1 else (T.tq, T.ts)
        deps("g", ["gq" if phase == 1 else "tq"], [])
        for sizes, buf, wrap in ((DIRECT_CODES, q, _u8), (DIRECT_SCALES, s, lambda a: a)):
            dm = _masks(topo.engines(core, near[0]), sizes)
            xs = []
            for i, d in enumerate(near):
                a = 128 + 16 * i + 2 if phase == 1 else S + S * (4 + i)
                to = (S if phase == 1 else 128 - 4 * S) + S * _slot(d, core, T, topo)
                xs.append(_xfer(topo, core, d, dm[i], T.sem["arn%d" % phase], wrap(buf[:, a:a + S]), wrap(buf[:, to:to + S])))
            g.remote_dma_fused(xs, local_sem=T.sem.sent)
        mark(new_stage("arn%d" % phase, _arrivals(core, T, topo)), [], ["near%d" % phase])

    def spread(i):
        a, b = XS[i:i + 2]
        cp(T.x2[:].indirect(T.of[:, a:b]), T.a1[:, 32 * a + 1:32 * b:2], ["a1", "of", "x2"], ["x2"])
        cut("v")

    def layer(bank, q, s, r):
        for b in range(4):
            mm(bank + b, 128, T.zq[:, 128 * b:128 * b + 128], T.zp[:, 128 * b:128 * b + 128], q, s, ["z", "gq"] + r)

    def upward(h, bank, q, s, r):
        for b in range(4):
            mm(bank + b, 128, T.eq[:, 128 * b:128 * b + 128], T.es[:, 128 * b:128 * b + 128], q, s, ["eq"] + r)
        for b in range(4):
            tt(T.il[:, 448 * h + 2 * b + 1:448 * h + 448:8], T.gcomp[:, A * h + b:A * h + A:4], T["ps%d" % (bank + b)][:, 72:128],
               ALU.add, ["gcomp", "ps%d" % (bank + b)], ["il%d" % h])
        cut("v")
        scan(T.io2[:, 448 * h:448 * h + 448], T.keep[:, 0:448], T.il[:, 448 * h:448 * h + 448], 0.0, ALU.mult, ALU.add,
             ["il", "il%d" % h, "keep"], ["io%d" % h])
        cp(T.x2[:].indirect(T.ox[:, 14 * h:14 * h + 14]), T.io2[:, 448 * h + 1:448 * h + 448:2], ["io%d" % h, "ox", "x2"], ["x2", "x2c"])
        cut("v")

    send_far(1)
    send_near(1)
    act(T.both[:], T.win1[:, 0:A].indirect(T.oh[:]), ACT.Copy, ["oh", "win1"], ["both"])
    for p in range(8):
        o = 64 * ((p + 4) % 8)
        act(T.yx[:, S * p:S * p + S], T.both[:, o + 8:o + 64:4], ACT.Identity, ["both"], ["yx0"], bias=2048.0 * p)
    cut("a")
    for p in range(8):
        act(T.gcomp[:, 56 * p:56 * p + 56], (T.gt if p < 4 else T.gf)[:, 64 * (p % 4) + 8:64 * (p % 4) + 64], ACT.Copy,
            ["gt", "gf"], ["gcomp"])
    cut("a")
    spread(0)
    scan(T.yx[:, 128:128 + B], kc[:, 256:256 + B], T.yx[:, 0:B], 0.0, ALU.add, ALU.min, ["yx0", "C1"], ["yx1"])
    cut("v")
    spread(1)
    ts(kj[:, 0:28], T.yx[:, 131:128 + B:4], PT, None, ALU.add, None, ["yx1"], ["yx2"])
    cut("v")
    spread(2)
    ts(kj[:, 32:60], kj[:, 0:28], 2047, None, ALU.bitwise_and, None, ["yx2"], ["yx3"])
    cut("v")
    spread(3)
    cp(T.ox[:], kj[:, 32:60], ["yx3"], ["ox"])
    cut("v")
    spread(4)

    layer(4, T.gq[:, 70:198], T.gs[:, 70:198], ["near1"])
    relu4(T.tt, 58, 70, 4, "tt", 0, (0, 1, 2, 3))
    quant(T.tq[:, 0:128], T.ts[:, 0:128], T.tt[:], ["tt"], ["tq"])
    cut("v")
    send_near(2)
    act(T.il[:, 0:448:2], T.xb[:].indirect(T.ox[:, 0:14]), ACT.Copy, ["ox"], ["il"])
    cut("a")
    spread(5)
    layer(0, T.gq[:, 14:142], T.gs[:, 14:142], ["near1", "far1"])
    relu4(T.tf, 56, 0, 0, "tf", 0, (0, 1, 2, 3))
    quant(T.tfq[:, 0:128], T.tfs[:, 0:128], T.tf[:], ["tf"], ["tfq"])
    cut("v")
    send_far(2)
    act(T.il[:, 448:896:2], T.xb[:].indirect(T.ox[:, 14:28]), ACT.Copy, ["ox"], ["il"])
    for p in range(8):
        act(T.olb[:, S * order[p]:S * order[p] + S], T.both[:, 64 * p + 8:64 * p + 64:4], ACT.Identity, ["both"], ["olb"], scale=0.25)
    cut("a")
    spread(6)

    upward(0, 4, T.tq[:, 42:170], T.ts[:, 42:170], ["tq", "near2"])
    dma("y", [(T.ol[i:i + 1, :], T.olb[16 * i:16 * i + 1, :]) for i in range(8)], ["olb", "near2"], [])
    upward(1, 0, T.tfq[:, 56:184], T.tfs[:, 56:184], ["tfq", "far2"])
    for h, (a, b) in enumerate(((0, O1), (O1, C))):
        quant(T.oq[:, a:b], T.osb[:, a:b], T.x2[:, 4 * a:4 * b], ["x2c"], ["oq%d" % h])
        cut("v")
        mm(4 + h, b - a, T.vq[:], T.vs[:], T.oq[:, a:b], T.osb[:, a:b], ["vq", "oq%d" % h])
        dma("y", [(T.oc[:, 4 * a:4 * b], _u8(T.oq[:, a:b]))], ["oq%d" % h], [])
    dma("y", [(T.osc[4 * i:4 * i + 4, :], T.osb[32 * i:32 * i + 4, :]) for i in (0, 1)], ["oq0", "oq1"], [])
    act(T.yb[:, 0:O1], T.ps4[:, 0:O1], ACT.Copy, ["ps4"], ["y0"])
    cp(T.yb[:, O1:C], T.ps5[:, 0:C - O1], ["ps5"], ["y1"])
    dma("a", [(T.y[:, 0:O1], T.yb[:, 0:O1])], ["y0"], [])
    dma("y", [(T.y[:, O1:C], T.yb[:, O1:C])], ["y1"], [])
    dma("a", [(T.osc[4 * i:4 * i + 4, :], T.osb[32 * i:32 * i + 4, :]) for i in (2, 3)], ["oq0", "oq1"], [])

    g.wait_ge(T.sem.sent, 4 * sum(FIRST) + 2 * (sum(DIRECT_CODES) + sum(DIRECT_SCALES)))
    for st in stages:
        if not st["waited"]:
            need("g", st)
